import numpy as np, ml_dtypes
CORES = [24,25,26,27,28,29,30,31]
N = 8
BF = ml_dtypes.bfloat16
def gentries(a):
    return np.ascontiguousarray(a.reshape(8, 16, -1).transpose(0, 2, 1)).reshape(8, -1)
def gtable(e):
    e = np.asarray(e); return np.ascontiguousarray(e.reshape(8, -1, 16).transpose(0, 2, 1)).reshape(128, -1).astype(np.int32)
V, K, RO = 1024, 2, 4
W = N * V
def apart(rng, M, n=8):
    s = []
    for j in range(M - K, M):
        t = rng.integers(0, j + 1, (n, W)); clash = np.zeros((n, W), bool)
        for a in s: clash |= a == t
        s.append(np.where(clash, j, t))
    return np.stack(s, 1)
def far(rng):
    return (np.arange(W) + 1 + apart(rng, W - 1)) % W
def near(rng, h):
    t = apart(rng, 2 * h); return (np.arange(W) + np.where(t < h, t - h, t - h + 1)) % W
def mixed(rng):
    share = np.repeat(rng.choice(np.array([0.05, 0.2, 0.5]), (8, 1, N)), V, axis=2)
    return np.where(rng.random((8, 1, W)) < share, near(rng, 8), far(rng))
def points(rng):
    cen = rng.integers(0, 256, (8, 16, 48)); lab = rng.integers(0, 48, (8, W))
    noise = rng.standard_normal((8, 16, W)) * np.exp2(rng.integers(1, 6, (8, 1, W)))
    return np.clip(np.rint(np.take_along_axis(cen, lab[:, None, :], 2) + noise), 0, 255).astype(np.int64)
def stairs(rng, X, nb):
    z = rng.integers(0, 256) + 256 * rng.permutation(W // 256); o = np.concatenate([z, rng.permutation(np.setdiff1d(np.arange(W), z))])
    Q = o[:K * (K + 1)].reshape(K + 1, K)[::-1].T; P = o[K * (K + 1):K * (K + 1) + W // 16]; j = np.arange(K)
    X[:, P] = 0; nb[:, P] = Q[:, :1]
    for s in range(K):
        for t in range(K + 1):
            X[:, Q[s, t]] = (4080 - K * t - s + np.arange(16)) // 16
            nb[(s + t + j) % K, Q[s, t]] = Q[s, (t + 1 + j) % (K + 1)]
def pack(X, nb):
    x = np.ascontiguousarray(X.reshape(8, 16, N, V).transpose(2, 0, 1, 3)).reshape(N, 128, V)
    e = np.ascontiguousarray(nb.reshape(8, K, N, V).transpose(2, 0, 1, 3)).reshape(N, 8, K * V)
    return {"x": x.astype(np.float32).astype(BF), "nb": np.stack([gtable(a) for a in e])}
def setup_inputs(rng):
    return pack(points(rng), mixed(rng))
def setup_inputs_ties(rng):
    q = rng.permutation(8); X = rng.integers(0, 2, (8, 16, W)); nb = mixed(rng)
    X[q[0]] = 255 * rng.integers(0, 2, (1, W)); X[q[1]] = rng.integers(0, 256, (16, 1)); X[q[2]] = rng.integers(0, 4, (16, W))
    X[q[3]] = 255 * rng.integers(0, 2, (16, W)); X[q[4]] = 100 * (np.arange(16)[:, None] == rng.integers(0, 16, (1, W)))
    stairs(rng, X[int(q[5])], nb[int(q[5])])
    return pack(X, nb)
def setup_inputs_ring(rng):
    nb = np.zeros((8, K, W), np.int64); h = np.array([0, 1, 0, 2])[:K, None]; m = np.array([1, 1, 2, 2])[:K, None]
    for g in range(8):
        p = rng.permutation(W); pos = np.argsort(p)
        e = ((((pos - h) % W) ^ m) + h) % W
        nb[g] = p[e][rng.permutation(K)]
    return pack(points(rng), nb)
def setup_inputs_hubs(rng):
    X = points(rng); nb = np.zeros((8, K, W), np.int64); H = 2 * K + 1; ends = np.array([0, V - 1, V, W - 1]); q = rng.permutation(8); remote = q[:2]
    for g in range(8):
        o = rng.permutation(np.setdiff1d(np.arange(W), ends)); hub = rng.permutation(np.concatenate([ends, o[:H - 4]])); P = o[H - 4:H - 4 + W // 16]
        m = rng.integers(0, H, W); m[hub] = np.arange(H); k = (m + 1 + apart(rng, H - 1, 1)[0]) % H
        if g in remote:
            X[g] = rng.integers(200, 256, (16, W)); X[g][:, hub] = rng.integers(0, 32, (16, H))
        k[:, hub[0]] = np.array([4, 1, 2, 3])[:K]; k[:, hub[1]] = np.array([0, 4, 2, 3])[:K]; k[:, P] = np.arange(K)[:, None]
        nb[g] = hub[k]; X[g][0, hub[:4]] = 255; X[g][0, hub[4]] = 0; X[g][:, P] = X[g][:, hub[4:5]]
    g = int(q[2]); h = int(rng.integers(0, W)); a = int(rng.integers(0, K)); others = np.arange(W) != h
    e = far(rng)[g]; e = np.where(others & (e == h), e[a], e); e[a, others] = h
    nb[g] = e; X[g][:, h] = 255; X[g][:, int(e[a, h])] = 128
    return pack(X, nb)
def setup_inputs_away(rng):
    sh = (np.arange(8) + rng.integers(0, N)) % N; q = rng.permutation(N); g = int(rng.choice(np.flatnonzero(sh))); u = np.arange(W); X = points(rng)
    to = (np.arange(N)[None, :] + sh[:, None]) % N
    to[:, q[1:1 + N // 2]] = q[0]; to[g] = q[0]; to[g, q[0]] = q[1]
    base = to[:, u // V][:, None, :] * V
    nb = base + (u % V + 1 + apart(rng, V - 1)) % V
    o = rng.permutation(V); at = np.argsort(o)
    nb[g] = base[g] + o[(at[u % V] + 1 + np.arange(K)[:, None]) % V]
    X[g] = np.where(u // V == q[0], 192, 0) + rng.integers(0, 64, (16, W))
    return pack(X, nb)
def setup_inputs_spread(rng):
    X = (np.exp2(8 * rng.random((8, 1, W))) * rng.random((8, 16, W)) * (rng.random((8, 1, W)) > 0.0625)).astype(np.int64)
    nb = far(rng); u = np.arange(W)
    for g in rng.permutation(8)[:2]:
        for i in range(K):
            o = rng.permutation(V); at = np.argsort(o)
            nb[g, i] = (u // V + 1 + i) % N * V + o[(at[u % V] + 1) % V]
    return pack(X, nb)
def check_inputs(d):
    bad = []; x = np.asarray(d["x"]).astype(np.float32)
    if not np.all((x >= 0) & (x <= 255) & (x == np.floor(x))): bad.append("whole numbers of x")
    e = np.stack([gentries(a) for a in d["nb"]]).astype(np.int64).reshape(N, 8, K, V)
    if np.min(e) < 0 or np.max(e) > W - 1: bad.append("range of nb")
    s = np.sort(e, axis=2)
    if np.any(s[:, :, 1:] == s[:, :, :-1]): bad.append("different neighbours")
    if np.any(e == np.arange(W).reshape(N, 1, 1, V)): bad.append("no point its own neighbour")
    return bad
def reference(x, nb):
    X = np.ascontiguousarray(x.astype(np.float32).astype(np.int64).reshape(N, 8, 16, V).transpose(1, 2, 0, 3)).reshape(8, 16, W)
    b = np.stack([gentries(a) for a in nb]).astype(np.int64).reshape(N, 8, K, V)
    b = np.ascontiguousarray(b.transpose(1, 2, 0, 3)).reshape(8, K, W)
    def dist(c):
        return np.add.reduce(np.abs(X - np.take_along_axis(X, c[:, None, :], 2)), axis=1)
    d = np.stack([dist(b[:, i]) for i in range(K)], 1); u = np.arange(W)[None, :]; slot = np.arange(K)[None, :, None]
    for t in range(RO):
        old = b.copy()
        for i in range(K):
            c = np.take_along_axis(old[:, (i + t) & (K - 1)], old[:, i], 1); e = dist(c)
            s = np.argmax(d, axis=1)
            new = (c != u) & np.all(b != c[:, None, :], axis=1) & (e < np.max(d, axis=1))
            hit = new[:, None, :] & (slot == s[:, None, :])
            b = np.where(hit, c[:, None, :], b); d = np.where(hit, e[:, None, :], d)
    bo = np.ascontiguousarray(b.reshape(8, K, N, V).transpose(2, 0, 1, 3)).reshape(N, 8, K * V)
    do = np.ascontiguousarray(d.reshape(8, K, N, V).transpose(2, 0, 1, 3)).reshape(N, 8, K * V)
    return {"ynb": np.stack([gtable(a) for a in bo]).astype(np.float32), "yd": np.stack([gtable(a) for a in do]).astype(np.float32)}

@@ -1,0 +1,466 @@
+from concourse.bass import DstId, RemoteDMATransfer
+from concourse.mybir import AluOpType as ALU, ActivationFunctionType as ACT
+
+N = 8
+V = 1024
+RO = 4
+BIG = 8192.0
+BANKS = ["pw0", "pw1", "pc0", "pc1", "pb0", "pb1", "pe0", "pe1"]
+
+SCRATCH = {
+    "xs": ("sbuf", [128, V], "bfloat16"),
+    "xr": ("sbuf", [128, N * V], "bfloat16"),
+    "xw": ("sbuf", [128, N * V], "bfloat16"),
+    "own": ("sbuf", [128, V], "bfloat16"),
+    "nbd": ("dram", [N, 128, 16], "int32"),
+    "nbl": ("dram", [N, 128, 16], "int32"),
+    "od1": ("dram", [N, 128, 16], "float32"),
+    "od2": ("dram", [N, 128, 16], "float32"),
+    "ol1": ("dram", [N, 128, 16], "float32"),
+    "ol2": ("dram", [N, 128, 16], "float32"),
+    "pidx": ("sbuf", [128, 8], "int32"),
+    "pbit": ("sbuf", [128, 8], "int32"),
+    "pflt": ("sbuf", [128, 8], "float32"),
+    "pcol": ("sbuf", [128, 8], "float32"),
+    "j16": ("sbuf", [128, 128], "float32"),
+    "j128": ("sbuf", [128, 128], "float32"),
+    "owi": ("sbuf", [128, 64], "int32"),
+    "sob": ("sbuf", [128, 16], "float32"),
+    "per": ("sbuf", [128, 128], "bfloat16"),
+    "sel": ("sbuf", [128, 8], "float32"),
+    "selb": ("sbuf", [128, 16], "bfloat16"),
+    "repb": ("sbuf", [128, 1024], "bfloat16"),
+    "repf": ("sbuf", [128, 1024], "float32"),
+    "bi": ("sbuf", [128, 128], "bfloat16"),
+    "nbi": ("sbuf", [128, 128], "bfloat16"),
+    "k0": ("sbuf", [128, 128], "bfloat16"),
+    "wa": ("sbuf", [128, 64], "float32"),
+    "ow": ("sbuf", [128, 64], "uint16"),
+    "so": ("sbuf", [128, 16], "uint16"),
+    "ol": ("sbuf", [128, 128], "uint16"),
+    "of": ("sbuf", [128, 128], "uint16"),
+    "oc": ("sbuf", [128, 128], "uint16"),
+    "ob": ("sbuf", [128, 128], "uint16"),
+    "ui": ("sbuf", [128, 128], "int32"),
+    "lo32": ("sbuf", [128, 128], "int32"),
+    "of32": ("sbuf", [128, 128], "int32"),
+    "uf": ("sbuf", [128, 128], "float32"),
+    "u1": ("sbuf", [128, 128], "float32"),
+    "da": ("sbuf", [128, 128], "float32"),
+    "da1": ("sbuf", [128, 128], "float32"),
+    "dl0": ("sbuf", [128, 128], "float32"),
+    "dl1": ("sbuf", [128, 128], "float32"),
+    "dl2": ("sbuf", [128, 128], "float32"),
+    "eq": ("sbuf", [128, 448], "bfloat16"),
+    "win": ("sbuf", [128, 1024], "float32"),
+    "cw": ("sbuf", [128, 1024], "float32"),
+    "cb": ("sbuf", [128, 128], "float32"),
+    "msk": ("sbuf", [128, 2048], "bfloat16"),
+    "g1": ("sbuf", [128, 2048], "float32"),
+    "dif": ("sbuf", [128, 2048], "bfloat16"),
+    "ab": ("sbuf", [128, 2048], "bfloat16"),
+    "dif0": ("sbuf", [128, 2048], "bfloat16"),
+    "ab0": ("sbuf", [128, 2048], "bfloat16"),
+}
+for _b in BANKS:
+    SCRATCH[_b] = ("psum", [128, 512], "float32")
+
+SEMAPHORES = ["cv", "ca", "cp", "cg", "xld", "nbs", "nbo", "nbarr", "nbsent", "nbld", "xarr", "xsent",
+              "o1", "o2", "o3", "o4", "oarr", "osent", "y1", "y2"]
+
+
+def bits(engines):
+    m = 0
+    for e in engines:
+        m |= 1 << e
+    return m
+
+
+def x_calls(T, topo, r):
+    me = T.cores[r]
+    others = [(r + k) % N for k in range(1, N)]
+    far = [s for s in others if topo.die(T.cores[s]) != topo.die(me)]
+    near = [s for s in others if topo.die(T.cores[s]) == topo.die(me)]
+    calls = []
+    while far or near:
+        pair = ([far.pop(0)] if far else []) + ([near.pop(0)] if near else [])
+        calls.append([(s, topo.engines(me, T.cores[s])[k::len(pair)]) for k, s in enumerate(pair)])
+    return calls
+
+
+def rank_program(g, core, T, topo):
+    r = T.rank_of(core)
+    if r is None:
+        return
+    S = T.sem
+    queue = {"v": g.vector, "a": g.scalar, "p": g.tensor, "g": g, "s": g.sync}
+    own_sem = {"v": "cv", "a": "ca", "p": "cp", "g": "cg"}
+    count = {"v": 0, "a": 0, "p": 0, "g": 0}
+    waited = {e: {} for e in queue}
+    writer = {}
+    readers = {}
+    bank = {b: {} for b in BANKS}
+
+    def wait(e, tok):
+        if waited[e].get(tok[0], 0) < tok[1]:
+            queue[e].wait_ge(S[tok[0]], tok[1])
+            waited[e][tok[0]] = tok[1]
+
+    def need(e, R, W):
+        toks = {}
+
+        def add(t):
+            if e == "p" and t[0] == "cp":
+                return
+            toks[t[0]] = max(toks.get(t[0], 0), t[1])
+        for k in R:
+            for t in writer.get(k, []):
+                add(t)
+        for k in W:
+            for t in writer.get(k, []) + readers.get(k, []):
+                add(t)
+        for k in list(R) + list(W):
+            b = k.split(":")[0]
+            if b in bank:
+                for e2, t in bank[b].items():
+                    if e2 != e:
+                        add(t)
+        for s, n in toks.items():
+            wait(e, (s, n))
+
+    def note(e, tok, R, W):
+        for k in R:
+            readers.setdefault(k, []).append(tok)
+        for k in W:
+            writer[k] = [tok]
+            readers[k] = []
+        for k in list(R) + list(W):
+            b = k.split(":")[0]
+            if b in bank:
+                bank[b][e] = tok
+
+    def op(e, call, R, W):
+        need(e, R, W)
+        count[e] += 1
+        call().then_inc(S[own_sem[e]], 1)
+        note(e, (own_sem[e], count[e]), R, W)
+
+    def dma(e, out, in_, sem, R, W):
+        need(e, R, W)
+        queue[e].dma_start(out, in_).then_inc(S[sem], 16)
+        note(e, (sem, 16), R, W)
+
+    v, a, p = g.vector, g.scalar, g.tensor
+
+    def tt(out, in0, in1, o, R, W):
+        op("v", lambda: v.tensor_tensor(out, in0, in1, o), R, W)
+
+    def ts(out, in0, s1, o0, R, W, s2=None, o1=None):
+        if o1 is None:
+            op("v", lambda: v.tensor_scalar(out, in0, s1, None, o0), R, W)
+        else:
+            op("v", lambda: v.tensor_scalar(out, in0, s1, s2, o0, o1), R, W)
+
+    def cp(out, in_, R, W):
+        op("v", lambda: v.tensor_copy(out, in_), R, W)
+
+    def act(out, in_, f, R, W):
+        op("a", lambda: a.activation(out, in_, f), R, W)
+
+    def mm(out, lhsT, rhs, R, W, start=True, stop=True):
+        op("p", lambda: p.matmul(out, lhsT, rhs, start, stop), R, W)
+
+    def dst(s):
+        rid, pid, _ = topo.addr(T.cores[s])
+        return DstId(rid=rid, pnc=pid)
+
+    others = [(r + k) % N for k in range(1, N)]
+    eng = topo.engines(core, T.cores[others[0]])
+    mine = slice(16 * r, 16 * r + 16)
+
+    dma("a", T.nbd[:], T.nb[:], "nbs", [], ["nbd"])
+    dma("s", T.xs[:], T.x[:], "xld", [], ["xs"])
+    dma("s", T.nbl[r], T.nb[mine, :], "nbo", [], ["nblown"])
+
+    def iota(out, pattern, cm, key, flt):
+        if flt:
+            op("g", lambda: g.iota(out, pattern, 0, cm, allow_small_or_imprecise_dtypes=True), [], [key])
+        else:
+            op("g", lambda: g.iota(out, pattern, 0, cm), [], [key])
+
+    iota(T.pidx[:], [[0, 8]], 1, "pidx", False)
+    iota(T.j16[:], [[0, 8], [1, 16]], 0, "j16", True)
+    iota(T.j128[:], [[1, 128]], 0, "j128", True)
+    iota(T.owi[:], [[128, 8], [1024, 8]], 1, "owi", False)
+    iota(T.sob[:, 0:8], [[512, 2], [16, 4]], 0, "sob0", True)
+    iota(T.sob[:, 8:16], [[0, 2], [16, 4]], 0, "sob1", True)
+    ts(T.pbit[:, 0:1], T.pidx[:, 0:1], 15, ALU.bitwise_and, ["pidx"], ["pb0_"])
+    ts(T.pbit[:, 1:2], T.pidx[:, 0:1], 4, ALU.logical_shift_right, ["pidx"], ["pb1_"])
+    ts(T.pbit[:, 2:3], T.pidx[:, 0:1], 7, ALU.bitwise_and, ["pidx"], ["pb2_"])
+    ts(T.pbit[:, 3:4], T.pidx[:, 0:1], 8, ALU.bitwise_and, ["pidx"], ["pb3_"])
+    cp(T.pflt[:, 0:4], T.pbit[:, 0:4], ["pb0_", "pb1_", "pb2_", "pb3_"], ["pflt"])
+    cp(T.pflt[:, 4:5], T.pidx[:, 0:1], ["pidx"], ["pf4"])
+    ts(T.per[:], T.j16[:], T.pflt[:, 0:1], ALU.is_equal, ["j16", "pflt"], ["per"])
+    ts(T.sel[:], T.j16[:, 0:8], T.pflt[:, 1:2], ALU.is_equal, ["j16", "pflt"], ["sel"])
+    xcalls = x_calls(T, topo, r)
+    xorder = [s for c in xcalls for s, _ in c] + [r]
+    for s in xorder:
+        ts(T.repb[:, 128 * s:128 * s + 128], T.per[:], T.sel[:, s:s + 1], ALU.mult, ["per", "sel"], ["repb%d" % s])
+    for s in range(N):
+        op("a", lambda: a.activation(T.repf[:, 128 * s:128 * s + 128], T.per[:], ACT.Identity,
+                                     scale=T.sel[:, s:s + 1]), ["per", "sel"], ["repf%d" % s])
+
+    need("g", ["nbd"], [])
+    g.remote_dma_fused([RemoteDMATransfer(dst_ids=[dst(s)], dma_engine_mask=bits(eng[2 * k:2 * k + 2]),
+                                          remote_sem=S.nbarr, src=T.nbd[s], dst=T.nbl[r])
+                        for k, s in enumerate(others)], local_sem=S.nbsent)
+    writer["nbl"] = [("nbarr", 2 * (N - 1))]
+    dma("s", T.ui[:], T.nbl[:], "nbld", ["nbl", "nblown"], ["ui"])
+
+    rot = [("pw0", "pw1"), ("pc0", "pc1")]
+    sent = 0
+    nx = 0
+    for call in xcalls + [[(r, None)]]:
+        for s, _ in call:
+            b0, b1 = rot[nx % 2]
+            nx += 1
+            to = T.xw if s == r else T.xr
+            lhs = T.repb[:, 128 * s:128 * s + 128]
+            mm(T[b0][:], lhs, T.xs[:, 0:512], ["repb%d" % s, "xs"], [b0])
+            mm(T[b1][:], lhs, T.xs[:, 512:V], ["repb%d" % s, "xs"], [b1])
+            cp(to[:, V * s:V * s + 512], T[b0][:], [b0], ["xr%da" % s])
+            act(to[:, V * s + 512:V * s + V], T[b1][:], ACT.Copy, [b1], ["xr%db" % s])
+        if call[0][0] == r:
+            break
+        need("g", [k % s for s, _ in call for k in ("xr%da", "xr%db")], [])
+        if len(call) == 1:
+            s, e = call[0]
+            rid, pid, _ = topo.addr(T.cores[s])
+            g.remote_dma(T.xw[:, V * r:V * r + V], T.xr[:, V * s:V * s + V], S.xarr, S.xsent, pid, rid, bits(e))
+        else:
+            g.remote_dma_fused([RemoteDMATransfer(dst_ids=[dst(s)], dma_engine_mask=bits(e), remote_sem=S.xarr,
+                                                  src=T.xr[:, V * s:V * s + V], dst=T.xw[:, V * r:V * r + V])
+                                for s, e in call], local_sem=S.xsent)
+        sent += sum(len(e) for _, e in call)
+    arrive = sum(len(e) for q in others for c in x_calls(T, topo, q) for s, e in c if s == r)
+    writer["xw"] = [("xarr", arrive)] + writer["xr%da" % r] + writer["xr%db" % r]
+
+    cp(T.selb[:, 0:8], T.sel[:], ["sel"], ["selb"])
+    ts(T.pcol[:, 0:1], T.pflt[:, 2:3], 64.0, ALU.mult, ["pflt"], ["pc0_"], T.pflt[:, 3:4], ALU.add)
+    ts(T.pcol[:, 1:2], T.pflt[:, 1:2], 1024.0, ALU.mult, ["pflt"], ["pc1_"], T.pflt[:, 0:1], ALU.add)
+    ts(T.bi[:], T.j128[:], T.pflt[:, 4:5], ALU.is_equal, ["j128", "pf4"], ["bi"], BIG, ALU.mult)
+    ts(T.nbi[:], T.j128[:], T.pflt[:, 4:5], ALU.is_equal, ["j128", "pf4"], ["nbi"], -BIG, ALU.mult)
+    ts(T.so[:], T.sob[:], T.pcol[:, 0:1], ALU.add, ["sob0", "sob1", "pc0_", "pflt"], ["so"], T.pflt[:, 1:2], ALU.add)
+    ts(T.wa[:], T.j128[:, 0:64], 16.0, ALU.mult, ["j128", "pc1_"], ["wa"], T.pcol[:, 1:2], ALU.add)
+    cp(T.ow[:], T.owi[:], ["owi"], ["ow"])
+    op("v", lambda: v.memset(T.k0[:, 0:64], 0.5 / BIG), [], ["k0a"])
+    op("v", lambda: v.memset(T.k0[:, 64:128], 1.0), [], ["k0b"])
+
+    REPF = ["repf%d" % s for s in range(N)]
+
+    def repeat(banks, src, key):
+        per_bank = N // len(banks)
+        for k in range(N):
+            b = banks[k // per_bank]
+            c = 64 * (k % per_bank)
+            mm(T[b][:, c:c + 64], T.repf[:, 128 * k:128 * k + 128], src, [key, REPF[k]], [b + ":%d" % k])
+
+    def bank_keys(b, ks):
+        return [b + ":%d" % k for k in ks]
+
+    def mask(c):
+        act(T.msk[:, 512 * c:512 * c + 512], T.per[:, 0:16].indirect(T.ol[:, 32 * c:32 * c + 32]), ACT.Copy,
+            ["per", "ol"], ["msk%d" % c])
+
+    def gather1(c, t):
+        s = (c // 2 + t) % 2
+        cols = slice(512 * c, 512 * c + 512)
+        tt(T.g1[:, cols], T.win[:, 512 * s:512 * s + 512].indirect(T.of[:, 32 * c:32 * c + 32]), T.msk[:, cols],
+           ALU.mult, ["win%da" % s, "win%db" % s, "of", "msk%d" % c], ["g1%d" % c])
+        b = "pb%d" % (c // 2)
+        for y in range(4 * c, 4 * c + 4):
+            mm(T[b][:, 8 * (y % 8):8 * (y % 8) + 8], T.g1[:, 128 * y:128 * y + 128], T.sel[:],
+               ["g1%d" % c, "sel"], [b + ":%d" % (y % 8)])
+
+    def gather2(lo, hi, off, okey, dif, ab, tag):
+        o = lo % V
+        tt(dif[:, lo:hi], T.xw[:].indirect(off[:, lo // 16:hi // 16]), T.own[:, o:o + hi - lo], ALU.subtract,
+           ["xw", okey, "own%d" % (o // 512)], ["dif%s%d" % (tag, lo)])
+
+    def absolute(lo, hi, dif, ab, tag):
+        act(ab[:, lo:hi], dif[:, lo:hi], ACT.Abs, ["dif%s%d" % (tag, lo)], ["ab%s%d" % (tag, lo)])
+
+    def sums(lo, hi, ab, tag, twice):
+        b = "pe%d" % (lo // V)
+        for y in range(lo // 128, hi // 128):
+            for d in range(2 if twice else 1):
+                c = 64 * d + 8 * (y % 8)
+                mm(T[b][:, c:c + 8], ab[:, 128 * y:128 * y + 128], T.selb[:, 0:8], ["ab%s%d" % (tag, lo), "selb"],
+                   [b + ":e"], start=not twice, stop=not twice)
+
+    def to_sbuf_c(i):
+        act(T.cb[:, 64 * i:64 * i + 64], T["pb%d" % i][:, 0:64], ACT.Copy, bank_keys("pb%d" % i, range(8)),
+            ["cb%d" % i])
+        repeat(["pc%d" % i], T.cb[:, 64 * i:64 * i + 64], "cb%d" % i)
+
+    def window_c(i):
+        act(T.cw[:, 512 * i:512 * i + 512], T["pc%d" % i][:], ACT.Copy, bank_keys("pc%d" % i, range(8)), ["cw%d" % i])
+
+    def offsets_c(i):
+        cp(T.oc[:, 64 * i:64 * i + 64], T.cb[:, 64 * i:64 * i + 64], ["cb%d" % i], ["oc%d" % i])
+
+    def eqc(k):
+        return T.eq[:, 64 * k:64 * k + 64]
+
+    def penal(b, k, stop=False):
+        for d in range(2):
+            mm(T[b][:, 64 * d:64 * d + 64], T.bi[:], eqc(k), ["bi", "eq%d" % k], [b + ":e"], False, False)
+
+    def not_max(b, k, stop):
+        mm(T[b][:, 0:64], T.bi[:], eqc(k), ["bi", "eq%d" % k], [b + ":e"], False, False)
+        mm(T[b][:, 64:128], T.nbi[:], eqc(k), ["nbi", "eq%d" % k], [b + ":e"], False, stop)
+
+    def open_sum(b):
+        mm(T[b][:, 0:128], T.bi[:], T.k0[:], ["bi", "k0a", "k0b"], [b + ":e"], True, False)
+
+    def checks(i):
+        dl = T.dl0 if i == 0 else T.dl1
+        w = T.cw[:, 512 * i:512 * i + 512]
+        tt(dl[:], w.indirect(T.so[:, 8:16]), T.uf[:], ALU.subtract, ["cw%d" % i, "so", "uf"], ["dl%d" % i])
+        tt(eqc(2 * i), w.indirect(T.so[:, 0:4]), T.wa[:], ALU.is_equal, ["cw%d" % i, "so", "wa"], ["eq%d" % (2 * i)])
+        half = dl[:, 64:128] if i == 0 else dl[:, 0:64]
+        ts(eqc(2 * i + 1), half, 0.0, ALU.is_equal, ["dl%d" % i], ["eq%d" % (2 * i + 1)])
+        if i == 1:
+            tt(eqc(4), T.dl1[:, 0:64], T.dl0[:, 0:64], ALU.is_equal, ["dl0", "dl1"], ["eq4"])
+
+    def slot_max(src, key, k):
+        tt(eqc(k), src[:, 64:128], src[:, 0:64], ALU.is_gt, [key], ["eq%d" % k])
+
+    E0, E1 = T.pe0[:, 0:128], T.pe1[:, 0:128]
+    H0, H1 = T.pe0[:, 128:256], T.pe1[:, 128:256]
+    T0, T1 = T.pe0[:, 256:384], T.pe1[:, 256:384]
+    CH = [(0, 512), (512, 1024), (1024, 1536), (1536, 1792), (1792, 2048)]
+
+    cp(T.uf[:], T.ui[:], ["ui"], ["uf"])
+    for t in range(RO):
+        s0, s1 = t % 2, (t + 1) % 2
+        repeat(["pw0", "pc0"], T.uf[:, 64 * s0:64 * s0 + 64], "uf")
+        repeat(["pw1"], T.uf[:, 64 * s1:64 * s1 + 64], "uf")
+        if t > 0:
+            tt(T.ui[:], T.u1[:], T1, ALU.add, ["u1", "pe1:t"], ["ui"])
+        ts(T.lo32[:], T.ui[:], 15, ALU.bitwise_and, ["ui"], ["lo32"])
+        ts(T.of32[:], T.ui[:], 4, ALU.logical_shift_right, ["ui"], ["of32"])
+        cp(T.ol[:], T.lo32[:], ["lo32"], ["ol"])
+        cp(T.of[:], T.of32[:], ["of32"], ["of"])
+        if t > 0:
+            tt(T.da[:], T.da1[:], E1, ALU.min, ["da1", "pe1:e"], ["da"])
+        cp(T.win[:, 512 * s0:512 * s0 + 256], T.pw0[:, 0:256], bank_keys("pw0", range(4)), ["win%da" % s0])
+        if t > 0:
+            slot_max(T.da, "da", 5)
+        cp(T.win[:, 512 * s0 + 256:512 * s0 + 512], T.pc0[:, 0:256], bank_keys("pc0", range(4, 8)), ["win%db" % s0])
+        mask(0)
+        mask(1)
+        act(T.win[:, 512 * s1:512 * s1 + 512], T.pw1[:], ACT.Copy, bank_keys("pw1", range(8)),
+            ["win%da" % s1, "win%db" % s1])
+        mask(2)
+        mask(3)
+        gather1(0, t)
+        gather1(1, t)
+        gather1(2, t)
+        to_sbuf_c(0)
+        gather1(3, t)
+        if t == 0:
+            op("v", lambda: v.tensor_copy(T.ob[:], T.win[:].indirect(T.so[:, 0:8])),
+               ["win0a", "win0b", "win1a", "win1b", "so"], ["ob"])
+            to_sbuf_c(1)
+            window_c(0)
+            window_c(1)
+            offsets_c(0)
+            offsets_c(1)
+            checks(0)
+            checks(1)
+            for h in range(2):
+                act(T.own[:, 512 * h:512 * h + 512], T.xw[:].indirect(T.ow[:, 32 * h:32 * h + 32]), ACT.Copy,
+                    ["xw", "ow"], ["own%d" % h])
+            for c in range(4):
+                gather2(512 * c, 512 * c + 512, T.ob, "ob", T.dif0, T.ab0, "i")
+                absolute(512 * c, 512 * c + 512, T.dif0, T.ab0, "i")
+                sums(512 * c, 512 * c + 512, T.ab0, "i", False)
+            gather2(0, 512, T.oc, "oc0", T.dif, T.ab, "r")
+            ts(T.da[:, 0:64], T.pe0[:, 0:64], 0.5, ALU.add, ["pe0:e"], ["daa"])
+            cp(T.da[:, 64:128], T.pe1[:, 0:64], ["pe1:e"], ["dab"])
+            writer["da"] = writer["daa"] + writer["dab"]
+            absolute(0, 512, T.dif, T.ab, "r")
+            gather2(512, 1024, T.oc, "oc0", T.dif, T.ab, "r")
+            slot_max(T.da, "da", 5)
+            absolute(512, 1024, T.dif, T.ab, "r")
+        else:
+            offsets_c(0)
+            window_c(0)
+            to_sbuf_c(1)
+            gather2(0, 512, T.oc, "oc0", T.dif, T.ab, "r")
+            offsets_c(1)
+            checks(0)
+            absolute(0, 512, T.dif, T.ab, "r")
+            window_c(1)
+            gather2(512, 1024, T.oc, "oc0", T.dif, T.ab, "r")
+            checks(1)
+            absolute(512, 1024, T.dif, T.ab, "r")
+        open_sum("pe0")
+        penal("pe0", 0)
+        penal("pe0", 1)
+        sums(0, 512, T.ab, "r", True)
+        sums(512, 1024, T.ab, "r", True)
+        not_max("pe0", 5, True)
+        open_sum("pe1")
+        penal("pe1", 2)
+        penal("pe1", 3)
+        penal("pe1", 4)
+        gather2(*CH[2], T.oc, "oc1", T.dif, T.ab, "r")
+        absolute(*CH[2], T.dif, T.ab, "r")
+        sums(*CH[2], T.ab, "r", True)
+        tt(T.da1[:], T.da[:], E0, ALU.min, ["da", "pe0:e"], ["da1"])
+        tt(H0, T.da[:], E0, ALU.is_gt, ["da", "pe0:e"], ["pe0:h"])
+        gather2(*CH[3], T.oc, "oc1", T.dif, T.ab, "r")
+        absolute(*CH[3], T.dif, T.ab, "r")
+        sums(*CH[3], T.ab, "r", True)
+        slot_max(T.da1, "da1", 6)
+        tt(T0, T.dl0[:], H0, ALU.mult, ["dl0", "pe0:h"], ["pe0:t"])
+        gather2(*CH[4], T.oc, "oc1", T.dif, T.ab, "r")
+        absolute(*CH[4], T.dif, T.ab, "r")
+        not_max("pe1", 6, False)
+        b = "pe1"
+        lo, hi = CH[4]
+        last = [(y, d) for y in range(lo // 128, hi // 128) for d in range(2)]
+        for y, d in last:
+            c = 64 * d + 8 * (y % 8)
+            mm(T[b][:, c:c + 8], T.ab[:, 128 * y:128 * y + 128], T.selb[:, 0:8], ["abr%d" % lo, "selb"],
+               [b + ":e"], False, (y, d) == last[-1])
+        tt(T.dl2[:], T.dl1[:], T0, ALU.subtract, ["dl1", "pe0:t"], ["dl2"])
+        tt(T.u1[:], T.uf[:], T0, ALU.add, ["uf", "pe0:t"], ["u1"])
+        tt(H1, T.da1[:], E1, ALU.is_gt, ["da1", "pe1:e"], ["pe1:h"])
+        if t == RO - 1:
+            tt(T.da[:], T.da1[:], E1, ALU.min, ["da1", "pe1:e"], ["da"])
+        tt(T1, T.dl2[:], H1, ALU.mult, ["dl2", "pe1:h"], ["pe1:t"])
+        if t == RO - 1:
+            ts(T.da[:, 0:64], T.da[:, 0:64], -0.5, ALU.add, ["da"], ["da"])
+        tt(T.uf[:], T.u1[:], T1, ALU.add, ["u1", "pe1:t"], ["uf"])
+
+    dma("a", T.od2[:], T.da[:], "o2", ["da"], ["od2"])
+    dma("s", T.od1[:], T.uf[:], "o1", ["uf"], ["od1"])
+    dma("a", T.ol2[r], T.da[mine, :], "o4", ["da"], ["ol2own"])
+    dma("s", T.ol1[r], T.uf[mine, :], "o3", ["uf"], ["ol1own"])
+    need("g", ["od1", "od2"], [])
+    back = []
+    for k, s in enumerate(others):
+        back.append(RemoteDMATransfer(dst_ids=[dst(s)], dma_engine_mask=bits(eng[2 * k:2 * k + 1]),
+                                      remote_sem=S.oarr, src=T.od1[s], dst=T.ol1[r]))
+        back.append(RemoteDMATransfer(dst_ids=[dst(s)], dma_engine_mask=bits(eng[2 * k + 1:2 * k + 2]),
+                                      remote_sem=S.oarr, src=T.od2[s], dst=T.ol2[r]))
+    g.remote_dma_fused(back, local_sem=S.osent)
+    writer["ol"] = [("oarr", 2 * (N - 1))]
+    dma("s", T.ynb[:], T.ol1[:], "y1", ["ol", "ol1own"], ["y1"])
+    dma("a", T.yd[:], T.ol2[:], "y2", ["ol", "ol2own"], ["y2"])
+    for tok in [("nbsent", 2 * (N - 1)), ("xsent", sent), ("osent", 2 * (N - 1)), ("cv", count["v"]),
+                ("ca", count["a"]), ("cp", count["p"]), ("cg", count["g"]), ("y1", 16), ("y2", 16)]:
+        wait("g", tok)

@@ -7,65 +7,33 @@ RO = 4
 BIG = 8192.0
 BANKS = ["pw0", "pw1", "pc0", "pc1", "pb0", "pb1", "pe0", "pe1"]
 
-SCRATCH = {
-    "xs": ("sbuf", [128, V], "bfloat16"),
-    "xr": ("sbuf", [128, N * V], "bfloat16"),
-    "xw": ("sbuf", [128, N * V], "bfloat16"),
-    "own": ("sbuf", [128, V], "bfloat16"),
-    "nbd": ("dram", [N, 128, 16], "int32"),
-    "nbl": ("dram", [N, 128, 16], "int32"),
-    "od1": ("dram", [N, 128, 16], "float32"),
-    "od2": ("dram", [N, 128, 16], "float32"),
-    "ol1": ("dram", [N, 128, 16], "float32"),
-    "ol2": ("dram", [N, 128, 16], "float32"),
-    "pidx": ("sbuf", [128, 8], "int32"),
-    "pbit": ("sbuf", [128, 8], "int32"),
-    "pflt": ("sbuf", [128, 8], "float32"),
-    "pcol": ("sbuf", [128, 8], "float32"),
-    "j16": ("sbuf", [128, 128], "float32"),
-    "j128": ("sbuf", [128, 128], "float32"),
-    "owi": ("sbuf", [128, 64], "int32"),
-    "sob": ("sbuf", [128, 16], "float32"),
-    "per": ("sbuf", [128, 128], "bfloat16"),
-    "sel": ("sbuf", [128, 8], "float32"),
-    "selb": ("sbuf", [128, 16], "bfloat16"),
-    "repb": ("sbuf", [128, 1024], "bfloat16"),
-    "repf": ("sbuf", [128, 1024], "float32"),
-    "bi": ("sbuf", [128, 128], "bfloat16"),
-    "nbi": ("sbuf", [128, 128], "bfloat16"),
-    "k0": ("sbuf", [128, 128], "bfloat16"),
-    "wa": ("sbuf", [128, 64], "float32"),
-    "ow": ("sbuf", [128, 64], "uint16"),
-    "so": ("sbuf", [128, 16], "uint16"),
-    "ol": ("sbuf", [128, 128], "uint16"),
-    "of": ("sbuf", [128, 128], "uint16"),
-    "oc": ("sbuf", [128, 128], "uint16"),
-    "ob": ("sbuf", [128, 128], "uint16"),
-    "ui": ("sbuf", [128, 128], "int32"),
-    "lo32": ("sbuf", [128, 128], "int32"),
-    "of32": ("sbuf", [128, 128], "int32"),
-    "uf": ("sbuf", [128, 128], "float32"),
-    "u1": ("sbuf", [128, 128], "float32"),
-    "da": ("sbuf", [128, 128], "float32"),
-    "da1": ("sbuf", [128, 128], "float32"),
-    "dl0": ("sbuf", [128, 128], "float32"),
-    "dl1": ("sbuf", [128, 128], "float32"),
-    "dl2": ("sbuf", [128, 128], "float32"),
-    "eq": ("sbuf", [128, 448], "bfloat16"),
-    "win": ("sbuf", [128, 1024], "float32"),
-    "cw": ("sbuf", [128, 1024], "float32"),
-    "cb": ("sbuf", [128, 128], "float32"),
-    "msk": ("sbuf", [128, 2048], "bfloat16"),
-    "g1": ("sbuf", [128, 2048], "float32"),
-    "dif": ("sbuf", [128, 2048], "bfloat16"),
-    "ab": ("sbuf", [128, 2048], "bfloat16"),
-    "dif0": ("sbuf", [128, 2048], "bfloat16"),
-    "ab0": ("sbuf", [128, 2048], "bfloat16"),
-}
-for _b in BANKS:
-    SCRATCH[_b] = ("psum", [128, 512], "float32")
+SCRATCH = {}
+for _names, _where, _shape, _dt in [
+        ("xs own repb", "sbuf", [128, V], "bfloat16"),
+        ("xr xw", "sbuf", [128, N * V], "bfloat16"),
+        ("nbd nbl", "dram", [N, 128, 16], "int32"),
+        ("od1 od2 ol1 ol2", "dram", [N, 128, 16], "float32"),
+        ("pidx pbit", "sbuf", [128, 8], "int32"),
+        ("pflt pcol sel", "sbuf", [128, 8], "float32"),
+        ("j16 j128 uf u1 da da1 dl0 dl1 dl2 cb", "sbuf", [128, 128], "float32"),
+        ("owi", "sbuf", [128, 64], "int32"),
+        ("sob", "sbuf", [128, 16], "float32"),
+        ("per bi nbi k0", "sbuf", [128, 128], "bfloat16"),
+        ("selb", "sbuf", [128, 16], "bfloat16"),
+        ("repf win cw", "sbuf", [128, V], "float32"),
+        ("wa", "sbuf", [128, 64], "float32"),
+        ("ow", "sbuf", [128, 64], "uint16"),
+        ("so", "sbuf", [128, 16], "uint16"),
+        ("ol of oc ob", "sbuf", [128, 128], "uint16"),
+        ("ui lo32 of32", "sbuf", [128, 128], "int32"),
+        ("eq", "sbuf", [128, 448], "bfloat16"),
+        ("msk dif ab dif0 ab0", "sbuf", [128, 2048], "bfloat16"),
+        ("g1", "sbuf", [128, 2048], "float32"),
+        (" ".join(BANKS), "psum", [128, 512], "float32")]:
+    for _n in _names.split():
+        SCRATCH[_n] = (_where, _shape, _dt)
 
-SEMAPHORES = ["cv", "ca", "cp", "cg", "xld", "nbs", "nbo", "nbarr", "nbsent", "nbld", "xarr", "xsent",
+SEMAPHORES = ["cv", "ca", "cp", "cg", "xld", "xo", "nbs", "nbo", "nbarr", "nbsent", "nbld", "xarr", "xsent",
               "o1", "o2", "o3", "o4", "oarr", "osent", "y1", "y2"]
 
 
@@ -203,8 +171,7 @@ def rank_program(g, core, T, topo):
     ts(T.per[:], T.j16[:], T.pflt[:, 0:1], ALU.is_equal, ["j16", "pflt"], ["per"])
     ts(T.sel[:], T.j16[:, 0:8], T.pflt[:, 1:2], ALU.is_equal, ["j16", "pflt"], ["sel"])
     xcalls = x_calls(T, topo, r)
-    xorder = [s for c in xcalls for s, _ in c] + [r]
-    for s in xorder:
+    for s in [s for c in xcalls for s, _ in c]:
         ts(T.repb[:, 128 * s:128 * s + 128], T.per[:], T.sel[:, s:s + 1], ALU.mult, ["per", "sel"], ["repb%d" % s])
     for s in range(N):
         op("a", lambda: a.activation(T.repf[:, 128 * s:128 * s + 128], T.per[:], ACT.Identity,
@@ -216,22 +183,21 @@ def rank_program(g, core, T, topo):
                         for k, s in enumerate(others)], local_sem=S.nbsent)
     writer["nbl"] = [("nbarr", 2 * (N - 1))]
     dma("s", T.ui[:], T.nbl[:], "nbld", ["nbl", "nblown"], ["ui"])
+    for b in range(N):
+        g.sync.dma_start(T.xw[16 * b:16 * b + 16, V * r:V * r + V], T.x[mine, :]).then_inc(S.xo, 16)
 
     rot = [("pw0", "pw1"), ("pc0", "pc1")]
     sent = 0
     nx = 0
-    for call in xcalls + [[(r, None)]]:
+    for call in xcalls:
         for s, _ in call:
             b0, b1 = rot[nx % 2]
             nx += 1
-            to = T.xw if s == r else T.xr
             lhs = T.repb[:, 128 * s:128 * s + 128]
             mm(T[b0][:], lhs, T.xs[:, 0:512], ["repb%d" % s, "xs"], [b0])
             mm(T[b1][:], lhs, T.xs[:, 512:V], ["repb%d" % s, "xs"], [b1])
-            cp(to[:, V * s:V * s + 512], T[b0][:], [b0], ["xr%da" % s])
-            act(to[:, V * s + 512:V * s + V], T[b1][:], ACT.Copy, [b1], ["xr%db" % s])
-        if call[0][0] == r:
-            break
+            cp(T.xr[:, V * s:V * s + 512], T[b0][:], [b0], ["xr%da" % s])
+            act(T.xr[:, V * s + 512:V * s + V], T[b1][:], ACT.Copy, [b1], ["xr%db" % s])
         need("g", [k % s for s, _ in call for k in ("xr%da", "xr%db")], [])
         if len(call) == 1:
             s, e = call[0]
@@ -243,18 +209,20 @@ def rank_program(g, core, T, topo):
                                 for s, e in call], local_sem=S.xsent)
         sent += sum(len(e) for _, e in call)
     arrive = sum(len(e) for q in others for c in x_calls(T, topo, q) for s, e in c if s == r)
-    writer["xw"] = [("xarr", arrive)] + writer["xr%da" % r] + writer["xr%db" % r]
+    writer["xw"] = [("xarr", arrive), ("xo", 16 * N)]
 
-    cp(T.selb[:, 0:8], T.sel[:], ["sel"], ["selb"])
-    ts(T.pcol[:, 0:1], T.pflt[:, 2:3], 64.0, ALU.mult, ["pflt"], ["pc0_"], T.pflt[:, 3:4], ALU.add)
-    ts(T.pcol[:, 1:2], T.pflt[:, 1:2], 1024.0, ALU.mult, ["pflt"], ["pc1_"], T.pflt[:, 0:1], ALU.add)
-    ts(T.bi[:], T.j128[:], T.pflt[:, 4:5], ALU.is_equal, ["j128", "pf4"], ["bi"], BIG, ALU.mult)
-    ts(T.nbi[:], T.j128[:], T.pflt[:, 4:5], ALU.is_equal, ["j128", "pf4"], ["nbi"], -BIG, ALU.mult)
-    ts(T.so[:], T.sob[:], T.pcol[:, 0:1], ALU.add, ["sob0", "sob1", "pc0_", "pflt"], ["so"], T.pflt[:, 1:2], ALU.add)
-    ts(T.wa[:], T.j128[:, 0:64], 16.0, ALU.mult, ["j128", "pc1_"], ["wa"], T.pcol[:, 1:2], ALU.add)
-    cp(T.ow[:], T.owi[:], ["owi"], ["ow"])
-    op("v", lambda: v.memset(T.k0[:, 0:64], 0.5 / BIG), [], ["k0a"])
-    op("v", lambda: v.memset(T.k0[:, 64:128], 1.0), [], ["k0b"])
+    def round_constants():
+        cp(T.ow[:], T.owi[:], ["owi"], ["ow"])
+        cp(T.selb[:, 0:8], T.sel[:], ["sel"], ["selb"])
+        ts(T.pcol[:, 0:1], T.pflt[:, 2:3], 64.0, ALU.mult, ["pflt"], ["pc0_"], T.pflt[:, 3:4], ALU.add)
+        ts(T.pcol[:, 1:2], T.pflt[:, 1:2], 1024.0, ALU.mult, ["pflt"], ["pc1_"], T.pflt[:, 0:1], ALU.add)
+        ts(T.bi[:], T.j128[:], T.pflt[:, 4:5], ALU.is_equal, ["j128", "pf4"], ["bi"], BIG, ALU.mult)
+        ts(T.nbi[:], T.j128[:], T.pflt[:, 4:5], ALU.is_equal, ["j128", "pf4"], ["nbi"], -BIG, ALU.mult)
+        ts(T.so[:], T.sob[:], T.pcol[:, 0:1], ALU.add, ["sob0", "sob1", "pc0_", "pflt"], ["so"],
+           T.pflt[:, 1:2], ALU.add)
+        ts(T.wa[:], T.j128[:, 0:64], 16.0, ALU.mult, ["j128", "pc1_"], ["wa"], T.pcol[:, 1:2], ALU.add)
+        op("v", lambda: v.memset(T.k0[:, 0:64], 0.5 / BIG), [], ["k0a"])
+        op("v", lambda: v.memset(T.k0[:, 64:128], 1.0), [], ["k0b"])
 
     REPF = ["repf%d" % s for s in range(N)]
 
@@ -312,7 +280,7 @@ def rank_program(g, core, T, topo):
     def eqc(k):
         return T.eq[:, 64 * k:64 * k + 64]
 
-    def penal(b, k, stop=False):
+    def penal(b, k):
         for d in range(2):
             mm(T[b][:, 64 * d:64 * d + 64], T.bi[:], eqc(k), ["bi", "eq%d" % k], [b + ":e"], False, False)
 
@@ -341,6 +309,18 @@ def rank_program(g, core, T, topo):
     T0, T1 = T.pe0[:, 256:384], T.pe1[:, 256:384]
     CH = [(0, 512), (512, 1024), (1024, 1536), (1536, 1792), (1792, 2048)]
 
+    def first_sum():
+        open_sum("pe0")
+        penal("pe0", 0)
+        penal("pe0", 1)
+        sums(0, 512, T.ab, "r", True)
+        sums(512, 1024, T.ab, "r", True)
+        not_max("pe0", 5, True)
+
+    def first_step():
+        tt(T.da1[:], T.da[:], E0, ALU.min, ["da", "pe0:e"], ["da1"])
+        tt(H0, T.da[:], E0, ALU.is_gt, ["da", "pe0:e"], ["pe0:h"])
+
     cp(T.uf[:], T.ui[:], ["ui"], ["uf"])
     for t in range(RO):
         s0, s1 = t % 2, (t + 1) % 2
@@ -354,6 +334,8 @@ def rank_program(g, core, T, topo):
         cp(T.of[:], T.of32[:], ["of32"], ["of"])
         if t > 0:
             tt(T.da[:], T.da1[:], E1, ALU.min, ["da1", "pe1:e"], ["da"])
+        else:
+            round_constants()
         cp(T.win[:, 512 * s0:512 * s0 + 256], T.pw0[:, 0:256], bank_keys("pw0", range(4)), ["win%da" % s0])
         if t > 0:
             slot_max(T.da, "da", 5)
@@ -367,67 +349,72 @@ def rank_program(g, core, T, topo):
         gather1(0, t)
         gather1(1, t)
         gather1(2, t)
-        to_sbuf_c(0)
-        gather1(3, t)
         if t == 0:
+            to_sbuf_c(0)
             op("v", lambda: v.tensor_copy(T.ob[:], T.win[:].indirect(T.so[:, 0:8])),
                ["win0a", "win0b", "win1a", "win1b", "so"], ["ob"])
+            gather1(3, t)
+            act(T.own[:, 0:512], T.xw[:].indirect(T.ow[:, 0:32]), ACT.Copy, ["xw", "ow"], ["own0"])
+            act(T.own[:, 512:V], T.xw[:].indirect(T.ow[:, 32:64]), ACT.Copy, ["xw", "ow"], ["own1"])
             to_sbuf_c(1)
             window_c(0)
-            window_c(1)
             offsets_c(0)
-            offsets_c(1)
-            checks(0)
-            checks(1)
-            for h in range(2):
-                act(T.own[:, 512 * h:512 * h + 512], T.xw[:].indirect(T.ow[:, 32 * h:32 * h + 32]), ACT.Copy,
-                    ["xw", "ow"], ["own%d" % h])
             for c in range(4):
                 gather2(512 * c, 512 * c + 512, T.ob, "ob", T.dif0, T.ab0, "i")
                 absolute(512 * c, 512 * c + 512, T.dif0, T.ab0, "i")
                 sums(512 * c, 512 * c + 512, T.ab0, "i", False)
+                if c == 1:
+                    window_c(1)
+            offsets_c(1)
+            checks(0)
             gather2(0, 512, T.oc, "oc0", T.dif, T.ab, "r")
             ts(T.da[:, 0:64], T.pe0[:, 0:64], 0.5, ALU.add, ["pe0:e"], ["daa"])
             cp(T.da[:, 64:128], T.pe1[:, 0:64], ["pe1:e"], ["dab"])
             writer["da"] = writer["daa"] + writer["dab"]
+            checks(1)
             absolute(0, 512, T.dif, T.ab, "r")
             gather2(512, 1024, T.oc, "oc0", T.dif, T.ab, "r")
             slot_max(T.da, "da", 5)
             absolute(512, 1024, T.dif, T.ab, "r")
+            first_sum()
+            open_sum("pe1")
+            gather2(*CH[2], T.oc, "oc1", T.dif, T.ab, "r")
+            absolute(*CH[2], T.dif, T.ab, "r")
+            sums(*CH[2], T.ab, "r", True)
+            first_step()
+            gather2(*CH[3], T.oc, "oc1", T.dif, T.ab, "r")
         else:
-            offsets_c(0)
+            cp(T.oc[:, 0:64], T.pb0[:, 0:64], bank_keys("pb0", range(8)), ["oc0"])
+            to_sbuf_c(0)
+            act(T.dif[:, 0:512], T.xw[:].indirect(T.oc[:, 0:32]), ACT.Copy, ["xw", "oc0"], ["difr0"])
+            gather1(3, t)
+            mm(T.pw1[:], T.bi[:], T.dif[:, 0:512], ["bi", "difr0"], ["pw1:x"], True, False)
+            mm(T.pw1[:], T.nbi[:], T.own[:, 0:512], ["nbi", "own0"], ["pw1:x"], False, True)
             window_c(0)
             to_sbuf_c(1)
-            gather2(0, 512, T.oc, "oc0", T.dif, T.ab, "r")
+            gather2(*CH[1], T.oc, "oc0", T.dif, T.ab, "r")
             offsets_c(1)
             checks(0)
-            absolute(0, 512, T.dif, T.ab, "r")
+            op("a", lambda: a.activation(T.ab[:, 0:512], T.pw1[:], ACT.Abs, scale=1.0 / BIG), ["pw1:x"], ["abr0"])
+            absolute(*CH[1], T.dif, T.ab, "r")
             window_c(1)
-            gather2(512, 1024, T.oc, "oc0", T.dif, T.ab, "r")
+            first_sum()
+            open_sum("pe1")
+            gather2(*CH[2], T.oc, "oc1", T.dif, T.ab, "r")
+            absolute(*CH[2], T.dif, T.ab, "r")
+            sums(*CH[2], T.ab, "r", True)
+            gather2(*CH[3], T.oc, "oc1", T.dif, T.ab, "r")
+            first_step()
             checks(1)
-            absolute(512, 1024, T.dif, T.ab, "r")
-        open_sum("pe0")
-        penal("pe0", 0)
-        penal("pe0", 1)
-        sums(0, 512, T.ab, "r", True)
-        sums(512, 1024, T.ab, "r", True)
-        not_max("pe0", 5, True)
-        open_sum("pe1")
-        penal("pe1", 2)
-        penal("pe1", 3)
-        penal("pe1", 4)
-        gather2(*CH[2], T.oc, "oc1", T.dif, T.ab, "r")
-        absolute(*CH[2], T.dif, T.ab, "r")
-        sums(*CH[2], T.ab, "r", True)
-        tt(T.da1[:], T.da[:], E0, ALU.min, ["da", "pe0:e"], ["da1"])
-        tt(H0, T.da[:], E0, ALU.is_gt, ["da", "pe0:e"], ["pe0:h"])
-        gather2(*CH[3], T.oc, "oc1", T.dif, T.ab, "r")
         absolute(*CH[3], T.dif, T.ab, "r")
         sums(*CH[3], T.ab, "r", True)
         slot_max(T.da1, "da1", 6)
         tt(T0, T.dl0[:], H0, ALU.mult, ["dl0", "pe0:h"], ["pe0:t"])
         gather2(*CH[4], T.oc, "oc1", T.dif, T.ab, "r")
         absolute(*CH[4], T.dif, T.ab, "r")
+        penal("pe1", 2)
+        penal("pe1", 3)
+        penal("pe1", 4)
         not_max("pe1", 6, False)
         b = "pe1"
         lo, hi = CH[4]

@@ -15,10 +15,10 @@ for _names, _where, _shape, _dt in [
         ("od1 od2 ol1 ol2", "dram", [N, 128, 16], "float32"),
         ("pidx pbit", "sbuf", [128, 8], "int32"),
         ("pflt pcol sel", "sbuf", [128, 8], "float32"),
-        ("j16 j128 uf u1 da da1 dl0 dl1 dl2 cb", "sbuf", [128, 128], "float32"),
+        ("j16 j128 uf u1 da da1 dl0 dl1 dl2", "sbuf", [128, 128], "float32"),
         ("owi", "sbuf", [128, 64], "int32"),
         ("sob", "sbuf", [128, 16], "float32"),
-        ("per bi nbi k0", "sbuf", [128, 128], "bfloat16"),
+        ("per bi nbi k0 ch cl", "sbuf", [128, 128], "bfloat16"),
         ("selb", "sbuf", [128, 16], "bfloat16"),
         ("repf win cw", "sbuf", [128, V], "float32"),
         ("wa", "sbuf", [128, 64], "float32"),
@@ -171,18 +171,28 @@ def rank_program(g, core, T, topo):
     ts(T.per[:], T.j16[:], T.pflt[:, 0:1], ALU.is_equal, ["j16", "pflt"], ["per"])
     ts(T.sel[:], T.j16[:, 0:8], T.pflt[:, 1:2], ALU.is_equal, ["j16", "pflt"], ["sel"])
     xcalls = x_calls(T, topo, r)
-    for s in [s for c in xcalls for s, _ in c]:
+    for s in [s for c in xcalls for s, _ in c] + [r]:
         ts(T.repb[:, 128 * s:128 * s + 128], T.per[:], T.sel[:, s:s + 1], ALU.mult, ["per", "sel"], ["repb%d" % s])
     for s in range(N):
         op("a", lambda: a.activation(T.repf[:, 128 * s:128 * s + 128], T.per[:], ACT.Identity,
                                      scale=T.sel[:, s:s + 1]), ["per", "sel"], ["repf%d" % s])
+    cp(T.ow[:], T.owi[:], ["owi"], ["ow"])
+    cp(T.selb[:, 0:8], T.sel[:], ["sel"], ["selb"])
+    ts(T.pcol[:, 0:1], T.pflt[:, 2:3], 64.0, ALU.mult, ["pflt"], ["pc0_"], T.pflt[:, 3:4], ALU.add)
+    ts(T.pcol[:, 1:2], T.pflt[:, 1:2], 1024.0, ALU.mult, ["pflt"], ["pc1_"], T.pflt[:, 0:1], ALU.add)
+    ts(T.bi[:], T.j128[:], T.pflt[:, 4:5], ALU.is_equal, ["j128", "pf4"], ["bi"], BIG, ALU.mult)
+    ts(T.nbi[:], T.j128[:], T.pflt[:, 4:5], ALU.is_equal, ["j128", "pf4"], ["nbi"], -BIG, ALU.mult)
+    ts(T.so[:], T.sob[:], T.pcol[:, 0:1], ALU.add, ["sob0", "sob1", "pc0_", "pflt"], ["so"], T.pflt[:, 1:2], ALU.add)
+    ts(T.wa[:], T.j128[:, 0:64], 16.0, ALU.mult, ["j128", "pc1_"], ["wa"], T.pcol[:, 1:2], ALU.add)
+    op("v", lambda: v.memset(T.k0[:, 0:64], 0.5 / BIG), [], ["k0a"])
+    op("v", lambda: v.memset(T.k0[:, 64:128], 1.0), [], ["k0b"])
 
     need("g", ["nbd"], [])
     g.remote_dma_fused([RemoteDMATransfer(dst_ids=[dst(s)], dma_engine_mask=bits(eng[2 * k:2 * k + 2]),
                                           remote_sem=S.nbarr, src=T.nbd[s], dst=T.nbl[r])
                         for k, s in enumerate(others)], local_sem=S.nbsent)
     writer["nbl"] = [("nbarr", 2 * (N - 1))]
-    dma("s", T.ui[:], T.nbl[:], "nbld", ["nbl", "nblown"], ["ui"])
+    dma("s", T.ui[:], T.nbl[:], "nbld", ["nbl", "nblown"], ["ui0", "ui1"])
     for b in range(N):
         g.sync.dma_start(T.xw[16 * b:16 * b + 16, V * r:V * r + V], T.x[mine, :]).then_inc(S.xo, 16)
 
@@ -211,34 +221,19 @@ def rank_program(g, core, T, topo):
     arrive = sum(len(e) for q in others for c in x_calls(T, topo, q) for s, e in c if s == r)
     writer["xw"] = [("xarr", arrive), ("xo", 16 * N)]
 
-    def round_constants():
-        cp(T.ow[:], T.owi[:], ["owi"], ["ow"])
-        cp(T.selb[:, 0:8], T.sel[:], ["sel"], ["selb"])
-        ts(T.pcol[:, 0:1], T.pflt[:, 2:3], 64.0, ALU.mult, ["pflt"], ["pc0_"], T.pflt[:, 3:4], ALU.add)
-        ts(T.pcol[:, 1:2], T.pflt[:, 1:2], 1024.0, ALU.mult, ["pflt"], ["pc1_"], T.pflt[:, 0:1], ALU.add)
-        ts(T.bi[:], T.j128[:], T.pflt[:, 4:5], ALU.is_equal, ["j128", "pf4"], ["bi"], BIG, ALU.mult)
-        ts(T.nbi[:], T.j128[:], T.pflt[:, 4:5], ALU.is_equal, ["j128", "pf4"], ["nbi"], -BIG, ALU.mult)
-        ts(T.so[:], T.sob[:], T.pcol[:, 0:1], ALU.add, ["sob0", "sob1", "pc0_", "pflt"], ["so"],
-           T.pflt[:, 1:2], ALU.add)
-        ts(T.wa[:], T.j128[:, 0:64], 16.0, ALU.mult, ["j128", "pc1_"], ["wa"], T.pcol[:, 1:2], ALU.add)
-        op("v", lambda: v.memset(T.k0[:, 0:64], 0.5 / BIG), [], ["k0a"])
-        op("v", lambda: v.memset(T.k0[:, 64:128], 1.0), [], ["k0b"])
-
-    REPF = ["repf%d" % s for s in range(N)]
-
     def repeat(banks, src, key):
         per_bank = N // len(banks)
         for k in range(N):
             b = banks[k // per_bank]
             c = 64 * (k % per_bank)
-            mm(T[b][:, c:c + 64], T.repf[:, 128 * k:128 * k + 128], src, [key, REPF[k]], [b + ":%d" % k])
+            mm(T[b][:, c:c + 64], T.repf[:, 128 * k:128 * k + 128], src, [key, "repf%d" % k], [b + ":%d" % k])
 
     def bank_keys(b, ks):
         return [b + ":%d" % k for k in ks]
 
     def mask(c):
         act(T.msk[:, 512 * c:512 * c + 512], T.per[:, 0:16].indirect(T.ol[:, 32 * c:32 * c + 32]), ACT.Copy,
-            ["per", "ol"], ["msk%d" % c])
+            ["per", "ol%d" % (c // 2)], ["msk%d" % c])
 
     def gather1(c, t):
         s = (c // 2 + t) % 2
@@ -250,32 +245,40 @@ def rank_program(g, core, T, topo):
             mm(T[b][:, 8 * (y % 8):8 * (y % 8) + 8], T.g1[:, 128 * y:128 * y + 128], T.sel[:],
                ["g1%d" % c, "sel"], [b + ":%d" % (y % 8)])
 
+    OWN = [(0, 256), (256, 512), (512, V)]
+
+    def own_keys(lo, hi):
+        return ["own%d" % x for x, y in OWN if x < hi and lo < y]
+
     def gather2(lo, hi, off, okey, dif, ab, tag):
         o = lo % V
         tt(dif[:, lo:hi], T.xw[:].indirect(off[:, lo // 16:hi // 16]), T.own[:, o:o + hi - lo], ALU.subtract,
-           ["xw", okey, "own%d" % (o // 512)], ["dif%s%d" % (tag, lo)])
+           ["xw", okey] + own_keys(o, o + hi - lo), ["dif%s%d" % (tag, lo)])
 
     def absolute(lo, hi, dif, ab, tag):
         act(ab[:, lo:hi], dif[:, lo:hi], ACT.Abs, ["dif%s%d" % (tag, lo)], ["ab%s%d" % (tag, lo)])
 
-    def sums(lo, hi, ab, tag, twice):
+    def sums(lo, hi, ab, tag, twice, close=False):
         b = "pe%d" % (lo // V)
-        for y in range(lo // 128, hi // 128):
-            for d in range(2 if twice else 1):
-                c = 64 * d + 8 * (y % 8)
-                mm(T[b][:, c:c + 8], ab[:, 128 * y:128 * y + 128], T.selb[:, 0:8], ["ab%s%d" % (tag, lo), "selb"],
-                   [b + ":e"], start=not twice, stop=not twice)
+        todo = [(y, d) for y in range(lo // 128, hi // 128) for d in range(2 if twice else 1)]
+        for y, d in todo:
+            c = 64 * d + 8 * (y % 8)
+            mm(T[b][:, c:c + 8], ab[:, 128 * y:128 * y + 128], T.selb[:, 0:8], ["ab%s%d" % (tag, lo), "selb"],
+               [b + ":e"], not twice, not twice or (close and (y, d) == todo[-1]))
 
-    def to_sbuf_c(i):
-        act(T.cb[:, 64 * i:64 * i + 64], T["pb%d" % i][:, 0:64], ACT.Copy, bank_keys("pb%d" % i, range(8)),
-            ["cb%d" % i])
-        repeat(["pc%d" % i], T.cb[:, 64 * i:64 * i + 64], "cb%d" % i)
+    def digits_c(i):
+        h = slice(64 * i, 64 * i + 64)
+        src, ks = T["pb%d" % i][:, 0:64], bank_keys("pb%d" % i, range(8))
+        cp(T.ch[:, h], src, ks, ["ch%d" % i])
+        cp(T.oc[:, h], src, ks, ["oc%d" % i])
+        tt(T.cl[:, h], src, T.ch[:, h], ALU.subtract, ks + ["ch%d" % i], ["cl%d" % i])
+        for k in range(N):
+            out, lhs = T["pc%d" % i][:, 64 * k:64 * k + 64], T.repb[:, 128 * k:128 * k + 128]
+            mm(out, lhs, T.ch[:, h], ["ch%d" % i, "repb%d" % k], ["pc%d:%d" % (i, k)], True, False)
+            mm(out, lhs, T.cl[:, h], ["cl%d" % i, "repb%d" % k], ["pc%d:%d" % (i, k)], False, True)
 
     def window_c(i):
         act(T.cw[:, 512 * i:512 * i + 512], T["pc%d" % i][:], ACT.Copy, bank_keys("pc%d" % i, range(8)), ["cw%d" % i])
-
-    def offsets_c(i):
-        cp(T.oc[:, 64 * i:64 * i + 64], T.cb[:, 64 * i:64 * i + 64], ["cb%d" % i], ["oc%d" % i])
 
     def eqc(k):
         return T.eq[:, 64 * k:64 * k + 64]
@@ -291,10 +294,12 @@ def rank_program(g, core, T, topo):
     def open_sum(b):
         mm(T[b][:, 0:128], T.bi[:], T.k0[:], ["bi", "k0a", "k0b"], [b + ":e"], True, False)
 
+    UF = ["uf0", "uf1"]
+
     def checks(i):
         dl = T.dl0 if i == 0 else T.dl1
         w = T.cw[:, 512 * i:512 * i + 512]
-        tt(dl[:], w.indirect(T.so[:, 8:16]), T.uf[:], ALU.subtract, ["cw%d" % i, "so", "uf"], ["dl%d" % i])
+        tt(dl[:], w.indirect(T.so[:, 8:16]), T.uf[:], ALU.subtract, ["cw%d" % i, "so"] + UF, ["dl%d" % i])
         tt(eqc(2 * i), w.indirect(T.so[:, 0:4]), T.wa[:], ALU.is_equal, ["cw%d" % i, "so", "wa"], ["eq%d" % (2 * i)])
         half = dl[:, 64:128] if i == 0 else dl[:, 0:64]
         ts(eqc(2 * i + 1), half, 0.0, ALU.is_equal, ["dl%d" % i], ["eq%d" % (2 * i + 1)])
@@ -305,9 +310,8 @@ def rank_program(g, core, T, topo):
         tt(eqc(k), src[:, 64:128], src[:, 0:64], ALU.is_gt, [key], ["eq%d" % k])
 
     E0, E1 = T.pe0[:, 0:128], T.pe1[:, 0:128]
-    H0, H1 = T.pe0[:, 128:256], T.pe1[:, 128:256]
-    T0, T1 = T.pe0[:, 256:384], T.pe1[:, 256:384]
-    CH = [(0, 512), (512, 1024), (1024, 1536), (1536, 1792), (1792, 2048)]
+    H0, T0 = T.pe0[:, 128:256], T.pe0[:, 256:384]
+    CH = [(0, 512), (512, 1024), (1024, 1536), (1536, 1920), (1920, 2048)]
 
     def first_sum():
         open_sum("pe0")
@@ -321,122 +325,145 @@ def rank_program(g, core, T, topo):
         tt(T.da1[:], T.da[:], E0, ALU.min, ["da", "pe0:e"], ["da1"])
         tt(H0, T.da[:], E0, ALU.is_gt, ["da", "pe0:e"], ["pe0:h"])
 
-    cp(T.uf[:], T.ui[:], ["ui"], ["uf"])
+    SUB = ["pw1", "pw0"]
+
+    def scalar_gather(k):
+        lo, hi = CH[k]
+        act(T.dif[:, lo:hi], T.xw[:].indirect(T.oc[:, lo // 16:hi // 16]), ACT.Copy, ["xw", "oc0"], ["difr%d" % lo])
+
+    def tensor_subtract(k):
+        lo, hi = CH[k]
+        mm(T[SUB[k]][:], T.bi[:], T.dif[:, lo:hi], ["bi", "difr%d" % lo], [SUB[k] + ":x"], True, False)
+        mm(T[SUB[k]][:], T.nbi[:], T.own[:, lo:hi], ["nbi"] + own_keys(lo, hi), [SUB[k] + ":x"], False, True)
+
+    def scalar_abs(k):
+        lo, hi = CH[k]
+        op("a", lambda: a.activation(T.ab[:, lo:hi], T[SUB[k]][:], ACT.Abs, scale=1.0 / BIG), [SUB[k] + ":x"],
+           ["abr%d" % lo])
+
+    def lists():
+        ts(T.lo32[:, 0:64], T.ui[:, 0:64], 15, ALU.bitwise_and, ["ui0"], ["lo32a"])
+        ts(T.of32[:], T.ui[:], 4, ALU.logical_shift_right, ["ui0", "ui1"], ["of32"])
+        cp(T.ol[:, 0:64], T.lo32[:, 0:64], ["lo32a"], ["ol0"])
+        ts(T.lo32[:, 64:128], T.ui[:, 64:128], 15, ALU.bitwise_and, ["ui1"], ["lo32b"])
+        cp(T.of[:], T.of32[:], ["of32"], ["of"])
+        cp(T.ol[:, 64:128], T.lo32[:, 64:128], ["lo32b"], ["ol1"])
+
+    def round_gather(k):
+        gather2(*CH[k], T.oc, "oc%d" % (CH[k][0] // V), T.dif, T.ab, "r")
+
+    def round_abs(k):
+        absolute(*CH[k], T.dif, T.ab, "r")
+
+    cp(T.uf[:], T.ui[:], ["ui0"], UF)
     for t in range(RO):
         s0, s1 = t % 2, (t + 1) % 2
-        repeat(["pw0", "pc0"], T.uf[:, 64 * s0:64 * s0 + 64], "uf")
-        repeat(["pw1"], T.uf[:, 64 * s1:64 * s1 + 64], "uf")
-        if t > 0:
-            tt(T.ui[:], T.u1[:], T1, ALU.add, ["u1", "pe1:t"], ["ui"])
-        ts(T.lo32[:], T.ui[:], 15, ALU.bitwise_and, ["ui"], ["lo32"])
-        ts(T.of32[:], T.ui[:], 4, ALU.logical_shift_right, ["ui"], ["of32"])
-        cp(T.ol[:], T.lo32[:], ["lo32"], ["ol"])
-        cp(T.of[:], T.of32[:], ["of32"], ["of"])
-        if t > 0:
-            tt(T.da[:], T.da1[:], E1, ALU.min, ["da1", "pe1:e"], ["da"])
-        else:
-            round_constants()
+        repeat(["pw0", "pc0"], T.uf[:, 64 * s0:64 * s0 + 64], "uf%d" % s0)
+        repeat(["pw1", "pc1"], T.uf[:, 64 * s1:64 * s1 + 64], "uf%d" % s1)
+        lists()
         cp(T.win[:, 512 * s0:512 * s0 + 256], T.pw0[:, 0:256], bank_keys("pw0", range(4)), ["win%da" % s0])
-        if t > 0:
-            slot_max(T.da, "da", 5)
         cp(T.win[:, 512 * s0 + 256:512 * s0 + 512], T.pc0[:, 0:256], bank_keys("pc0", range(4, 8)), ["win%db" % s0])
         mask(0)
         mask(1)
-        act(T.win[:, 512 * s1:512 * s1 + 512], T.pw1[:], ACT.Copy, bank_keys("pw1", range(8)),
-            ["win%da" % s1, "win%db" % s1])
+        act(T.win[:, 512 * s1:512 * s1 + 256], T.pw1[:, 0:256], ACT.Copy, bank_keys("pw1", range(4)), ["win%da" % s1])
         mask(2)
         mask(3)
         gather1(0, t)
         gather1(1, t)
+        cp(T.win[:, 512 * s1 + 256:512 * s1 + 512], T.pc1[:, 0:256], bank_keys("pc1", range(4, 8)), ["win%db" % s1])
+        if t > 0:
+            tt(T.da[:], T.da1[:], E1, ALU.min, ["da1", "pe1:e"], ["da"])
+            slot_max(T.da, "da", 5)
+        digits_c(0)
         gather1(2, t)
         if t == 0:
-            to_sbuf_c(0)
             op("v", lambda: v.tensor_copy(T.ob[:], T.win[:].indirect(T.so[:, 0:8])),
                ["win0a", "win0b", "win1a", "win1b", "so"], ["ob"])
             gather1(3, t)
-            act(T.own[:, 0:512], T.xw[:].indirect(T.ow[:, 0:32]), ACT.Copy, ["xw", "ow"], ["own0"])
-            act(T.own[:, 512:V], T.xw[:].indirect(T.ow[:, 32:64]), ACT.Copy, ["xw", "ow"], ["own1"])
-            to_sbuf_c(1)
             window_c(0)
-            offsets_c(0)
-            for c in range(4):
-                gather2(512 * c, 512 * c + 512, T.ob, "ob", T.dif0, T.ab0, "i")
-                absolute(512 * c, 512 * c + 512, T.dif0, T.ab0, "i")
-                sums(512 * c, 512 * c + 512, T.ab0, "i", False)
-                if c == 1:
-                    window_c(1)
-            offsets_c(1)
             checks(0)
-            gather2(0, 512, T.oc, "oc0", T.dif, T.ab, "r")
+            digits_c(1)
+            for lo, hi in OWN:
+                act(T.own[:, lo:hi], T.xw[:].indirect(T.ow[:, lo // 16:hi // 16]), ACT.Copy, ["xw", "ow"],
+                    ["own%d" % lo])
+            for c, (lo, hi) in enumerate(OWN + [(V, 1536), (1536, 2 * V)]):
+                gather2(lo, hi, T.ob, "ob", T.dif0, T.ab0, "i")
+                if c == 2:
+                    scalar_gather(0)
+                    tensor_subtract(0)
+                absolute(lo, hi, T.dif0, T.ab0, "i")
+                sums(lo, hi, T.ab0, "i", False)
+            window_c(1)
+            round_gather(1)
+            scalar_abs(0)
+            round_abs(1)
             ts(T.da[:, 0:64], T.pe0[:, 0:64], 0.5, ALU.add, ["pe0:e"], ["daa"])
             cp(T.da[:, 64:128], T.pe1[:, 0:64], ["pe1:e"], ["dab"])
             writer["da"] = writer["daa"] + writer["dab"]
-            checks(1)
-            absolute(0, 512, T.dif, T.ab, "r")
-            gather2(512, 1024, T.oc, "oc0", T.dif, T.ab, "r")
+            round_gather(2)
             slot_max(T.da, "da", 5)
-            absolute(512, 1024, T.dif, T.ab, "r")
             first_sum()
             open_sum("pe1")
-            gather2(*CH[2], T.oc, "oc1", T.dif, T.ab, "r")
-            absolute(*CH[2], T.dif, T.ab, "r")
+            round_abs(2)
             sums(*CH[2], T.ab, "r", True)
+            checks(1)
+            round_gather(3)
             first_step()
-            gather2(*CH[3], T.oc, "oc1", T.dif, T.ab, "r")
         else:
-            cp(T.oc[:, 0:64], T.pb0[:, 0:64], bank_keys("pb0", range(8)), ["oc0"])
-            to_sbuf_c(0)
-            act(T.dif[:, 0:512], T.xw[:].indirect(T.oc[:, 0:32]), ACT.Copy, ["xw", "oc0"], ["difr0"])
-            gather1(3, t)
-            mm(T.pw1[:], T.bi[:], T.dif[:, 0:512], ["bi", "difr0"], ["pw1:x"], True, False)
-            mm(T.pw1[:], T.nbi[:], T.own[:, 0:512], ["nbi", "own0"], ["pw1:x"], False, True)
+            scalar_gather(0)
             window_c(0)
-            to_sbuf_c(1)
-            gather2(*CH[1], T.oc, "oc0", T.dif, T.ab, "r")
-            offsets_c(1)
+            scalar_gather(1)
+            tensor_subtract(0)
+            gather1(3, t)
             checks(0)
-            op("a", lambda: a.activation(T.ab[:, 0:512], T.pw1[:], ACT.Abs, scale=1.0 / BIG), ["pw1:x"], ["abr0"])
-            absolute(*CH[1], T.dif, T.ab, "r")
+            tensor_subtract(1)
+            digits_c(1)
+            scalar_abs(0)
+            scalar_abs(1)
+            round_gather(2)
             window_c(1)
             first_sum()
             open_sum("pe1")
-            gather2(*CH[2], T.oc, "oc1", T.dif, T.ab, "r")
-            absolute(*CH[2], T.dif, T.ab, "r")
+            round_abs(2)
             sums(*CH[2], T.ab, "r", True)
-            gather2(*CH[3], T.oc, "oc1", T.dif, T.ab, "r")
+            round_gather(3)
             first_step()
             checks(1)
-        absolute(*CH[3], T.dif, T.ab, "r")
+        round_abs(3)
         sums(*CH[3], T.ab, "r", True)
         slot_max(T.da1, "da1", 6)
         tt(T0, T.dl0[:], H0, ALU.mult, ["dl0", "pe0:h"], ["pe0:t"])
-        gather2(*CH[4], T.oc, "oc1", T.dif, T.ab, "r")
-        absolute(*CH[4], T.dif, T.ab, "r")
         penal("pe1", 2)
         penal("pe1", 3)
         penal("pe1", 4)
         not_max("pe1", 6, False)
-        b = "pe1"
-        lo, hi = CH[4]
-        last = [(y, d) for y in range(lo // 128, hi // 128) for d in range(2)]
-        for y, d in last:
-            c = 64 * d + 8 * (y % 8)
-            mm(T[b][:, c:c + 8], T.ab[:, 128 * y:128 * y + 128], T.selb[:, 0:8], ["abr%d" % lo, "selb"],
-               [b + ":e"], False, (y, d) == last[-1])
+        round_gather(4)
+        round_abs(4)
+        sums(*CH[4], T.ab, "r", True, close=True)
         tt(T.dl2[:], T.dl1[:], T0, ALU.subtract, ["dl1", "pe0:t"], ["dl2"])
-        tt(T.u1[:], T.uf[:], T0, ALU.add, ["uf", "pe0:t"], ["u1"])
-        tt(H1, T.da1[:], E1, ALU.is_gt, ["da1", "pe1:e"], ["pe1:h"])
+        tt(T.u1[:], T.uf[:], T0, ALU.add, UF + ["pe0:t"], ["u1"])
+        for s in [s1, s0]:
+            h = slice(64 * s, 64 * s + 64)
+            tt(T.pe1[:, 128 + 64 * s:192 + 64 * s], T.da1[:, h], T.pe1[:, h], ALU.is_gt, ["da1", "pe1:e"],
+               ["pe1:h%d" % s])
         if t == RO - 1:
             tt(T.da[:], T.da1[:], E1, ALU.min, ["da1", "pe1:e"], ["da"])
-        tt(T1, T.dl2[:], H1, ALU.mult, ["dl2", "pe1:h"], ["pe1:t"])
+        for s in [s1, s0]:
+            h = slice(64 * s, 64 * s + 64)
+            tt(T.pe1[:, 256 + 64 * s:320 + 64 * s], T.dl2[:, h], T.pe1[:, 128 + 64 * s:192 + 64 * s], ALU.mult,
+               ["dl2", "pe1:h%d" % s], ["pe1:t%d" % s])
         if t == RO - 1:
             ts(T.da[:, 0:64], T.da[:, 0:64], -0.5, ALU.add, ["da"], ["da"])
-        tt(T.uf[:], T.u1[:], T1, ALU.add, ["u1", "pe1:t"], ["uf"])
+        outs = [(T.uf, "uf", s1), (T.ui, "ui", 0), (T.uf, "uf", s0), (T.ui, "ui", 1)]
+        for to, key, s in outs[::2] if t == RO - 1 else outs:
+            h = slice(64 * s, 64 * s + 64)
+            tt(to[:, h], T.u1[:, h], T.pe1[:, 256 + 64 * s:320 + 64 * s], ALU.add, ["u1", "pe1:t%d" % s],
+               ["%s%d" % (key, s)])
 
     dma("a", T.od2[:], T.da[:], "o2", ["da"], ["od2"])
-    dma("s", T.od1[:], T.uf[:], "o1", ["uf"], ["od1"])
+    dma("s", T.od1[:], T.uf[:], "o1", UF, ["od1"])
     dma("a", T.ol2[r], T.da[mine, :], "o4", ["da"], ["ol2own"])
-    dma("s", T.ol1[r], T.uf[mine, :], "o3", ["uf"], ["ol1own"])
+    dma("s", T.ol1[r], T.uf[mine, :], "o3", UF, ["ol1own"])
     need("g", ["od1", "od2"], [])
     back = []
     for k, s in enumerate(others):

@@ -4,36 +4,70 @@ from concourse.mybir import AluOpType as ALU, ActivationFunctionType as ACT
 N = 8
 V = 1024
 RO = 4
-BIG = 8192.0
-BANKS = ["pw0", "pw1", "pc0", "pc1", "pb0", "pb1", "pe0", "pe1"]
+BIG = float(1 << 24)
+DS = 4096.0
+HALF = 2048
+WB = ["w0", "w1", "w2", "w3"]
+BANKS = WB + ["pb0", "pb1", "pe0", "pe1"]
+HI0, HI1, LO1, LO0 = range(4)
+BLK = [(HI0, LO0), (HI1, LO1)]
+PART = [slice(0, 32), slice(32, 64)]
+SKIPS = [[0, 1], [2, 3, 4]]
+DUP = [False, False]
+SLOT = [slice(HI0, LO0 + 1, LO0 - HI0), slice(HI1, LO1 + 1)]
+GATE = 1
+CH = [(0, 512), (512, 1024), (1024, 1536), (1536, 1792), (1792, 2048)]
+
+FIRST = """stack0 stv0 lists stack1 stv1 offsets mask0 mask1 rep0 winv0 mask2 winv1 rep1 num1 wina2 num0 iopen wina3
+    bsum1 mask3 bsum0 num2 xy0 list0 zt difv0 num3 own1 now own0 open0 own2 ob check0 fa1 adddig0 if1 bsum3
+    bsum2 list1 xy1 presub0 ia1 presub1 if2 if3 if0 if4 skip0 fa0 ia2 check1 ia3 sub0 ia0 sub1 fv2 ia4 ca ka
+    difa1 fv4 max0 aa0 check2 skip1 fv3 open1 adddig1 aa1 sum0 notmax0 av2 sum1 skip2 check3 step0 check4 av4
+    max1 skip3 sum2 skip4 av3 sum4 notmax1 sum3 close0 close1 cut0 cut1 low0 digits0 digits1 low1"""
+LATER = """stack0 lists mask0 stack1 stv0 mask1 offsets rep0 stv1 rep1 winv0 wina2 winv1 presub0 wina3 num1 mask2 bsum1
+    mask3 num0 now presub1 open0 bsum0 num2 xy0 bsum2 list0 open1 difv0 num3 fa1 cv max0 adddig0 fa0 check0 sub1
+    bsum3 list1 xy1 aa1 check1 sub0 notmax0 fv3 skip0 skip1 difa1 aa0 av3 sum1 adddig1 fv2 sum0 check3 fv4 av2
+    check2 sum3 step0 skip3 check4 skip2 av4 sum2 skip4 sum4 max1 notmax1 close0 close1 cut0 cut1 low0 digits0
+    digits1 low1"""
 
 SCRATCH = {}
 for _names, _where, _shape, _dt in [
-        ("xs own repb", "sbuf", [128, V], "bfloat16"),
+        ("xs own", "sbuf", [128, V], "bfloat16"),
         ("xr xw", "sbuf", [128, N * V], "bfloat16"),
         ("nbd nbl", "dram", [N, 128, 16], "int32"),
-        ("od1 od2 ol1 ol2", "dram", [N, 128, 16], "float32"),
+        ("od ob2", "dram", [N, 128, 32], "float32"),
         ("pidx pbit", "sbuf", [128, 8], "int32"),
-        ("pflt pcol sel", "sbuf", [128, 8], "float32"),
-        ("j16 j128 uf u1 da da1 dl0 dl1 dl2", "sbuf", [128, 128], "float32"),
+        ("pf pc", "sbuf", [128, 16], "float32"),
+        ("j16 j8 un da", "sbuf", [128, 128], "float32"),
+        ("j144", "sbuf", [128, 144], "float32"),
         ("owi", "sbuf", [128, 64], "int32"),
-        ("sob", "sbuf", [128, 16], "float32"),
-        ("per bi nbi k0 ch cl", "sbuf", [128, 128], "bfloat16"),
-        ("selb", "sbuf", [128, 16], "bfloat16"),
-        ("repf win cw", "sbuf", [128, V], "float32"),
-        ("wa", "sbuf", [128, 64], "float32"),
+        ("zoi", "sbuf", [128, 16], "float32"),
+        ("sel1", "sbuf", [128, 32], "bfloat16"),
+        ("per up down one neg big m128 wx wy wz dlow dhigh swx swy pen", "sbuf", [128, 128], "bfloat16"),
+        ("rep xy zt", "sbuf", [128, 256], "bfloat16"),
+        ("rw", "sbuf", [128, N * 128], "bfloat16"),
+        ("sel8", "sbuf", [128, 8], "float32"),
+        ("rw0", "sbuf", [128, 128], "bfloat16"),
+        ("dg2", "sbuf", [128, 256], "bfloat16"),
+        ("lx ly", "sbuf", [128, 144], "bfloat16"),
+        ("selw", "sbuf", [128, 8], "bfloat16"),
+        ("sel4", "sbuf", [128, 4, 8], "bfloat16"),
+        ("k0", "sbuf", [128, (2 * RO + 1) * 4, 64], "bfloat16"),
+        ("ref", "sbuf", [128, 320], "float32"),
+        ("eq", "sbuf", [128, 320], "bfloat16"),
         ("ow", "sbuf", [128, 64], "uint16"),
-        ("so", "sbuf", [128, 16], "uint16"),
-        ("ol of oc ob", "sbuf", [128, 128], "uint16"),
-        ("ui lo32 of32", "sbuf", [128, 128], "int32"),
-        ("eq", "sbuf", [128, 448], "bfloat16"),
-        ("msk dif ab dif0 ab0", "sbuf", [128, 2048], "bfloat16"),
-        ("g1", "sbuf", [128, 2048], "float32"),
-        (" ".join(BANKS), "psum", [128, 512], "float32")]:
+        ("zo", "sbuf", [128, 16], "uint16"),
+        ("of oc ob", "sbuf", [128, 128], "uint16"),
+        ("ol", "sbuf", [128, 2, 64], "uint16"),
+        ("ui di", "sbuf", [128, 128], "int32"),
+        ("ka kb dgi", "sbuf", [128, 4, 64], "int32"),
+        ("dg", "sbuf", [128, 4, 64], "bfloat16"),
+        ("win msk g1 dif ab dif0 ab0", "sbuf", [128, 2048], "bfloat16"),
+        (" ".join(BANKS[:6]), "psum", [128, 512], "float32"),
+        ("pe0 pe1", "psum", [128, 8, 64], "float32")]:
     for _n in _names.split():
         SCRATCH[_n] = (_where, _shape, _dt)
 
-SEMAPHORES = ["cv", "ca", "cp", "cg", "xld", "xo", "nbs", "nbo", "nbarr", "nbsent", "nbld", "xarr", "xsent",
+SEMAPHORES = ["cv", "ca", "cp", "cg", "xld", "go", "nbs", "nbo", "nbarr", "nbsent", "nbld", "xarr", "xsent",
               "o1", "o2", "o3", "o4", "oarr", "osent", "y1", "y2"]
 
 
@@ -53,7 +87,7 @@ def x_calls(T, topo, r):
     while far or near:
         pair = ([far.pop(0)] if far else []) + ([near.pop(0)] if near else [])
         calls.append([(s, topo.engines(me, T.cores[s])[k::len(pair)]) for k, s in enumerate(pair)])
-    return calls
+    return sorted(calls, key=len)
 
 
 def rank_program(g, core, T, topo):
@@ -107,7 +141,11 @@ def rank_program(g, core, T, topo):
             if b in bank:
                 bank[b][e] = tok
 
+    def parts(keys):
+        return [k + h for k in keys for h in (("0", "1") if k in ("ka", "dg") else ("",))]
+
     def op(e, call, R, W):
+        R, W = parts(R), parts(W)
         need(e, R, W)
         count[e] += 1
         call().then_inc(S[own_sem[e]], 1)
@@ -135,8 +173,18 @@ def rank_program(g, core, T, topo):
     def act(out, in_, f, R, W):
         op("a", lambda: a.activation(out, in_, f), R, W)
 
+    def copy(e, out, in_, R, W):
+        if e == "v":
+            cp(out, in_, R, W)
+        else:
+            act(out, in_, ACT.Copy, R, W)
+
     def mm(out, lhsT, rhs, R, W, start=True, stop=True):
         op("p", lambda: p.matmul(out, lhsT, rhs, start, stop), R, W)
+
+    def group(out, terms, R, W):
+        for k, (lhsT, rhs) in enumerate(terms):
+            mm(out, lhsT, rhs, R, W, k == 0, k == len(terms) - 1)
 
     def dst(s):
         rid, pid, _ = topo.addr(T.cores[s])
@@ -146,68 +194,113 @@ def rank_program(g, core, T, topo):
     eng = topo.engines(core, T.cores[others[0]])
     mine = slice(16 * r, 16 * r + 16)
 
-    dma("a", T.nbd[:], T.nb[:], "nbs", [], ["nbd"])
+    dma("s", T.nbd[:], T.nb[:], "nbs", [], ["nbd"])
     dma("s", T.xs[:], T.x[:], "xld", [], ["xs"])
     dma("s", T.nbl[r], T.nb[mine, :], "nbo", [], ["nblown"])
 
-    def iota(out, pattern, cm, key, flt):
+    def iota(out, pattern, base, cm, key, flt=True):
         if flt:
-            op("g", lambda: g.iota(out, pattern, 0, cm, allow_small_or_imprecise_dtypes=True), [], [key])
+            op("g", lambda: g.iota(out, pattern, base, cm, allow_small_or_imprecise_dtypes=True), [], [key])
         else:
-            op("g", lambda: g.iota(out, pattern, 0, cm), [], [key])
+            op("g", lambda: g.iota(out, pattern, base, cm), [], [key])
 
-    iota(T.pidx[:], [[0, 8]], 1, "pidx", False)
-    iota(T.j16[:], [[0, 8], [1, 16]], 0, "j16", True)
-    iota(T.j128[:], [[1, 128]], 0, "j128", True)
-    iota(T.owi[:], [[128, 8], [1024, 8]], 1, "owi", False)
-    iota(T.sob[:, 0:8], [[512, 2], [16, 4]], 0, "sob0", True)
-    iota(T.sob[:, 8:16], [[0, 2], [16, 4]], 0, "sob1", True)
-    ts(T.pbit[:, 0:1], T.pidx[:, 0:1], 15, ALU.bitwise_and, ["pidx"], ["pb0_"])
-    ts(T.pbit[:, 1:2], T.pidx[:, 0:1], 4, ALU.logical_shift_right, ["pidx"], ["pb1_"])
-    ts(T.pbit[:, 2:3], T.pidx[:, 0:1], 7, ALU.bitwise_and, ["pidx"], ["pb2_"])
-    ts(T.pbit[:, 3:4], T.pidx[:, 0:1], 8, ALU.bitwise_and, ["pidx"], ["pb3_"])
-    cp(T.pflt[:, 0:4], T.pbit[:, 0:4], ["pb0_", "pb1_", "pb2_", "pb3_"], ["pflt"])
-    cp(T.pflt[:, 4:5], T.pidx[:, 0:1], ["pidx"], ["pf4"])
-    ts(T.per[:], T.j16[:], T.pflt[:, 0:1], ALU.is_equal, ["j16", "pflt"], ["per"])
-    ts(T.sel[:], T.j16[:, 0:8], T.pflt[:, 1:2], ALU.is_equal, ["j16", "pflt"], ["sel"])
-    xcalls = x_calls(T, topo, r)
-    for s in [s for c in xcalls for s, _ in c] + [r]:
-        ts(T.repb[:, 128 * s:128 * s + 128], T.per[:], T.sel[:, s:s + 1], ALU.mult, ["per", "sel"], ["repb%d" % s])
-    for s in range(N):
-        op("a", lambda: a.activation(T.repf[:, 128 * s:128 * s + 128], T.per[:], ACT.Identity,
-                                     scale=T.sel[:, s:s + 1]), ["per", "sel"], ["repf%d" % s])
-    cp(T.ow[:], T.owi[:], ["owi"], ["ow"])
-    cp(T.selb[:, 0:8], T.sel[:], ["sel"], ["selb"])
-    ts(T.pcol[:, 0:1], T.pflt[:, 2:3], 64.0, ALU.mult, ["pflt"], ["pc0_"], T.pflt[:, 3:4], ALU.add)
-    ts(T.pcol[:, 1:2], T.pflt[:, 1:2], 1024.0, ALU.mult, ["pflt"], ["pc1_"], T.pflt[:, 0:1], ALU.add)
-    ts(T.bi[:], T.j128[:], T.pflt[:, 4:5], ALU.is_equal, ["j128", "pf4"], ["bi"], BIG, ALU.mult)
-    ts(T.nbi[:], T.j128[:], T.pflt[:, 4:5], ALU.is_equal, ["j128", "pf4"], ["nbi"], -BIG, ALU.mult)
-    ts(T.so[:], T.sob[:], T.pcol[:, 0:1], ALU.add, ["sob0", "sob1", "pc0_", "pflt"], ["so"], T.pflt[:, 1:2], ALU.add)
-    ts(T.wa[:], T.j128[:, 0:64], 16.0, ALU.mult, ["j128", "pc1_"], ["wa"], T.pcol[:, 1:2], ALU.add)
-    op("v", lambda: v.memset(T.k0[:, 0:64], 0.5 / BIG), [], ["k0a"])
-    op("v", lambda: v.memset(T.k0[:, 64:128], 1.0), [], ["k0b"])
+    iota(T.pidx[:], [[0, 8]], 0, 1, "pidx", False)
+    iota(T.j16[:], [[0, 8], [1, 16]], 0, 0, "j16")
+    iota(T.j144[:], [[1, 144]], 0, 0, "j144")
+    FIELD = dict(p31=31, p8=8, p112=112, pno8=119, p7=7, p120=120, p14=14, p1=1)
+    col = {name: T.pf[:, k:k + 1] for k, name in enumerate(list(FIELD) + ["p"])}
+    for k, m in enumerate(FIELD.values()):
+        ts(T.pbit[:, k:k + 1], T.pidx[:, 0:1], m, ALU.bitwise_and, ["pidx"], ["pbit%d" % k])
+    cp(T.pf[:, 0:8], T.pbit[:], ["pbit%d" % k for k in range(8)], ["pf"])
+    cp(col["p"], T.pidx[:, 0:1], ["pidx"], ["p"])
+
+    def column(k, name, src, scale, bias, R=()):
+        col[name] = T.pc[:, k:k + 1]
+        op("a", lambda: a.activation(col[name], col[src], ACT.Identity, bias=bias, scale=scale),
+           ["pf", "p"] + list(R), [name])
+
+    def match(name, out, src, key, s1, o, at):
+        ts(out, src, s1, o, [key, "pf", "p", at], [name], col[at], ALU.is_equal)
+
+    def scaled(e, name, out, src, key, scale):
+        by = col.get(scale, scale)
+        if e == "v":
+            ts(out, src, by, ALU.mult, [key, str(scale)], [name])
+        else:
+            op("a", lambda: a.activation(out, src, ACT.Identity, scale=by), [key, str(scale)], [name])
+
+    j128 = T.j144[:, 0:128]
+    for k in range(2):
+        match("rep%d" % k, T.rep[:, 128 * k:128 * k + 128], T.j16[:], "j16", 16.0 * k, ALU.add, "p31")
+    column(0, "low", "p8", -0.125, 1.0)
+    column(1, "high", "p8", 0.125, 0.0)
+    column(2, "wlow", "low", 127.0, 1.0, ["low"])
+    column(3, "whigh", "high", 127.0, 1.0, ["high"])
+    column(4, "aty", "p8", -1.0, col["p112"])
+    column(5, "z1", "p14", 64.0, col["p1"])
+    column(6, "z2", "p112", 0.125, col["z1"], ["z1"])
+    column(7, "self", "p112", 63.0, col["p"])
+    match("down", T.down[:], j128, "j144", 0.0, ALU.add, "pno8")
+    match("up", T.up[:], j128, "j144", -8.0, ALU.add, "pno8")
+    match("one", T.one[:], j128, "j144", 0.0, ALU.add, "p")
+    match("rw", T.rw0[:], T.j16[:], "j16", col["p112"], ALU.add, "p")
+    match("sel8", T.sel8[:], T.j16[:, 0:8], "j16", 16.0, ALU.mult, "p112")
+
+    def constants_late():
+        for name, src, scale in [("dlow", "down", "low"), ("swy", "up", "low"), ("swx", "down", "high"),
+                                 ("dhigh", "up", "high"), ("m128", "one", -128.0), ("neg", "one", -1.0)]:
+            scaled("a", name, T[name][:], T[src][:], src, scale)
+        for u in range(N):
+            col["g%d" % u] = T.sel8[:, u:u + 1]
+            writer["g%d" % u] = writer["sel8"]
+            scaled("va"[u // 6], "rw%d" % u, T.rw[:, 128 * u:128 * u + 128], T.rw0[:], "rw", "g%d" % u)
+        match("per", T.per[:], T.j8[:], "j8", 0.0, ALU.add, "p7")
+        scaled("v", "selw", T.selw[:], T.sel8[:], "sel8", "wlow")
+        match("sel1", T.sel1[:], T.j8[:, 0:32], "j8", 16.0, ALU.mult, "p112")
+        match("lx", T.lx[:], T.j144[:], "j144", -7.0, ALU.add, "p120")
+        match("ly", T.ly[:], T.j144[:], "j144", -15.0, ALU.add, "aty")
+        for name, src, scale in [("wx", "down", "wlow"), ("wz", "up", "wlow"), ("wy", "up", "whigh"),
+                                 ("big", "one", BIG)]:
+            scaled("a", name, T[name][:], T[src][:], src, scale)
+        scaled("v", "sel4", T.sel4[:], T.sel1[:], "sel1", DS)
+        for k in (1, 4):
+            ts(T.ref[:, 64 * k:64 * k + 64], T.j144[:, 0:64], 16.0, ALU.mult, ["j144", "self"], ["ref"],
+               col["self"], ALU.add)
+        cp(T.ow[:], T.owi[:], ["owi"], ["ow"])
+        ts(T.zo[:], T.zoi[:], col["z2"], ALU.add, ["zoi", "z2"], ["zo"])
+        op("v", lambda: v.memset(T.k0[:, SLOT[0], :], float(HALF)), [], ["k0a0"])
+        op("v", lambda: v.memset(T.k0[:, SLOT[1], :], 0.0), [], ["k0b0"])
+        ts(T.k0[:, 4:8, :], T.k0[:, 0:4, :], 128.0, ALU.add, ["k0a0", "k0b0"], ["k0a1", "k0b1"])
 
     need("g", ["nbd"], [])
-    g.remote_dma_fused([RemoteDMATransfer(dst_ids=[dst(s)], dma_engine_mask=bits(eng[2 * k:2 * k + 2]),
+    g.remote_dma_fused([RemoteDMATransfer(dst_ids=[dst(s)], dma_engine_mask=bits(eng[2 * k:2 * k + 1]),
                                           remote_sem=S.nbarr, src=T.nbd[s], dst=T.nbl[r])
                         for k, s in enumerate(others)], local_sem=S.nbsent)
-    writer["nbl"] = [("nbarr", 2 * (N - 1))]
-    dma("s", T.ui[:], T.nbl[:], "nbld", ["nbl", "nblown"], ["ui0", "ui1"])
-    for b in range(N):
-        g.sync.dma_start(T.xw[16 * b:16 * b + 16, V * r:V * r + V], T.x[mine, :]).then_inc(S.xo, 16)
+    writer["nbl"] = [("nbarr", N - 1)]
+    dma("s", T.ui[:], T.nbl[:], "nbld", ["nbl", "nblown"], ["ui"])
+    g.sync.sem_inc(S.go, 1)
 
-    rot = [("pw0", "pw1"), ("pc0", "pc1")]
+    xcalls = x_calls(T, topo, r)
     sent = 0
-    nx = 0
-    for call in xcalls:
-        for s, _ in call:
-            b0, b1 = rot[nx % 2]
-            nx += 1
-            lhs = T.repb[:, 128 * s:128 * s + 128]
-            mm(T[b0][:], lhs, T.xs[:, 0:512], ["repb%d" % s, "xs"], [b0])
-            mm(T[b1][:], lhs, T.xs[:, 512:V], ["repb%d" % s, "xs"], [b1])
-            cp(T.xr[:, V * s:V * s + 512], T[b0][:], [b0], ["xr%da" % s])
-            act(T.xr[:, V * s + 512:V * s + V], T[b1][:], ACT.Copy, [b1], ["xr%db" % s])
+
+    def spread(k, s):
+        to = T.xw if s == r else T.xr
+        b0, b1 = WB[2 * (k % 2)], WB[2 * (k % 2) + 1]
+        rows = slice(32 * (s // 2), 32 * (s // 2) + 32)
+        lhs = T.rep[rows, 128 * (s % 2):128 * (s % 2) + 128]
+        mm(T[b0][:], lhs, T.xs[rows, 0:512], ["rep%d" % (s % 2), "xs"], [b0 + ":"])
+        mm(T[b1][:], lhs, T.xs[rows, 512:V], ["rep%d" % (s % 2), "xs"], [b1 + ":"])
+        cp(to[:, V * s:V * s + 512], T[b0][:], [b0 + ":"], ["xr%da" % s])
+        act(to[:, V * s + 512:V * s + V], T[b1][:], ACT.Copy, [b1 + ":"], ["xr%db" % s])
+
+    for k, s in enumerate([s for call in xcalls for s, _ in call] + [r]):
+        spread(k, s)
+    for k, call in enumerate(xcalls):
+        if k == GATE:
+            iota(T.j8[:], [[0, 16], [1, 8]], 0, 0, "j8")
+            iota(T.owi[:], [[128, 8], [1024, 8]], 0, 1, "owi", False)
+            iota(T.zoi[:], [[1024, 2], [16, 8]], 0, 0, "zoi")
+            wait("g", ("go", 1))
         need("g", [k % s for s, _ in call for k in ("xr%da", "xr%db")], [])
         if len(call) == 1:
             s, e = call[0]
@@ -219,38 +312,149 @@ def rank_program(g, core, T, topo):
                                 for s, e in call], local_sem=S.xsent)
         sent += sum(len(e) for _, e in call)
     arrive = sum(len(e) for q in others for c in x_calls(T, topo, q) for s, e in c if s == r)
-    writer["xw"] = [("xarr", arrive), ("xo", 16 * N)]
+    writer["xw"] = [("xarr", arrive)] + writer["xr%da" % r] + writer["xr%db" % r]
 
-    def repeat(banks, src, key):
-        per_bank = N // len(banks)
+    for f in range(2, 2 * RO + 1):
+        iota(T.k0[:, 4 * f:4 * f + 2, :], [[-HALF, 2], [0, 64]], HALF + 128 * f, 0, "k0a%d" % f)
+        iota(T.k0[:, 4 * f + 2:4 * f + 4, :], [[HALF, 2], [0, 64]], 128 * f, 0, "k0b%d" % f)
+    constants_late()
+
+    def lists():
+        for s in range(2):
+            group(T.pb1[:, 128 + 64 * s:192 + 64 * s],
+                  [(T.m128[:], T.dg[:, BLK[s][0], :]), (T.neg[:], T.dg[:, BLK[s][1], :])],
+                  ["dg", "m128", "neg"], ["pb1:n"])
+
+    def offsets():
+        ts(T.of[:], T.pb1[:, 128:256], -0.125, ALU.mult, ["pb1:n"], ["of"], -0.4375, ALU.add)
+
+    def repeat(s, first):
         for k in range(N):
-            b = banks[k // per_bank]
-            c = 64 * (k % per_bank)
-            mm(T[b][:, c:c + 64], T.repf[:, 128 * k:128 * k + 128], src, [key, "repf%d" % k], [b + ":%d" % k])
+            b = WB[2 * (0 if first else 1) + k // 4]
+            c = 128 * (k % 4)
+            mm(T[b][:, c:c + 128], T.rw[:, 128 * k:128 * k + 128], T.dg2[:, 128 * s:128 * s + 128],
+               ["dg2%d" % s, "rw%d" % k], [b + ":"])
 
-    def bank_keys(b, ks):
-        return [b + ":%d" % k for k in ks]
+    def stack(s, first):
+        b = "pb0" if first else "pe0"
+        for h, (hi, lo) in enumerate([(T.dlow, T.swy), (T.swx, T.dhigh)]):
+            out = T.pb0[:, 256 + h:384:2] if first else T.pb1[:, 256 + h:384:2]
+            group(out, [(hi[:], T.dg[:, BLK[s][0], :]), (lo[:], T.dg[:, BLK[s][1], :])],
+                  ["dg%d" % s, "dlow", "swy", "swx", "dhigh"], ["pb%d:s" % (0 if first else 1)])
+
+    def stacked(e, s, first):
+        b = "pb0" if first else "pb1"
+        copy(e, T.dg2[:, 128 * s:128 * s + 128], T[b][:, 256:384], [b + ":s"], ["dg2%d" % s])
+
+    def window(e, s, first, half):
+        b = WB[2 * (0 if first else 1) + half]
+        c = V * s + 512 * half
+        copy(e, T.win[:, c:c + 512], T[b][:], [b + ":"], ["win%d%d" % (s, half)])
 
     def mask(c):
-        act(T.msk[:, 512 * c:512 * c + 512], T.per[:, 0:16].indirect(T.ol[:, 32 * c:32 * c + 32]), ACT.Copy,
-            ["per", "ol%d" % (c // 2)], ["msk%d" % c])
+        act(T.msk[:, 512 * c:512 * c + 512], T.per[:].indirect(T.ol[:, 1 - c // 2, PART[c % 2]]), ACT.Copy,
+            ["per", "low%d" % (c // 2)], ["msk%d" % c])
 
-    def gather1(c, t):
+    def close(s):
+        tt(T.ka[:, SLOT[s], :], T.kb[:, SLOT[s], :], T.pe1[:, SLOT[s], :], ALU.min, ["kb", "pe1:"], ["ka%d" % s])
+
+    def cut(s):
+        ts(T.dgi[:, SLOT[s], :], T.ka[:, SLOT[s], :], 127, ALU.bitwise_and, ["ka%d" % s], ["dgi%d" % s])
+
+    def digits(s):
+        cp(T.dg[:, SLOT[s], :], T.dgi[:, SLOT[s], :], ["dgi%d" % s], ["dg%d" % s])
+
+    def low(s):
+        cp(T.ol[:, 1 - s, :], T.dgi[:, BLK[s][1], :], ["dgi%d" % s], ["low%d" % s])
+
+    def numbers(c, t):
         s = (c // 2 + t) % 2
         cols = slice(512 * c, 512 * c + 512)
-        tt(T.g1[:, cols], T.win[:, 512 * s:512 * s + 512].indirect(T.of[:, 32 * c:32 * c + 32]), T.msk[:, cols],
-           ALU.mult, ["win%da" % s, "win%db" % s, "of", "msk%d" % c], ["g1%d" % c])
+        tt(T.g1[:, cols], T.win[:, V * s:V * s + V].indirect(T.of[:, 32 * c:32 * c + 32]), T.msk[:, cols],
+           ALU.mult, ["win%d0" % s, "win%d1" % s, "of", "msk%d" % c], ["g1%d" % c])
+
+    def number_sums(c):
         b = "pb%d" % (c // 2)
         for y in range(4 * c, 4 * c + 4):
-            mm(T[b][:, 8 * (y % 8):8 * (y % 8) + 8], T.g1[:, 128 * y:128 * y + 128], T.sel[:],
-               ["g1%d" % c, "sel"], [b + ":%d" % (y % 8)])
+            mm(T[b][:, 8 * (y % 8):8 * (y % 8) + 8], T.g1[:, 128 * y:128 * y + 128], T.selw[:],
+               ["g1%d" % c, "selw"], [b + ":c"])
+
+    def cand_list(i):
+        cp(T.oc[:, 64 * i:64 * i + 64], T["pb%d" % i][:, 0:64], ["pb%d:c" % i], ["oc%d" % i])
+
+    XY, SUB = ["w0", "w1"], ["w2", "w3", "w2"]
+
+    def cand_digits(i):
+        for h, (m, key) in enumerate([(T.lx, "lx"), (T.ly, "ly")]):
+            group(T[XY[i]][:, 64 * h:64 * h + 64],
+                  [(m[:, 7 - q:135 - q], T.g1[:, V * i + 8 * h + q:V * i + V:16]) for q in range(8)],
+                  [key, "g1%d" % (2 * i), "g1%d" % (2 * i + 1)], [XY[i] + ":"])
+
+    def X(i):
+        return T.xy[:, 128 * i:128 * i + 64]
+
+    def Y(i):
+        return T.xy[:, 128 * i + 64:128 * i + 128]
+
+    def differences(e, i):
+        copy(e, T.xy[:, 128 * i:128 * i + 128], T[XY[i]][:, 0:128], [XY[i] + ":"], ["xy%d" % i])
+        for k in range(len(SKIPS[i]) if DUP[i] else 1):
+            group(T[XY[i]][:, 128 + 64 * k:192 + 64 * k], [(T.wx[:], X(i)), (T.wy[:], Y(i))],
+                  ["xy%d" % i, "wx", "wy"], [XY[i] + ":"])
+
+    def numbers_now():
+        op("a", lambda: a.activation(T.ref[:, 128:256], T.pb1[:, 128:256], ACT.Copy, scale=-1.0), ["pb1:n"], ["now"])
+
+    def first_candidate(e):
+        copy(e, T.ref[:, 0:64], T[XY[0]][:, 128:192], [XY[0] + ":"], ["c0"])
+
+    def eq(k):
+        return T.eq[:, 64 * k:64 * k + 64]
+
+    def check(k):
+        i = min(k // 2, 1)
+        if not DUP[i]:
+            c = 64 * (3, 4, 0, 1, 2)[k]
+            tt(eq(k), T[XY[i]][:, 128:192], T.ref[:, c:c + 64], ALU.is_equal,
+               [XY[i] + ":", ("now", "ref", "c0", "ref", "now")[k]], ["eq%d" % k])
+            return
+        n = 64 * len(SKIPS[i])
+        tt(T.eq[:, 128 * i:128 * i + n], T[XY[i]][:, 128:128 + n], T.ref[:, 192 * (1 - i):192 * (1 - i) + n],
+           ALU.is_equal, [XY[i] + ":", "ref", "now"] + ["c0"] * i, ["eq%d" % j for j in SKIPS[i]])
+
+    def slot_max(src, key):
+        tt(T.pen[:], src[:, LO1:LO0 + 1, :], src[:, HI0:HI1 + 1, :], ALU.is_gt, [key], ["pen"])
+
+    def add(b, blk, lhsT, rhs, R, stop=False):
+        mm(T[b][:, blk, :], lhsT, rhs, R, [b + ":"], False, stop)
+
+    def open_sum(b, f):
+        mm(T[b][:, 0:4, :], T.one[:], T.k0[:, 4 * f:4 * f + 4, :], ["one", "k0a%d" % f, "k0b%d" % f], [b + ":"],
+           True, False)
+
+    def add_digits(i, stop=False):
+        b = "pe%d" % i
+        for s in range(2):
+            add(b, BLK[s][0], T.dlow[:], X(i), ["xy%d" % i, "dlow"])
+            add(b, BLK[s][0], T.dhigh[:], Y(i), ["xy%d" % i, "dhigh"])
+            add(b, BLK[s][1], T.swx[:], X(i), ["xy%d" % i, "swx"])
+            add(b, BLK[s][1], T.swy[:], Y(i), ["xy%d" % i, "swy"], stop and s == 1)
+
+    def add_skips(k, stop=False):
+        for blk in range(4):
+            add("pe%d" % min(k // 2, 1), blk, T.big[:], eq(k), ["big", "eq%d" % k], stop and blk == 3)
+
+    def add_not_max(i, stop=False):
+        todo = [(s, blk) for s in range(2) for blk in BLK[s]]
+        for s, blk in todo:
+            add("pe%d" % i, blk, T.big[:], T.pen[:, 64 * s:64 * s + 64], ["big", "pen"], stop and (s, blk) == todo[-1])
 
     OWN = [(0, 256), (256, 512), (512, V)]
 
     def own_keys(lo, hi):
         return ["own%d" % x for x, y in OWN if x < hi and lo < y]
 
-    def gather2(lo, hi, off, okey, dif, ab, tag):
+    def features(lo, hi, off, okey, dif, tag):
         o = lo % V
         tt(dif[:, lo:hi], T.xw[:].indirect(off[:, lo // 16:hi // 16]), T.own[:, o:o + hi - lo], ALU.subtract,
            ["xw", okey] + own_keys(o, o + hi - lo), ["dif%s%d" % (tag, lo)])
@@ -258,223 +462,127 @@ def rank_program(g, core, T, topo):
     def absolute(lo, hi, dif, ab, tag):
         act(ab[:, lo:hi], dif[:, lo:hi], ACT.Abs, ["dif%s%d" % (tag, lo)], ["ab%s%d" % (tag, lo)])
 
-    def sums(lo, hi, ab, tag, twice, close=False):
-        b = "pe%d" % (lo // V)
-        todo = [(y, d) for y in range(lo // 128, hi // 128) for d in range(2 if twice else 1)]
-        for y, d in todo:
-            c = 64 * d + 8 * (y % 8)
-            mm(T[b][:, c:c + 8], ab[:, 128 * y:128 * y + 128], T.selb[:, 0:8], ["ab%s%d" % (tag, lo), "selb"],
-               [b + ":e"], not twice, not twice or (close and (y, d) == todo[-1]))
+    def sums(b, blks, lo, hi, ab, tag, stop=False):
+        n = len(range(4)[blks])
+        for y in range(lo // 128, hi // 128):
+            mm(T[b][:, blks, 8 * (y % 8):8 * (y % 8) + 8], ab[:, 128 * y:128 * y + 128], T.sel4[:, 0:n, :],
+               ["ab%s%d" % (tag, lo), "sel4"], [b + ":"], False, stop and y == hi // 128 - 1)
 
-    def digits_c(i):
-        h = slice(64 * i, 64 * i + 64)
-        src, ks = T["pb%d" % i][:, 0:64], bank_keys("pb%d" % i, range(8))
-        cp(T.ch[:, h], src, ks, ["ch%d" % i])
-        cp(T.oc[:, h], src, ks, ["oc%d" % i])
-        tt(T.cl[:, h], src, T.ch[:, h], ALU.subtract, ks + ["ch%d" % i], ["cl%d" % i])
-        for k in range(N):
-            out, lhs = T["pc%d" % i][:, 64 * k:64 * k + 64], T.repb[:, 128 * k:128 * k + 128]
-            mm(out, lhs, T.ch[:, h], ["ch%d" % i, "repb%d" % k], ["pc%d:%d" % (i, k)], True, False)
-            mm(out, lhs, T.cl[:, h], ["cl%d" % i, "repb%d" % k], ["pc%d:%d" % (i, k)], False, True)
-
-    def window_c(i):
-        act(T.cw[:, 512 * i:512 * i + 512], T["pc%d" % i][:], ACT.Copy, bank_keys("pc%d" % i, range(8)), ["cw%d" % i])
-
-    def eqc(k):
-        return T.eq[:, 64 * k:64 * k + 64]
-
-    def penal(b, k):
-        for d in range(2):
-            mm(T[b][:, 64 * d:64 * d + 64], T.bi[:], eqc(k), ["bi", "eq%d" % k], [b + ":e"], False, False)
-
-    def not_max(b, k, stop):
-        mm(T[b][:, 0:64], T.bi[:], eqc(k), ["bi", "eq%d" % k], [b + ":e"], False, False)
-        mm(T[b][:, 64:128], T.nbi[:], eqc(k), ["nbi", "eq%d" % k], [b + ":e"], False, stop)
-
-    def open_sum(b):
-        mm(T[b][:, 0:128], T.bi[:], T.k0[:], ["bi", "k0a", "k0b"], [b + ":e"], True, False)
-
-    UF = ["uf0", "uf1"]
-
-    def checks(i):
-        dl = T.dl0 if i == 0 else T.dl1
-        w = T.cw[:, 512 * i:512 * i + 512]
-        tt(dl[:], w.indirect(T.so[:, 8:16]), T.uf[:], ALU.subtract, ["cw%d" % i, "so"] + UF, ["dl%d" % i])
-        tt(eqc(2 * i), w.indirect(T.so[:, 0:4]), T.wa[:], ALU.is_equal, ["cw%d" % i, "so", "wa"], ["eq%d" % (2 * i)])
-        half = dl[:, 64:128] if i == 0 else dl[:, 0:64]
-        ts(eqc(2 * i + 1), half, 0.0, ALU.is_equal, ["dl%d" % i], ["eq%d" % (2 * i + 1)])
-        if i == 1:
-            tt(eqc(4), T.dl1[:, 0:64], T.dl0[:, 0:64], ALU.is_equal, ["dl0", "dl1"], ["eq4"])
-
-    def slot_max(src, key, k):
-        tt(eqc(k), src[:, 64:128], src[:, 0:64], ALU.is_gt, [key], ["eq%d" % k])
-
-    E0, E1 = T.pe0[:, 0:128], T.pe1[:, 0:128]
-    H0, T0 = T.pe0[:, 128:256], T.pe0[:, 256:384]
-    CH = [(0, 512), (512, 1024), (1024, 1536), (1536, 1920), (1920, 2048)]
-
-    def first_sum():
-        open_sum("pe0")
-        penal("pe0", 0)
-        penal("pe0", 1)
-        sums(0, 512, T.ab, "r", True)
-        sums(512, 1024, T.ab, "r", True)
-        not_max("pe0", 5, True)
-
-    def first_step():
-        tt(T.da1[:], T.da[:], E0, ALU.min, ["da", "pe0:e"], ["da1"])
-        tt(H0, T.da[:], E0, ALU.is_gt, ["da", "pe0:e"], ["pe0:h"])
-
-    SUB = ["pw1", "pw0"]
-
-    def scalar_gather(k):
+    def scalar_features(k):
         lo, hi = CH[k]
-        act(T.dif[:, lo:hi], T.xw[:].indirect(T.oc[:, lo // 16:hi // 16]), ACT.Copy, ["xw", "oc0"], ["difr%d" % lo])
+        act(T.dif[:, lo:hi], T.xw[:].indirect(T.oc[:, lo // 16:hi // 16]), ACT.Copy, ["xw", "oc%d" % (lo // V)],
+            ["difr%d" % lo])
 
-    def tensor_subtract(k):
+    def subtract(k):
         lo, hi = CH[k]
-        mm(T[SUB[k]][:], T.bi[:], T.dif[:, lo:hi], ["bi", "difr%d" % lo], [SUB[k] + ":x"], True, False)
-        mm(T[SUB[k]][:], T.nbi[:], T.own[:, lo:hi], ["nbi"] + own_keys(lo, hi), [SUB[k] + ":x"], False, True)
+        mm(T[SUB[k]][:, 0:hi - lo], T.one[:], T.dif[:, lo:hi], ["one", "difr%d" % lo], [SUB[k] + ":"], False, True)
+
+    def before_subtract(k):
+        lo, hi = CH[k]
+        o = lo % V
+        mm(T[SUB[k]][:, 0:hi - lo], T.neg[:], T.own[:, o:o + hi - lo], ["neg"] + own_keys(o, o + hi - lo),
+           [SUB[k] + ":"], True, False)
 
     def scalar_abs(k):
         lo, hi = CH[k]
-        op("a", lambda: a.activation(T.ab[:, lo:hi], T[SUB[k]][:], ACT.Abs, scale=1.0 / BIG), [SUB[k] + ":x"],
-           ["abr%d" % lo])
+        act(T.ab[:, lo:hi], T[SUB[k]][:, 0:hi - lo], ACT.Abs, [SUB[k] + ":"], ["abr%d" % lo])
 
-    def lists():
-        ts(T.lo32[:, 0:64], T.ui[:, 0:64], 15, ALU.bitwise_and, ["ui0"], ["lo32a"])
-        ts(T.of32[:], T.ui[:], 4, ALU.logical_shift_right, ["ui0", "ui1"], ["of32"])
-        cp(T.ol[:, 0:64], T.lo32[:, 0:64], ["lo32a"], ["ol0"])
-        ts(T.lo32[:, 64:128], T.ui[:, 64:128], 15, ALU.bitwise_and, ["ui1"], ["lo32b"])
-        cp(T.of[:], T.of32[:], ["of32"], ["of"])
-        cp(T.ol[:, 64:128], T.lo32[:, 64:128], ["lo32b"], ["ol1"])
-
-    def round_gather(k):
-        gather2(*CH[k], T.oc, "oc%d" % (CH[k][0] // V), T.dif, T.ab, "r")
+    def round_features(k):
+        features(*CH[k], T.oc, "oc%d" % (CH[k][0] // V), T.dif, "r")
 
     def round_abs(k):
         absolute(*CH[k], T.dif, T.ab, "r")
 
-    cp(T.uf[:], T.ui[:], ["ui0"], UF)
+    def round_sums(k, stop=False):
+        sums("pe%d" % (CH[k][0] // V), slice(0, 4), *CH[k], T.ab, "r", stop)
+
+    def start_lists():
+        op("v", lambda: v.tensor_copy(T.zt[:], T.win[:].indirect(T.zo[:])),
+           ["win00", "win01", "win10", "win11", "zo"], ["zt"])
+        group(T.pb0[:, 128:256], [(T.wx[:], T.zt[:, 0:256:2]), (T.wz[:], T.zt[:, 1:256:2])],
+              ["zt", "wx", "wz"], ["pb0:z"])
+
+    def own_features(k):
+        lo, hi = OWN[k]
+        act(T.own[:, lo:hi], T.xw[:].indirect(T.ow[:, lo // 16:hi // 16]), ACT.Copy, ["xw", "ow"], ["own%d" % lo])
+
+    def start_open():
+        open_sum("pe1", 0)
+        mm(T.pe1[:, 0:4, :], T.one[:], T.dg[:], ["one", "dg"], ["pe1:"], False, False)
+
+    START = OWN + [(V, 1536), (1536, 2 * V)]
+
+    def start_features(k):
+        features(*START[k], T.ob, "ob", T.dif0, "i")
+
+    def start_abs(k):
+        lo, hi = START[k]
+        absolute(lo, hi, T.dif0, T.ab0, "i")
+        sums("pe1", slice(0, 4, 3) if lo < V else slice(1, 3), lo, hi, T.ab0, "i", hi == 2 * V)
+
+    def step(to, tkey, src, skey, b):
+        tt(to[:], src[:], T[b][:, 0:4, :], ALU.min, [skey, b + ":"], [tkey])
+
+    ts(T.dgi[:, HI0:HI1 + 1, :], T.ui[:], 7, ALU.logical_shift_right, ["ui"], ["high digits"])
+    for s in range(2):
+        ts(T.dgi[:, BLK[s][1], :], T.ui[:, 64 * s:64 * s + 64], 127, ALU.bitwise_and, ["ui"], ["dgi%d" % s])
+    for call, s in [(digits, 0), (low, 0), (digits, 1), (low, 1)]:
+        call(s)
     for t in range(RO):
         s0, s1 = t % 2, (t + 1) % 2
-        repeat(["pw0", "pc0"], T.uf[:, 64 * s0:64 * s0 + 64], "uf%d" % s0)
-        repeat(["pw1", "pc1"], T.uf[:, 64 * s1:64 * s1 + 64], "uf%d" % s1)
-        lists()
-        cp(T.win[:, 512 * s0:512 * s0 + 256], T.pw0[:, 0:256], bank_keys("pw0", range(4)), ["win%da" % s0])
-        cp(T.win[:, 512 * s0 + 256:512 * s0 + 512], T.pc0[:, 0:256], bank_keys("pc0", range(4, 8)), ["win%db" % s0])
-        mask(0)
-        mask(1)
-        act(T.win[:, 512 * s1:512 * s1 + 256], T.pw1[:, 0:256], ACT.Copy, bank_keys("pw1", range(4)), ["win%da" % s1])
-        mask(2)
-        mask(3)
-        gather1(0, t)
-        gather1(1, t)
-        cp(T.win[:, 512 * s1 + 256:512 * s1 + 512], T.pc1[:, 0:256], bank_keys("pc1", range(4, 8)), ["win%db" % s1])
-        if t > 0:
-            tt(T.da[:], T.da1[:], E1, ALU.min, ["da1", "pe1:e"], ["da"])
-            slot_max(T.da, "da", 5)
-        digits_c(0)
-        gather1(2, t)
-        if t == 0:
-            op("v", lambda: v.tensor_copy(T.ob[:], T.win[:].indirect(T.so[:, 0:8])),
-               ["win0a", "win0b", "win1a", "win1b", "so"], ["ob"])
-            gather1(3, t)
-            window_c(0)
-            checks(0)
-            digits_c(1)
-            for lo, hi in OWN:
-                act(T.own[:, lo:hi], T.xw[:].indirect(T.ow[:, lo // 16:hi // 16]), ACT.Copy, ["xw", "ow"],
-                    ["own%d" % lo])
-            for c, (lo, hi) in enumerate(OWN + [(V, 1536), (1536, 2 * V)]):
-                gather2(lo, hi, T.ob, "ob", T.dif0, T.ab0, "i")
-                if c == 2:
-                    scalar_gather(0)
-                    tensor_subtract(0)
-                absolute(lo, hi, T.dif0, T.ab0, "i")
-                sums(lo, hi, T.ab0, "i", False)
-            window_c(1)
-            round_gather(1)
-            scalar_abs(0)
-            round_abs(1)
-            ts(T.da[:, 0:64], T.pe0[:, 0:64], 0.5, ALU.add, ["pe0:e"], ["daa"])
-            cp(T.da[:, 64:128], T.pe1[:, 0:64], ["pe1:e"], ["dab"])
-            writer["da"] = writer["daa"] + writer["dab"]
-            round_gather(2)
-            slot_max(T.da, "da", 5)
-            first_sum()
-            open_sum("pe1")
-            round_abs(2)
-            sums(*CH[2], T.ab, "r", True)
-            checks(1)
-            round_gather(3)
-            first_step()
-        else:
-            scalar_gather(0)
-            window_c(0)
-            scalar_gather(1)
-            tensor_subtract(0)
-            gather1(3, t)
-            checks(0)
-            tensor_subtract(1)
-            digits_c(1)
-            scalar_abs(0)
-            scalar_abs(1)
-            round_gather(2)
-            window_c(1)
-            first_sum()
-            open_sum("pe1")
-            round_abs(2)
-            sums(*CH[2], T.ab, "r", True)
-            round_gather(3)
-            first_step()
-            checks(1)
-        round_abs(3)
-        sums(*CH[3], T.ab, "r", True)
-        slot_max(T.da1, "da1", 6)
-        tt(T0, T.dl0[:], H0, ALU.mult, ["dl0", "pe0:h"], ["pe0:t"])
-        penal("pe1", 2)
-        penal("pe1", 3)
-        penal("pe1", 4)
-        not_max("pe1", 6, False)
-        round_gather(4)
-        round_abs(4)
-        sums(*CH[4], T.ab, "r", True, close=True)
-        tt(T.dl2[:], T.dl1[:], T0, ALU.subtract, ["dl1", "pe0:t"], ["dl2"])
-        tt(T.u1[:], T.uf[:], T0, ALU.add, UF + ["pe0:t"], ["u1"])
-        for s in [s1, s0]:
-            h = slice(64 * s, 64 * s + 64)
-            tt(T.pe1[:, 128 + 64 * s:192 + 64 * s], T.da1[:, h], T.pe1[:, h], ALU.is_gt, ["da1", "pe1:e"],
-               ["pe1:h%d" % s])
-        if t == RO - 1:
-            tt(T.da[:], T.da1[:], E1, ALU.min, ["da1", "pe1:e"], ["da"])
-        for s in [s1, s0]:
-            h = slice(64 * s, 64 * s + 64)
-            tt(T.pe1[:, 256 + 64 * s:320 + 64 * s], T.dl2[:, h], T.pe1[:, 128 + 64 * s:192 + 64 * s], ALU.mult,
-               ["dl2", "pe1:h%d" % s], ["pe1:t%d" % s])
-        if t == RO - 1:
-            ts(T.da[:, 0:64], T.da[:, 0:64], -0.5, ALU.add, ["da"], ["da"])
-        outs = [(T.uf, "uf", s1), (T.ui, "ui", 0), (T.uf, "uf", s0), (T.ui, "ui", 1)]
-        for to, key, s in outs[::2] if t == RO - 1 else outs:
-            h = slice(64 * s, 64 * s + 64)
-            tt(to[:, h], T.u1[:, h], T.pe1[:, 256 + 64 * s:320 + 64 * s], ALU.add, ["u1", "pe1:t%d" % s],
-               ["%s%d" % (key, s)])
+        piece = {
+            "close": close, "cut": cut, "digits": lambda k: digits((s1, s0)[k]), "low": low,
+            "lists": lists, "offsets": offsets,
+            "rep": lambda k: repeat((s0, s1)[k], k == 0),
+            "stack": lambda k: stack((s0, s1)[k], k == 0),
+            "stv": lambda k: stacked("v", (s0, s1)[k], k == 0), "sta": lambda k: stacked("a", (s0, s1)[k], k == 0),
+            "winv": lambda k: window("v", (s0, s1)[k // 2], k < 2, k % 2),
+            "wina": lambda k: window("a", (s0, s1)[k // 2], k < 2, k % 2),
+            "mask": mask, "num": lambda c: numbers(c, t), "bsum": number_sums, "list": cand_list,
+            "xy": cand_digits, "difv": lambda i: differences("v", i), "difa": lambda i: differences("a", i),
+            "check": check, "presub": before_subtract, "now": numbers_now,
+            "cv": lambda: first_candidate("v"), "ca": lambda: first_candidate("a"),
+            "open": lambda i: open_sum("pe%d" % i, 2 * t + 1 + i),
+            "max": lambda i: slot_max(*[(T.ka, "ka"), (T.kb, "kb")][i]),
+            "notmax": add_not_max, "adddig": add_digits, "skip": add_skips, "sum": round_sums,
+            "fa": scalar_features, "sub": subtract, "aa": scalar_abs, "fv": round_features, "av": round_abs,
+            "step": lambda i: step(T.kb, "kb", T.ka, "ka", "pe0"),
+            "zt": start_lists, "ob": lambda: cp(T.ob[:], T.pb0[:, 128:256], ["pb0:z"], ["ob"]),
+            "own": own_features, "iopen": start_open, "if": start_features, "ia": start_abs,
+            "ka": lambda: cp(T.ka[:], T.pe1[:, 0:4, :], ["pe1:"], ["ka"])}
+        order = [n for n in (FIRST if t == 0 else LATER).split() if t < RO - 1 or n[:-1] not in ("low", "digits")]
+        last = {}
+        for name in order:
+            if name[:-1] in ("notmax", "adddig", "skip", "sum"):
+                k = int(name[-1])
+                last[{"sum": CH[k][0] // V, "skip": min(k // 2, 1)}.get(name[:-1], k)] = name
+        for name in order:
+            if name in last.values():
+                piece[name[:-1]](int(name[-1]), True)
+            elif name[-1].isdigit():
+                piece[name[:-1]](int(name[-1]))
+            else:
+                piece[name]()
 
-    dma("a", T.od2[:], T.da[:], "o2", ["da"], ["od2"])
-    dma("s", T.od1[:], T.uf[:], "o1", UF, ["od1"])
-    dma("a", T.ol2[r], T.da[mine, :], "o4", ["da"], ["ol2own"])
-    dma("s", T.ol1[r], T.uf[mine, :], "o3", UF, ["ol1own"])
+    ts(T.di[:], T.ka[:, HI0:HI1 + 1, :], 12, ALU.logical_shift_right, ["ka"], ["di"])
+    ts(T.pb1[:, 128:256], T.dgi[:, HI0:HI1 + 1, :], 128.0, ALU.mult, ["dgi0", "dgi1"], ["pb1:n"])
+    cp(T.da[:], T.di[:], ["di"], ["da"])
+    for s in range(2):
+        tt(T.un[:, 64 * s:64 * s + 64], T.pb1[:, 128 + 64 * s:192 + 64 * s], T.dgi[:, BLK[s][1], :], ALU.add,
+           ["pb1:n", "dgi%d" % s], ["un%d" % s])
+    writer["un"] = writer["un1"]
+
+    dma("s", T.od[:, 0:64, :], T.un[:], "o1", ["un"], ["od1"])
+    dma("a", T.od[:, 64:128, :], T.da[:], "o2", ["da"], ["od2"])
+    dma("s", T.ob2[r, 0:64, :], T.un[mine, :], "o3", ["un"], ["ol1own"])
+    dma("a", T.ob2[r, 64:128, :], T.da[mine, :], "o4", ["da"], ["ol2own"])
     need("g", ["od1", "od2"], [])
-    back = []
-    for k, s in enumerate(others):
-        back.append(RemoteDMATransfer(dst_ids=[dst(s)], dma_engine_mask=bits(eng[2 * k:2 * k + 1]),
-                                      remote_sem=S.oarr, src=T.od1[s], dst=T.ol1[r]))
-        back.append(RemoteDMATransfer(dst_ids=[dst(s)], dma_engine_mask=bits(eng[2 * k + 1:2 * k + 2]),
-                                      remote_sem=S.oarr, src=T.od2[s], dst=T.ol2[r]))
-    g.remote_dma_fused(back, local_sem=S.osent)
+    g.remote_dma_fused([RemoteDMATransfer(dst_ids=[dst(s)], dma_engine_mask=bits(eng[2 * k:2 * k + 2]),
+                                          remote_sem=S.oarr, src=T.od[s], dst=T.ob2[r])
+                        for k, s in enumerate(others)], local_sem=S.osent)
     writer["ol"] = [("oarr", 2 * (N - 1))]
-    dma("s", T.ynb[:], T.ol1[:], "y1", ["ol", "ol1own"], ["y1"])
-    dma("a", T.yd[:], T.ol2[:], "y2", ["ol", "ol2own"], ["y2"])
-    for tok in [("nbsent", 2 * (N - 1)), ("xsent", sent), ("osent", 2 * (N - 1)), ("cv", count["v"]),
+    dma("s", T.ynb[:], T.ob2[:, 0:64, :], "y1", ["ol", "ol1own"], ["y1"])
+    dma("a", T.yd[:], T.ob2[:, 64:128, :], "y2", ["ol", "ol2own"], ["y2"])
+    for tok in [("nbsent", N - 1), ("xsent", sent), ("osent", 2 * (N - 1)), ("cv", count["v"]),
                 ("ca", count["a"]), ("cp", count["p"]), ("cg", count["g"]), ("y1", 16), ("y2", 16)]:
         wait("g", tok)

@@ -7,27 +7,41 @@ RO = 4
 BIG = float(1 << 24)
 DS = 4096.0
 HALF = 2048
-WB = ["w0", "w1", "w2", "w3"]
+WB = ["w0", "pe2", "w2", "w3"]
 BANKS = WB + ["pb0", "pb1", "pe0", "pe1"]
-HI0, HI1, LO1, LO0 = range(4)
+HI0, HI1, LO0, LO1 = range(4)
 BLK = [(HI0, LO0), (HI1, LO1)]
 PART = [slice(0, 32), slice(32, 64)]
-SKIPS = [[0, 1], [2, 3, 4]]
-DUP = [False, False]
-SLOT = [slice(HI0, LO0 + 1, LO0 - HI0), slice(HI1, LO1 + 1)]
+ROWS = [slice(0, 64), slice(64, 128)]
+SLOT = [slice(0, 4, 2), slice(1, 4, 2)]
+HI, LO = slice(0, 2), slice(2, 4)
 GATE = 1
+SHARED = 8
+MERGE = False
 CH = [(0, 512), (512, 1024), (1024, 1536), (1536, 1792), (1792, 2048)]
+OWN = [(0, 256), (256, 512), (512, V)]
+START = OWN + [(V, 1536), (1536, 2 * V)]
+XY, SUB = WB[:2], [WB[2], WB[3], WB[2]]
 
-FIRST = """stack0 stv0 lists stack1 stv1 offsets mask0 mask1 rep0 winv0 mask2 winv1 rep1 num1 wina2 num0 iopen wina3
-    bsum1 mask3 bsum0 num2 xy0 list0 zt difv0 num3 own1 now own0 open0 own2 ob check0 fa1 adddig0 if1 bsum3
-    bsum2 list1 xy1 presub0 ia1 presub1 if2 if3 if0 if4 skip0 fa0 ia2 check1 ia3 sub0 ia0 sub1 fv2 ia4 ca ka
-    difa1 fv4 max0 aa0 check2 skip1 fv3 open1 adddig1 aa1 sum0 notmax0 av2 sum1 skip2 check3 step0 check4 av4
-    max1 skip3 sum2 skip4 av3 sum4 notmax1 sum3 close0 close1 cut0 cut1 low0 digits0 digits1 low1"""
-LATER = """stack0 lists mask0 stack1 stv0 mask1 offsets rep0 stv1 rep1 winv0 wina2 winv1 presub0 wina3 num1 mask2 bsum1
-    mask3 num0 now presub1 open0 bsum0 num2 xy0 bsum2 list0 open1 difv0 num3 fa1 cv max0 adddig0 fa0 check0 sub1
-    bsum3 list1 xy1 aa1 check1 sub0 notmax0 fv3 skip0 skip1 difa1 aa0 av3 sum1 adddig1 fv2 sum0 check3 fv4 av2
-    check2 sum3 step0 skip3 check4 skip2 av4 sum2 skip4 sum4 max1 notmax1 close0 close1 cut0 cut1 low0 digits0
-    digits1 low1"""
+TAIL = " +close0 +close1 +cut0 +cut1 +low0 +digits0 +low1 +digits1"
+FIRST = """const0 const1 const2 const3 const5 const6 const7 const4 entry first0 firstlow first1 lists rep00 rep01 mask0 offsets
+    mask1 winv00 mask2 winv01 rep10 rep11 num1 wina10 num0 iopen wina11 bsum1 mask3 bsum0 num2 xy0 list0x zt difv0 num3 own1
+    nowa own0 open0 own2 ob check0 fa1 adddig0 if1 bsum3 bsum2 list1x xy1 presub0 ia1 isum1 presub1 if2 if3 if0 if4 skip0 fa0
+    ia2 isum2 check1 ia3 isum3 sub0 ia0 isum0 sub1 fv2 ia4 isum4 ca ka difa1 fv4 top0 aa0 check2 skip1 fv3 open1 adddig1 aa1
+    sum0 below0 again av2 sum1 skip2 check3 top1 step0 check4 av4 skip3 sum2 skip4 av3 sum4 below1 sum3""" + TAIL
+HEAD = """top0 mask1 mask0 rep00 rep01 winv00 wina01 lists mask2 offsets rep10 rep11 winv10 open1 num0 open0 below0
+    again num1 presub0 bsum0 list00 wina11 presub1 num2 mask3 bsum1 list01 xy0 bsum2 fa0 sub0 difa0 num3 xy1 nowv list10 fa1 aa0
+    check1 sub1 fv2 bsum3 adddig0 skip1 difa1 adddig1 aa1 check0 sum0 skip0 list11 cv fv4 sum1 check3 skip3 check4 fv3 av2
+    skip4 sum2 check2 av4 skip2 top1 sum4 av3 below1 step0 sum3"""
+LATER = HEAD + TAIL
+LAST = HEAD + " +close0 +close1 out0 +cut0 +cut1 out1 out2 out3"
+FIRST = "const0 const2 const8 const6 const5 const1 const3 const7 const4 entry0 entry1 first1 firstlow0 firstlow1 first0 rep10 mask1 winv10 lists offsets rep00 rep01 wina00 winv01 num1 mask0 num0 rep11 wina11 bsum0 zt mask2 num2 mask3 own0 xy0 ob num3 bsum1 list0x bsum2 own1 bsum3 own2 if1 iopen if0 if2 presub0 xy1 open0 if3 ir2 nowa ia1 fa0 difa0 adddig0 sub0 if4 isum2 fa1 ia3 ia0 presub1 sub1 isum3 isum0 check0 check1 list1x ir4 skip1 fv2 isum4 isum1 ka difa1 check4 check3 skip0 aa0 sum0 ca open1 adddig1 top0 fv3 below0 aa1 sum1 skip3 skip4 fv4 av2 again av3 sum2 sum3 check2 skip2 top1 below1 step0 av4 sum4 +close1 +close0 +cut1 +cut0 +low0 +digits0 +digits1 +low1"
+LAST = "open1 top0 rep00 mask0 winv00 mask1 rep01 wina01 rep10 winv10 lists again rep11 wina11 offsets num0 num1 open0 below0 mask2 presub0 bsum0 mask3 list00 bsum1 num2 list01 xy0 presub1 bsum2 fa0 sub0 difa0 num3 list10 xy1 fa1 sub1 check1 nowv fv2 bsum3 aa0 list11 adddig0 difa1 check0 adddig1 sum0 skip1 cv aa1 av2 fv4 sum1 av4 skip0 check3 skip3 check4 skip4 sum2 fv3 av3 check2 skip2 top1 sum4 step0 below1 sum3 +close1 +close0 +cut1 +cut0 out0 out1 out2 out3"
+FIRST = "consta8 const6 const2 const3 entry0 consta7 entry1 consta0 firstlow0 first1 rep10 first0 rep00 const4 consta5 firstlow1 consta1 lists winv10 mask1 offsets wina00 rep01 winv01 num1 mask0 num0 rep11 wina11 iopen xy0 zt mask2 num2 nowa ob bsum1 mask3 num3 own0 if0 open0 bsum0 list0x difa0 check0 adddig0 own1 if3 skip0 own2 fa1 presub1 bsum3 if2 fa0 if1 bsum2 presub0 if4 ia3 list1x xy1 ia0 sub1 isum0 ir2 check1 ir4 ia1 sub0 isum1 isum3 isum2 isum4 fv2 skip1 aa1 sum1 ka fv3 aa0 sum0 difa1 check4 open1 top0 ca adddig1 skip4 check3 below0 again fv4 check2 skip3 av2 sum2 av3 sum3 top1 skip2 below1 step0 av4 sum4 +close1 +close0 +cut1 +cut0 +low0 +digits0 +low1 +digits1"
+LATER = "open0 mask0 open1 rep01 wina01 rep00 mask1 top0 winv00 lists offsets rep10 winv10 rep11 presub0 num0 bsum0 mask2 below0 num1 list00 wina11 presub1 bsum1 mask3 xy0 num2 again bsum2 fa0 sub0 difa0 list01 fa1 num3 list10 xy1 nowv fv2 bsum3 list11 aa0 check1 sub1 aa1 adddig0 cv skip1 difv1 sum0 check0 adddig1 sum1 av2 fv4 av4 check2 check3 skip2 check4 skip0 skip3 fv3 sum2 skip4 top1 av3 sum4 below1 step0 sum3 +close0 +close1 +cut0 +low0 +cut1 +digits0 +low1 +digits1"
+EVEN = "mask1 top0 rep00 lists0 rep01 winv00 rep10 mask0 lists1 wina01 open0 winv10 rep11 offsets0 presub0 offsets1 num0 num1 wina11 presub1 bsum0 list00 mask2 num2 open1 again mask3 fa0 bsum1 list01 xy0 num3 below0 bsum2 sub0 list10 difa0 adddig0 nowv xy1 fv2 fa1 sub1 bsum3 aa0 sum0 check0 skip0 difa1 cv adddig1 check1 list11 fv4 skip1 check3 check4 aa1 sum1 skip3 skip4 fv3 av2 check2 top1 sum2 av4 skip2 sum4 av3 step0 below1 sum3 +close1 +close0 +cut1 +cut0 +low0 +digits0 +digits1 +low1"
+LAST = "rep01 rep00 lists top0 winv00 rep10 mask0 rep11 offsets open1 again winv10 wina01 num0 presub0 mask1 open0 wina11 below0 bsum0 num1 list00 xy0 bsum1 presub1 mask2 num2 bsum2 difv0 adddig0 list01 mask3 num3 fa0 fa1 nowv list10 sub0 aa0 check0 xy1 fv2 sub1 bsum3 list11 skip0 check1 sum0 difa1 cv fv3 aa1 check4 check3 skip1 av2 check2 fv4 adddig1 sum1 skip4 av3 skip3 sum2 skip2 av4 top1 step0 sum3 below1 sum4 +close0 +close1 +cut0 +cut1 out0 out1 out2 out3"
+TRACE, CUR = [], [None]
 
 SCRATCH = {}
 for _names, _where, _shape, _dt in [
@@ -35,35 +49,35 @@ for _names, _where, _shape, _dt in [
         ("xr xw", "sbuf", [128, N * V], "bfloat16"),
         ("nbd nbl", "dram", [N, 128, 16], "int32"),
         ("od ob2", "dram", [N, 128, 32], "float32"),
-        ("pidx pbit", "sbuf", [128, 8], "int32"),
+        ("pidx", "sbuf", [128, 8], "int32"),
+        ("pbit", "sbuf", [128, 16], "int32"),
         ("pf pc", "sbuf", [128, 16], "float32"),
-        ("j16 j8 un da", "sbuf", [128, 128], "float32"),
-        ("j144", "sbuf", [128, 144], "float32"),
+        ("un da", "sbuf", [128, 2, 64], "float32"),
+        ("lx ly", "sbuf", [128, 144], "bfloat16"),
+        ("j192", "sbuf", [128, 192], "bfloat16"),
+        ("down up", "sbuf", [128, 128], "bfloat16"),
+        ("sel", "sbuf", [128, 32], "bfloat16"),
         ("owi", "sbuf", [128, 64], "int32"),
         ("zoi", "sbuf", [128, 16], "float32"),
-        ("sel1", "sbuf", [128, 32], "bfloat16"),
-        ("per up down one neg big m128 wx wy wz dlow dhigh swx swy pen", "sbuf", [128, 128], "bfloat16"),
+        ("j16 j8 per one neg big nbig ones wx wy wz dlow dhigh swx swy", "sbuf", [128, 128], "bfloat16"),
+        ("pen", "sbuf", [128, 3, 64], "bfloat16"),
         ("rep xy zt", "sbuf", [128, 256], "bfloat16"),
         ("rw", "sbuf", [128, N * 128], "bfloat16"),
-        ("sel8", "sbuf", [128, 8], "float32"),
-        ("rw0", "sbuf", [128, 128], "bfloat16"),
-        ("dg2", "sbuf", [128, 256], "bfloat16"),
-        ("lx ly", "sbuf", [128, 144], "bfloat16"),
+        ("fold", "sbuf", [128, 4, 192], "bfloat16"),
         ("selw", "sbuf", [128, 8], "bfloat16"),
-        ("sel4", "sbuf", [128, 4, 8], "bfloat16"),
+        ("sel4 seld selr", "sbuf", [128, 4, 8], "bfloat16"),
         ("k0", "sbuf", [128, (2 * RO + 1) * 4, 64], "bfloat16"),
-        ("ref", "sbuf", [128, 320], "float32"),
-        ("eq", "sbuf", [128, 320], "bfloat16"),
+        ("ref", "sbuf", [128, 4, 64], "float32"),
+        ("eq", "sbuf", [128, 5, 64], "bfloat16"),
         ("ow", "sbuf", [128, 64], "uint16"),
         ("zo", "sbuf", [128, 16], "uint16"),
-        ("of oc ob", "sbuf", [128, 128], "uint16"),
-        ("ol", "sbuf", [128, 2, 64], "uint16"),
-        ("ui di", "sbuf", [128, 128], "int32"),
-        ("ka kb dgi", "sbuf", [128, 4, 64], "int32"),
-        ("dg", "sbuf", [128, 4, 64], "bfloat16"),
+        ("oc ob", "sbuf", [128, 128], "uint16"),
+        ("of ol", "sbuf", [128, 2, 64], "uint16"),
+        ("ui di", "sbuf", [128, 2, 64], "int32"),
+        ("ka kb dgi dgs", "sbuf", [128, 4, 64], "int32"),
+        ("dg dd", "sbuf", [128, 4, 64], "bfloat16"),
         ("win msk g1 dif ab dif0 ab0", "sbuf", [128, 2048], "bfloat16"),
-        (" ".join(BANKS[:6]), "psum", [128, 512], "float32"),
-        ("pe0 pe1", "psum", [128, 8, 64], "float32")]:
+        (" ".join(BANKS), "psum", [128, 8, 64], "float32")]:
     for _n in _names.split():
         SCRATCH[_n] = (_where, _shape, _dt)
 
@@ -76,6 +90,10 @@ def bits(engines):
     for e in engines:
         m |= 1 << e
     return m
+
+
+def place(rank):
+    return N // 2 * (rank % 2) + rank // 2
 
 
 def x_calls(T, topo, r):
@@ -112,21 +130,19 @@ def rank_program(g, core, T, topo):
         toks = {}
 
         def add(t):
-            if e == "p" and t[0] == "cp":
-                return
             toks[t[0]] = max(toks.get(t[0], 0), t[1])
         for k in R:
             for t in writer.get(k, []):
-                add(t)
+                if e != "p" or t[0] != "cp":
+                    add(t)
         for k in W:
             for t in writer.get(k, []) + readers.get(k, []):
-                add(t)
+                if t[0] != own_sem.get(e):
+                    add(t)
         for k in list(R) + list(W):
-            b = k.split(":")[0]
-            if b in bank:
-                for e2, t in bank[b].items():
-                    if e2 != e:
-                        add(t)
+            for e2, t in bank.get(k.split(":")[0], {}).items():
+                if e2 != e:
+                    add(t)
         for s, n in toks.items():
             wait(e, (s, n))
 
@@ -141,11 +157,8 @@ def rank_program(g, core, T, topo):
             if b in bank:
                 bank[b][e] = tok
 
-    def parts(keys):
-        return [k + h for k in keys for h in (("0", "1") if k in ("ka", "dg") else ("",))]
-
     def op(e, call, R, W):
-        R, W = parts(R), parts(W)
+        TRACE.append((CUR[0], R, W))
         need(e, R, W)
         count[e] += 1
         call().then_inc(S[own_sem[e]], 1)
@@ -169,6 +182,9 @@ def rank_program(g, core, T, topo):
 
     def cp(out, in_, R, W):
         op("v", lambda: v.tensor_copy(out, in_), R, W)
+
+    def fill(out, c, W):
+        op("v", lambda: v.memset(out, c), [], W)
 
     def act(out, in_, f, R, W):
         op("a", lambda: a.activation(out, in_, f), R, W)
@@ -196,7 +212,7 @@ def rank_program(g, core, T, topo):
 
     dma("s", T.nbd[:], T.nb[:], "nbs", [], ["nbd"])
     dma("s", T.xs[:], T.x[:], "xld", [], ["xs"])
-    dma("s", T.nbl[r], T.nb[mine, :], "nbo", [], ["nblown"])
+    dma("s", T.nbl[place(r)], T.nb[mine, :], "nbo", [], ["nblown"])
 
     def iota(out, pattern, base, cm, key, flt=True):
         if flt:
@@ -206,75 +222,75 @@ def rank_program(g, core, T, topo):
 
     iota(T.pidx[:], [[0, 8]], 0, 1, "pidx", False)
     iota(T.j16[:], [[0, 8], [1, 16]], 0, 0, "j16")
-    iota(T.j144[:], [[1, 144]], 0, 0, "j144")
-    FIELD = dict(p31=31, p8=8, p112=112, pno8=119, p7=7, p120=120, p14=14, p1=1)
-    col = {name: T.pf[:, k:k + 1] for k, name in enumerate(list(FIELD) + ["p"])}
-    for k, m in enumerate(FIELD.values()):
-        ts(T.pbit[:, k:k + 1], T.pidx[:, 0:1], m, ALU.bitwise_and, ["pidx"], ["pbit%d" % k])
-    cp(T.pf[:, 0:8], T.pbit[:], ["pbit%d" % k for k in range(8)], ["pf"])
-    cp(col["p"], T.pidx[:, 0:1], ["pidx"], ["p"])
-
-    def column(k, name, src, scale, bias, R=()):
+    iota(T.j192[:], [[1, 192]], 0, 0, "j192")
+    iota(T.j8[:], [[0, 16], [1, 8]], 0, 0, "j8")
+    FIELD = dict(p=(0, 127), p31=(0, 31), high=(3, 1), upper=(6, 1), grp=(4, 7), pno8=(0, 119), p7=(0, 7), p120=(0, 120),
+                 p6=(0, 6), p1=(0, 1), p48=(0, 48), p63=(0, 63), p56=(0, 56), p112=(0, 112))
+    col = {name: T.pf[:, k:k + 1] for k, name in enumerate(FIELD)}
+    for k, (sh, m) in enumerate(FIELD.values()):
+        ts(T.pbit[:, k:k + 1], T.pidx[:, 0:1], sh, ALU.logical_shift_right, ["pidx"], ["pbit"], m, ALU.bitwise_and)
+    cp(T.pf[:, 0:len(FIELD)], T.pbit[:, 0:len(FIELD)], ["pbit"], list(FIELD))
+    for k, (name, scale, src, bias) in enumerate([
+            ("dq", 8.0, "upper", "p7"), ("wlow", -127.0, "high", 128.0), ("wjoin", 127.0, "upper", -128.0),
+            ("lower", -1.0, "upper", 1.0), ("za", 128.0, "p6", "p1"), ("zb", 64.0, "high", "grp"),
+            ("self0", 127.0, "p48", "p63"),
+            ("rwat", 2.0, "p56", "dq"), ("low", -1.0, "high", 1.0), ("whigh", 127.0, "high", 1.0),
+            ("aty", -8.0, "high", "p112"), ("z", 2.0, "zb", "za"), ("self", float(V), "upper", "self0")]):
         col[name] = T.pc[:, k:k + 1]
-        op("a", lambda: a.activation(col[name], col[src], ACT.Identity, bias=bias, scale=scale),
-           ["pf", "p"] + list(R), [name])
+        op("a", lambda: a.activation(col[name], col[src], ACT.Identity, bias=col.get(bias, bias), scale=scale),
+           [src, str(bias)], [name])
 
-    def match(name, out, src, key, s1, o, at):
-        ts(out, src, s1, o, [key, "pf", "p", at], [name], col[at], ALU.is_equal)
+    def shifted(name, out, src, key, shift, at):
+        ts(out, src, float(shift), ALU.add, [key, at], [name], col[at], ALU.is_equal)
 
-    def scaled(e, name, out, src, key, scale):
-        by = col.get(scale, scale)
-        if e == "v":
-            ts(out, src, by, ALU.mult, [key, str(scale)], [name])
+    def scaled(name, out, src, key, w, bias=0.0):
+        if by[0] == "v":
+            ts(out, src, col.get(w, w), ALU.mult, [key, str(w), str(bias)], [name], col.get(bias, bias), ALU.add)
         else:
-            op("a", lambda: a.activation(out, src, ACT.Identity, scale=by), [key, str(scale)], [name])
+            op("a", lambda: a.activation(out, src, ACT.Identity, bias=col.get(bias, bias), scale=col.get(w, w)),
+               [key, str(w), str(bias)], [name])
 
-    j128 = T.j144[:, 0:128]
+    by = ["v"]
+
+    def constants(e, k):
+        by[0] = e
+        CONST[k]()
+
     for k in range(2):
-        match("rep%d" % k, T.rep[:, 128 * k:128 * k + 128], T.j16[:], "j16", 16.0 * k, ALU.add, "p31")
-    column(0, "low", "p8", -0.125, 1.0)
-    column(1, "high", "p8", 0.125, 0.0)
-    column(2, "wlow", "low", 127.0, 1.0, ["low"])
-    column(3, "whigh", "high", 127.0, 1.0, ["high"])
-    column(4, "aty", "p8", -1.0, col["p112"])
-    column(5, "z1", "p14", 64.0, col["p1"])
-    column(6, "z2", "p112", 0.125, col["z1"], ["z1"])
-    column(7, "self", "p112", 63.0, col["p"])
-    match("down", T.down[:], j128, "j144", 0.0, ALU.add, "pno8")
-    match("up", T.up[:], j128, "j144", -8.0, ALU.add, "pno8")
-    match("one", T.one[:], j128, "j144", 0.0, ALU.add, "p")
-    match("rw", T.rw0[:], T.j16[:], "j16", col["p112"], ALU.add, "p")
-    match("sel8", T.sel8[:], T.j16[:, 0:8], "j16", 16.0, ALU.mult, "p112")
+        shifted("rep%d" % k, T.rep[:, 128 * k:128 * k + 128], T.j16[:], "j16", 16 * k, "p31")
+    shifted("one", T.one[:], T.j192[:, 0:128], "j192", 0, "p")
+    shifted("down", T.down[:], T.j192[:, 0:128], "j192", 0, "pno8")
+    shifted("up", T.up[:], T.j192[:, 0:128], "j192", -8, "pno8")
+    shifted("fold", T.fold[:, 3, :], T.j192[:], "j192", -64, "p63")
+    shifted("lx", T.lx[:], T.j192[:, 0:144], "j192", -7, "p120")
+    shifted("sel", T.sel[:], T.j8[:, 0:32], "j8", 0, "grp")
+    shifted("per", T.per[:], T.j8[:], "j8", 0, "p7")
 
-    def constants_late():
-        for name, src, scale in [("dlow", "down", "low"), ("swy", "up", "low"), ("swx", "down", "high"),
-                                 ("dhigh", "up", "high"), ("m128", "one", -128.0), ("neg", "one", -1.0)]:
-            scaled("a", name, T[name][:], T[src][:], src, scale)
-        for u in range(N):
-            col["g%d" % u] = T.sel8[:, u:u + 1]
-            writer["g%d" % u] = writer["sel8"]
-            scaled("va"[u // 6], "rw%d" % u, T.rw[:, 128 * u:128 * u + 128], T.rw0[:], "rw", "g%d" % u)
-        match("per", T.per[:], T.j8[:], "j8", 0.0, ALU.add, "p7")
-        scaled("v", "selw", T.selw[:], T.sel8[:], "sel8", "wlow")
-        match("sel1", T.sel1[:], T.j8[:, 0:32], "j8", 16.0, ALU.mult, "p112")
-        match("lx", T.lx[:], T.j144[:], "j144", -7.0, ALU.add, "p120")
-        match("ly", T.ly[:], T.j144[:], "j144", -15.0, ALU.add, "aty")
-        for name, src, scale in [("wx", "down", "wlow"), ("wz", "up", "wlow"), ("wy", "up", "whigh"),
-                                 ("big", "one", BIG)]:
-            scaled("a", name, T[name][:], T[src][:], src, scale)
-        scaled("v", "sel4", T.sel4[:], T.sel1[:], "sel1", DS)
-        for k in (1, 4):
-            ts(T.ref[:, 64 * k:64 * k + 64], T.j144[:, 0:64], 16.0, ALU.mult, ["j144", "self"], ["ref"],
-               col["self"], ALU.add)
+    def late(*rows):
+        for name, src, w in rows:
+            if src == "fold":
+                scaled(name, T.fold[:, int(name[-1]), :], T.fold[:, 3, :], src, w)
+            else:
+                scaled(name, T[name][:], T[src][:, 0:8] if name == "selw" else T[src][:], src, w)
+
+    def fixed_lists():
+        ts(T.zo[:], T.zoi[:], col["z"], ALU.add, ["zoi", "z"], ["zo"])
         cp(T.ow[:], T.owi[:], ["owi"], ["ow"])
-        ts(T.zo[:], T.zoi[:], col["z2"], ALU.add, ["zoi", "z2"], ["zo"])
-        op("v", lambda: v.memset(T.k0[:, SLOT[0], :], float(HALF)), [], ["k0a0"])
-        op("v", lambda: v.memset(T.k0[:, SLOT[1], :], 0.0), [], ["k0b0"])
-        ts(T.k0[:, 4:8, :], T.k0[:, 0:4, :], 128.0, ALU.add, ["k0a0", "k0b0"], ["k0a1", "k0b1"])
+
+    def fills():
+        scaled("ref", T.ref[:, 1, :], T.j192[:, 0:64], "j192", 16.0, "self")
+        scaled("ones", T.ones[:], T.one[:], "one", 0.0, 1.0)
+
+    CONST = [lambda: late(("fold0", "fold", "wjoin")), lambda: late(("fold1", "fold", "lower"), ("fold2", "fold", "upper")),
+             lambda: late(("selw", "sel", "wlow"), ("wx", "down", "wlow"), ("wz", "up", "wlow"), ("wy", "up", "whigh")),
+             lambda: late(("sel4", "sel", DS), ("seld", "sel", -DS), ("selr", "sel", 2 * DS)), fixed_lists, fills,
+             lambda: late(("neg", "one", -1.0), ("big", "one", BIG), ("nbig", "one", -BIG)),
+             lambda: late(("dlow", "down", "low"), ("swx", "down", "high"), ("swy", "up", "low"), ("dhigh", "up", "high")),
+             lambda: shifted("ly", T.ly[:], T.j192[:, 0:144], "j192", -15, "aty")]
 
     need("g", ["nbd"], [])
     g.remote_dma_fused([RemoteDMATransfer(dst_ids=[dst(s)], dma_engine_mask=bits(eng[2 * k:2 * k + 1]),
-                                          remote_sem=S.nbarr, src=T.nbd[s], dst=T.nbl[r])
+                                          remote_sem=S.nbarr, src=T.nbd[s], dst=T.nbl[place(r)])
                         for k, s in enumerate(others)], local_sem=S.nbsent)
     writer["nbl"] = [("nbarr", N - 1)]
     dma("s", T.ui[:], T.nbl[:], "nbld", ["nbl", "nblown"], ["ui"])
@@ -290,15 +306,15 @@ def rank_program(g, core, T, topo):
         lhs = T.rep[rows, 128 * (s % 2):128 * (s % 2) + 128]
         mm(T[b0][:], lhs, T.xs[rows, 0:512], ["rep%d" % (s % 2), "xs"], [b0 + ":"])
         mm(T[b1][:], lhs, T.xs[rows, 512:V], ["rep%d" % (s % 2), "xs"], [b1 + ":"])
-        cp(to[:, V * s:V * s + 512], T[b0][:], [b0 + ":"], ["xr%da" % s])
+        copy("v" if k < SHARED else "a", to[:, V * s:V * s + 512], T[b0][:], [b0 + ":"], ["xr%da" % s])
         act(to[:, V * s + 512:V * s + V], T[b1][:], ACT.Copy, [b1 + ":"], ["xr%db" % s])
+        shifted("rw%d" % k, T.rw[:, 128 * k:128 * k + 128], T.j16[:], "j16", 16 * k, "rwat")
 
     for k, s in enumerate([s for call in xcalls for s, _ in call] + [r]):
         spread(k, s)
     for k, call in enumerate(xcalls):
         if k == GATE:
-            iota(T.j8[:], [[0, 16], [1, 8]], 0, 0, "j8")
-            iota(T.owi[:], [[128, 8], [1024, 8]], 0, 1, "owi", False)
+            iota(T.owi[:], [[128, 8], [V, 2], [2 * V, 4]], 0, 1, "owi", False)
             iota(T.zoi[:], [[1024, 2], [16, 8]], 0, 0, "zoi")
             wait("g", ("go", 1))
         need("g", [k % s for s, _ in call for k in ("xr%da", "xr%db")], [])
@@ -314,46 +330,22 @@ def rank_program(g, core, T, topo):
     arrive = sum(len(e) for q in others for c in x_calls(T, topo, q) for s, e in c if s == r)
     writer["xw"] = [("xarr", arrive)] + writer["xr%da" % r] + writer["xr%db" % r]
 
-    for f in range(2, 2 * RO + 1):
-        iota(T.k0[:, 4 * f:4 * f + 2, :], [[-HALF, 2], [0, 64]], HALF + 128 * f, 0, "k0a%d" % f)
-        iota(T.k0[:, 4 * f + 2:4 * f + 4, :], [[HALF, 2], [0, 64]], 128 * f, 0, "k0b%d" % f)
-    constants_late()
+    for f in range(2 * RO + 1):
+        iota(T.k0[:, 4 * f:4 * f + 4, :], [[0, 2], [-HALF, 2], [0, 64]], HALF + 128 * f, 0, "k0%d" % f)
 
-    def lists():
-        for s in range(2):
-            group(T.pb1[:, 128 + 64 * s:192 + 64 * s],
-                  [(T.m128[:], T.dg[:, BLK[s][0], :]), (T.neg[:], T.dg[:, BLK[s][1], :])],
-                  ["dg", "m128", "neg"], ["pb1:n"])
+    KA, DG = ["ka0", "ka1"], ["dg0", "dg1"]
 
-    def offsets():
-        ts(T.of[:], T.pb1[:, 128:256], -0.125, ALU.mult, ["pb1:n"], ["of"], -0.4375, ALU.add)
+    def entry(s):
+        for h in range(2):
+            ts(T.dgs[ROWS[0], 2 * s + h, :], T.ui[ROWS[h], s, :], 7, ALU.logical_shift_right, ["ui"], [])
+            ts(T.dgs[ROWS[1], 2 * s + h, :], T.ui[ROWS[h], s, :], 127, ALU.bitwise_and, ["ui"], ["dgs%d" % s])
 
-    def repeat(s, first):
-        for k in range(N):
-            b = WB[2 * (0 if first else 1) + k // 4]
-            c = 128 * (k % 4)
-            mm(T[b][:, c:c + 128], T.rw[:, 128 * k:128 * k + 128], T.dg2[:, 128 * s:128 * s + 128],
-               ["dg2%d" % s, "rw%d" % k], [b + ":"])
+    def first_digits(s):
+        cp(T.dg[:, 2 * s:2 * s + 2, :], T.dgs[:, 2 * s:2 * s + 2, :], ["dgs%d" % s], ["dg%d" % s])
 
-    def stack(s, first):
-        b = "pb0" if first else "pe0"
-        for h, (hi, lo) in enumerate([(T.dlow, T.swy), (T.swx, T.dhigh)]):
-            out = T.pb0[:, 256 + h:384:2] if first else T.pb1[:, 256 + h:384:2]
-            group(out, [(hi[:], T.dg[:, BLK[s][0], :]), (lo[:], T.dg[:, BLK[s][1], :])],
-                  ["dg%d" % s, "dlow", "swy", "swx", "dhigh"], ["pb%d:s" % (0 if first else 1)])
-
-    def stacked(e, s, first):
-        b = "pb0" if first else "pb1"
-        copy(e, T.dg2[:, 128 * s:128 * s + 128], T[b][:, 256:384], [b + ":s"], ["dg2%d" % s])
-
-    def window(e, s, first, half):
-        b = WB[2 * (0 if first else 1) + half]
-        c = V * s + 512 * half
-        copy(e, T.win[:, c:c + 512], T[b][:], [b + ":"], ["win%d%d" % (s, half)])
-
-    def mask(c):
-        act(T.msk[:, 512 * c:512 * c + 512], T.per[:].indirect(T.ol[:, 1 - c // 2, PART[c % 2]]), ACT.Copy,
-            ["per", "low%d" % (c // 2)], ["msk%d" % c])
+    def first_low(s):
+        for h in range(2):
+            cp(T.ol[ROWS[h], s, :], T.dgs[ROWS[1], 2 * s + h, :], ["dgs%d" % s], ["low%d" % s])
 
     def close(s):
         tt(T.ka[:, SLOT[s], :], T.kb[:, SLOT[s], :], T.pe1[:, SLOT[s], :], ALU.min, ["kb", "pe1:"], ["ka%d" % s])
@@ -362,33 +354,73 @@ def rank_program(g, core, T, topo):
         ts(T.dgi[:, SLOT[s], :], T.ka[:, SLOT[s], :], 127, ALU.bitwise_and, ["ka%d" % s], ["dgi%d" % s])
 
     def digits(s):
-        cp(T.dg[:, SLOT[s], :], T.dgi[:, SLOT[s], :], ["dgi%d" % s], ["dg%d" % s])
+        for d in range(2):
+            for h in range(2):
+                cp(T.dg[ROWS[d], 2 * s + h, :], T.dgi[ROWS[h], BLK[s][d], :], ["dgi%d" % s], ["dg%d" % s])
+
+    def all_digits():
+        for d, kind in enumerate((HI, LO)):
+            for h in range(2):
+                cp(T.dg[ROWS[d], h:4:2, :], T.dgi[ROWS[h], kind, :], ["dgi0", "dgi1"], DG)
 
     def low(s):
-        cp(T.ol[:, 1 - s, :], T.dgi[:, BLK[s][1], :], ["dgi%d" % s], ["low%d" % s])
+        cp(T.ol[:, s, :], T.dgi[:, BLK[s][1], :], ["dgi%d" % s], ["low%d" % s])
+
+    def unstack(out, w, s, W, whole=True):
+        for h in range(2):
+            mm(out, T.fold[:, w, 64 - 64 * h:192 - 64 * h], T.dg[:, 2 * s + h, :], ["dg%d" % s, "fold%d" % w], W,
+               whole and h == 0, whole and h == 1)
+
+    NOW = ["pb1:n0", "pb1:n1"]
+
+    def lists(ss=(0, 1)):
+        for s in ss:
+            unstack(T.pb1[:, 2 + s, :], 0, s, [NOW[s]])
+
+    def offsets(lo=0, hi=2):
+        ts(T.of[:, lo:hi, :], T.pb1[:, 2 + lo:2 + hi, :], -0.125, ALU.mult, NOW[lo:hi], ["of0", "of1"][lo:hi], -0.4375, ALU.add)
+
+    def numbers_now(e):
+        if e == "a":
+            op("a", lambda: a.activation(T.ref[:, 2:4, :], T.pb1[:, 2:4, :], ACT.Copy, scale=-1.0), NOW, ["now"])
+        else:
+            ts(T.ref[:, 2:4, :], T.pb1[:, 2:4, :], -1.0, ALU.mult, NOW, ["now"])
+
+    def repeat(s, j, h):
+        b = WB[2 * j + h]
+        for u in range(4 * h, 4 * h + 4):
+            mm(T[b][:, 2 * (u & 2):2 * (u & 2) + 4, u % 2:64:2], T.rw[:, 128 * u:128 * u + 128], T.dg[:, 2 * s:2 * s + 2, :],
+               ["dg%d" % s, "rw%d" % u], [b + ":", b + ":xy", b + ":d"])
+
+    def window(e, s, j, h):
+        c = V * s + 512 * h
+        copy(e, T.win[:, c:c + 512], T[WB[2 * j + h]][:], [WB[2 * j + h] + ":"], ["win%d%d" % (s, h)])
+
+    def mask(e, c):
+        copy(e, T.msk[:, 512 * c:512 * c + 512], T.per[:].indirect(T.ol[:, c // 2, PART[c % 2]]),
+             ["per", "low%d" % (c // 2)], ["msk%d" % c])
 
     def numbers(c, t):
         s = (c // 2 + t) % 2
-        cols = slice(512 * c, 512 * c + 512)
-        tt(T.g1[:, cols], T.win[:, V * s:V * s + V].indirect(T.of[:, 32 * c:32 * c + 32]), T.msk[:, cols],
-           ALU.mult, ["win%d0" % s, "win%d1" % s, "of", "msk%d" % c], ["g1%d" % c])
+        tt(T.g1[:, 512 * c:512 * c + 512], T.win[:, V * s:V * s + V].indirect(T.of[:, c // 2, PART[c % 2]]),
+           T.msk[:, 512 * c:512 * c + 512], ALU.mult, ["win%d0" % s, "win%d1" % s, "of%d" % (c // 2), "msk%d" % c], ["g1%d" % c])
 
     def number_sums(c):
         b = "pb%d" % (c // 2)
         for y in range(4 * c, 4 * c + 4):
-            mm(T[b][:, 8 * (y % 8):8 * (y % 8) + 8], T.g1[:, 128 * y:128 * y + 128], T.selw[:],
-               ["g1%d" % c, "selw"], [b + ":c"])
+            mm(T[b][:, 0, 8 * (y % 8):8 * (y % 8) + 8], T.g1[:, 128 * y:128 * y + 128], T.selw[:],
+               ["g1%d" % c, "selw"], ["%s:c%d" % (b, c % 2)])
 
-    def cand_list(i):
-        cp(T.oc[:, 64 * i:64 * i + 64], T["pb%d" % i][:, 0:64], ["pb%d:c" % i], ["oc%d" % i])
-
-    XY, SUB = ["w0", "w1"], ["w2", "w3", "w2"]
+    def cand_list(i, h):
+        hs = (0, 1) if h == "x" else (h,)
+        lo, hi = 32 * hs[0], 32 * hs[-1] + 32
+        cp(T.oc[:, 64 * i + lo:64 * i + hi], T["pb%d" % i][:, 0, lo:hi], ["pb%d:c%d" % (i, x) for x in hs],
+           ["oc%d" % (2 * i + x) for x in hs])
 
     def cand_digits(i):
         for h, (m, key) in enumerate([(T.lx, "lx"), (T.ly, "ly")]):
-            group(T[XY[i]][:, 64 * h:64 * h + 64],
-                  [(m[:, 7 - q:135 - q], T.g1[:, V * i + 8 * h + q:V * i + V:16]) for q in range(8)],
-                  [key, "g1%d" % (2 * i), "g1%d" % (2 * i + 1)], [XY[i] + ":"])
+            group(T[XY[i]][:, h, :], [(m[:, 7 - q:135 - q], T.g1[:, V * i + 8 * h + q:V * i + V:16]) for q in range(8)],
+                  [key, "g1%d" % (2 * i), "g1%d" % (2 * i + 1)], [XY[i] + ":", XY[i] + ":xy"])
 
     def X(i):
         return T.xy[:, 128 * i:128 * i + 64]
@@ -396,60 +428,58 @@ def rank_program(g, core, T, topo):
     def Y(i):
         return T.xy[:, 128 * i + 64:128 * i + 128]
 
-    def differences(e, i):
-        copy(e, T.xy[:, 128 * i:128 * i + 128], T[XY[i]][:, 0:128], [XY[i] + ":"], ["xy%d" % i])
-        for k in range(len(SKIPS[i]) if DUP[i] else 1):
-            group(T[XY[i]][:, 128 + 64 * k:192 + 64 * k], [(T.wx[:], X(i)), (T.wy[:], Y(i))],
-                  ["xy%d" % i, "wx", "wy"], [XY[i] + ":"])
+    def joined(e, i):
+        copy(e, T.xy[:, 128 * i:128 * i + 128], T[XY[i]][:, 0:2, :], [XY[i] + ":xy"], ["xy%d" % i])
+        for blk in (2, 3, 6)[:2 + i if MERGE else 1]:
+            group(T[XY[i]][:, blk, :], [(T.wx[:], X(i)), (T.wy[:], Y(i))], ["xy%d" % i, "wx", "wy"], [XY[i] + ":xy"])
 
-    def numbers_now():
-        op("a", lambda: a.activation(T.ref[:, 128:256], T.pb1[:, 128:256], ACT.Copy, scale=-1.0), ["pb1:n"], ["now"])
-
-    def first_candidate(e):
-        copy(e, T.ref[:, 0:64], T[XY[0]][:, 128:192], [XY[0] + ":"], ["c0"])
-
-    def eq(k):
-        return T.eq[:, 64 * k:64 * k + 64]
+    def pair_check(i):
+        tt(T.eq[:, 3 * i:3 * i + 2, :], T[XY[i]][:, 2:4, :], T.ref[:, 1:4:2 - i, :][:, 0:2, :] if False else
+           (T.ref[:, 1:4:2, :] if i == 0 else T.ref[:, 1:3, :]), ALU.is_equal, [XY[i] + ":xy", "now", "ref"],
+           ["eq%d" % k for k in ((0, 1), (3, 4))[i]])
 
     def check(k):
         i = min(k // 2, 1)
-        if not DUP[i]:
-            c = 64 * (3, 4, 0, 1, 2)[k]
-            tt(eq(k), T[XY[i]][:, 128:192], T.ref[:, c:c + 64], ALU.is_equal,
-               [XY[i] + ":", ("now", "ref", "c0", "ref", "now")[k]], ["eq%d" % k])
-            return
-        n = 64 * len(SKIPS[i])
-        tt(T.eq[:, 128 * i:128 * i + n], T[XY[i]][:, 128:128 + n], T.ref[:, 192 * (1 - i):192 * (1 - i) + n],
-           ALU.is_equal, [XY[i] + ":", "ref", "now"] + ["c0"] * i, ["eq%d" % j for j in SKIPS[i]])
+        tt(T.eq[:, k, :], T[XY[i]][:, 2, :], T.ref[:, (3, 1, 0, 1, 2)[k], :], ALU.is_equal,
+           [XY[i] + ":xy", ("now", "ref", "c0", "ref", "now")[k]], ["eq%d" % k])
 
-    def slot_max(src, key):
-        tt(T.pen[:], src[:, LO1:LO0 + 1, :], src[:, HI0:HI1 + 1, :], ALU.is_gt, [key], ["pen"])
+    def add(i, terms, R, stop):
+        for k, (blk, lhsT, rhs) in enumerate(terms):
+            mm(T["pe%d" % i][:, blk, :], lhsT, rhs, R, ["pe%d:" % i], False, stop and k == len(terms) - 1)
 
-    def add(b, blk, lhsT, rhs, R, stop=False):
-        mm(T[b][:, blk, :], lhsT, rhs, R, [b + ":"], False, stop)
+    def open_keys(i, f, under):
+        mm(T["pe%d" % i][:, 0:4, :], T.one[:], T.k0[:, 4 * f:4 * f + 4, :], ["one", "k0%d" % f], ["pe%d:" % i], True, False)
+        add(i, [(SLOT[s], T.nbig[:], T.ones[:]) for s in under], ["nbig", "ones"], False)
 
-    def open_sum(b, f):
-        mm(T[b][:, 0:4, :], T.one[:], T.k0[:, 4 * f:4 * f + 4, :], ["one", "k0a%d" % f, "k0b%d" % f], [b + ":"],
-           True, False)
+    def add_digits(i, stop):
+        pick = [(T.dlow, T.dhigh), (T.swx, T.swy)]
+        add(i, [(blk, pick[blk // 2][y][:], (X, Y)[y](i)) for blk in range(4) for y in range(2)],
+            ["xy%d" % i, "dlow", "dhigh", "swx", "swy"], stop)
 
-    def add_digits(i, stop=False):
-        b = "pe%d" % i
-        for s in range(2):
-            add(b, BLK[s][0], T.dlow[:], X(i), ["xy%d" % i, "dlow"])
-            add(b, BLK[s][0], T.dhigh[:], Y(i), ["xy%d" % i, "dhigh"])
-            add(b, BLK[s][1], T.swx[:], X(i), ["xy%d" % i, "swx"])
-            add(b, BLK[s][1], T.swy[:], Y(i), ["xy%d" % i, "swy"], stop and s == 1)
+    def digit_sum(i):
+        ks = [(0, 1), (2, 3, 4)][i]
+        for d, (wx, wy) in enumerate([(T.dlow, T.dhigh), (T.swx, T.swy)]):
+            group(T[XY[i]][:, 4 + d, :], [(wx[:], X(i)), (wy[:], Y(i))] + [(T.big[:], T.eq[:, k, :]) for k in ks],
+                  ["xy%d" % i, "dlow", "dhigh", "swx", "swy", "big"] + ["eq%d" % k for k in ks], [XY[i] + ":d"])
 
-    def add_skips(k, stop=False):
-        for blk in range(4):
-            add("pe%d" % min(k // 2, 1), blk, T.big[:], eq(k), ["big", "eq%d" % k], stop and blk == 3)
+    def digit_copy(e, i):
+        copy(e, T.dd[:, 2 * i:2 * i + 2, :], T[XY[i]][:, 4:6, :], [XY[i] + ":d"], ["dd%d" % i])
 
-    def add_not_max(i, stop=False):
-        todo = [(s, blk) for s in range(2) for blk in BLK[s]]
-        for s, blk in todo:
-            add("pe%d" % i, blk, T.big[:], T.pen[:, 64 * s:64 * s + 64], ["big", "pen"], stop and (s, blk) == todo[-1])
+    def digit_add(i, stop):
+        add(i, [(SLOT[s], T.one[:], T.dd[:, 2 * i:2 * i + 2, :]) for s in range(2)], ["one", "dd%d" % i], stop)
 
-    OWN = [(0, 256), (256, 512), (512, V)]
+    def add_skips(k, stop):
+        add(min(k // 2, 1), [(blk, T.big[:], T.eq[:, k, :]) for blk in range(4)], ["big", "eq%d" % k], stop)
+
+    def top(i):
+        if i == 0:
+            tt(T.pen[:, 0, :], T.ka[:, HI1, :], T.ka[:, HI0, :], ALU.is_gt, KA, ["pen0"])
+        else:
+            tt(T.pen[:, 1:3, :], T.ka[:, HI1:LO0 + 1, :], T.pe0[:, HI, :], ALU.is_gt, KA + ["pe0:"], ["pen1"])
+
+    def below(i, pens, key, stop):
+        add(i, [(blk, (T.big, T.nbig)[(blk + k // 2) % 2][:], T.pen[:, k, :]) for k in pens for blk in range(4)],
+            ["big", "nbig", key], stop)
 
     def own_keys(lo, hi):
         return ["own%d" % x for x, y in OWN if x < hi and lo < y]
@@ -462,123 +492,122 @@ def rank_program(g, core, T, topo):
     def absolute(lo, hi, dif, ab, tag):
         act(ab[:, lo:hi], dif[:, lo:hi], ACT.Abs, ["dif%s%d" % (tag, lo)], ["ab%s%d" % (tag, lo)])
 
-    def sums(b, blks, lo, hi, ab, tag, stop=False):
+    relu = {}
+
+    def positive(lo, hi, dif, ab, tag):
+        ts(ab[:, lo:hi], dif[:, lo:hi], 0.0, ALU.max, ["dif%s%d" % (tag, lo)], ["ab%s%d" % (tag, lo)])
+        relu[tag, lo] = dif
+
+    def sums(b, blks, lo, hi, ab, tag, stop):
         n = len(range(4)[blks])
+        dif = relu.pop((tag, lo), None)
+        terms = [(ab, T.sel4)] if dif is None else [(ab, T.selr), (dif, T.seld)]
         for y in range(lo // 128, hi // 128):
-            mm(T[b][:, blks, 8 * (y % 8):8 * (y % 8) + 8], ab[:, 128 * y:128 * y + 128], T.sel4[:, 0:n, :],
-               ["ab%s%d" % (tag, lo), "sel4"], [b + ":"], False, stop and y == hi // 128 - 1)
+            for k, (data, sel) in enumerate(terms):
+                mm(T[b][:, blks, 8 * (y % 8):8 * (y % 8) + 8], data[:, 128 * y:128 * y + 128], sel[:, 0:n, :],
+                   ["ab%s%d" % (tag, lo), "sel4", "selr", "seld"] + ["dif%s%d" % (tag, lo)] * k, [b + ":"], False,
+                   stop and y == hi // 128 - 1 and k == len(terms) - 1)
+
+    def sub_bank(k):
+        return T[SUB[k]][:, 0:(CH[k][1] - CH[k][0]) // 64, :]
 
     def scalar_features(k):
         lo, hi = CH[k]
-        act(T.dif[:, lo:hi], T.xw[:].indirect(T.oc[:, lo // 16:hi // 16]), ACT.Copy, ["xw", "oc%d" % (lo // V)],
+        act(T.dif[:, lo:hi], T.xw[:].indirect(T.oc[:, lo // 16:hi // 16]), ACT.Copy, ["xw", "oc%d" % (lo // 512)],
             ["difr%d" % lo])
-
-    def subtract(k):
-        lo, hi = CH[k]
-        mm(T[SUB[k]][:, 0:hi - lo], T.one[:], T.dif[:, lo:hi], ["one", "difr%d" % lo], [SUB[k] + ":"], False, True)
 
     def before_subtract(k):
         lo, hi = CH[k]
         o = lo % V
-        mm(T[SUB[k]][:, 0:hi - lo], T.neg[:], T.own[:, o:o + hi - lo], ["neg"] + own_keys(o, o + hi - lo),
-           [SUB[k] + ":"], True, False)
+        mm(sub_bank(k), T.neg[:], T.own[:, o:o + hi - lo], ["neg"] + own_keys(o, o + hi - lo), [SUB[k] + ":"], True, False)
+
+    def subtract(k):
+        lo, hi = CH[k]
+        mm(sub_bank(k), T.one[:], T.dif[:, lo:hi], ["one", "difr%d" % lo], [SUB[k] + ":"], False, True)
 
     def scalar_abs(k):
         lo, hi = CH[k]
-        act(T.ab[:, lo:hi], T[SUB[k]][:, 0:hi - lo], ACT.Abs, [SUB[k] + ":"], ["abr%d" % lo])
-
-    def round_features(k):
-        features(*CH[k], T.oc, "oc%d" % (CH[k][0] // V), T.dif, "r")
-
-    def round_abs(k):
-        absolute(*CH[k], T.dif, T.ab, "r")
-
-    def round_sums(k, stop=False):
-        sums("pe%d" % (CH[k][0] // V), slice(0, 4), *CH[k], T.ab, "r", stop)
+        act(T.ab[:, lo:hi], sub_bank(k), ACT.Abs, [SUB[k] + ":"], ["abr%d" % lo])
 
     def start_lists():
-        op("v", lambda: v.tensor_copy(T.zt[:], T.win[:].indirect(T.zo[:])),
-           ["win00", "win01", "win10", "win11", "zo"], ["zt"])
-        group(T.pb0[:, 128:256], [(T.wx[:], T.zt[:, 0:256:2]), (T.wz[:], T.zt[:, 1:256:2])],
-              ["zt", "wx", "wz"], ["pb0:z"])
+        cp(T.zt[:], T.win[:].indirect(T.zo[:]), ["win00", "win01", "win10", "win11", "zo"], ["zt"])
+        group(T.pb0[:, 2:4, :], [(T.wx[:], T.zt[:, 0:256:2]), (T.wz[:], T.zt[:, 1:256:2])], ["zt", "wx", "wz"], ["pb0:z"])
 
     def own_features(k):
         lo, hi = OWN[k]
         act(T.own[:, lo:hi], T.xw[:].indirect(T.ow[:, lo // 16:hi // 16]), ACT.Copy, ["xw", "ow"], ["own%d" % lo])
 
     def start_open():
-        open_sum("pe1", 0)
-        mm(T.pe1[:, 0:4, :], T.one[:], T.dg[:], ["one", "dg"], ["pe1:"], False, False)
+        open_keys(1, 0, (0, 1))
+        for blk in range(4):
+            unstack(T.pe1[:, blk, :], 1 + blk // 2, blk % 2, ["pe1:"], False)
 
-    START = OWN + [(V, 1536), (1536, 2 * V)]
+    RESULT = [lambda: ts(T.di[:], T.ka[:, HI, :], 12, ALU.logical_shift_right, KA, ["di"], 4095, ALU.bitwise_and),
+              lambda: ts(T.pb1[:, 2:4, :], T.dgi[:, HI, :], 128.0, ALU.mult, ["dgi0", "dgi1"], NOW),
+              lambda: cp(T.da[:], T.di[:], ["di"], ["da"]),
+              lambda: tt(T.un[:], T.pb1[:, 2:4, :], T.dgi[:, LO, :], ALU.add, NOW + ["dgi0", "dgi1"], ["un"])]
 
-    def start_features(k):
-        features(*START[k], T.ob, "ob", T.dif0, "i")
-
-    def start_abs(k):
-        lo, hi = START[k]
-        absolute(lo, hi, T.dif0, T.ab0, "i")
-        sums("pe1", slice(0, 4, 3) if lo < V else slice(1, 3), lo, hi, T.ab0, "i", hi == 2 * V)
-
-    def step(to, tkey, src, skey, b):
-        tt(to[:], src[:], T[b][:, 0:4, :], ALU.min, [skey, b + ":"], [tkey])
-
-    ts(T.dgi[:, HI0:HI1 + 1, :], T.ui[:], 7, ALU.logical_shift_right, ["ui"], ["high digits"])
-    for s in range(2):
-        ts(T.dgi[:, BLK[s][1], :], T.ui[:, 64 * s:64 * s + 64], 127, ALU.bitwise_and, ["ui"], ["dgi%d" % s])
-    for call, s in [(digits, 0), (low, 0), (digits, 1), (low, 1)]:
-        call(s)
-    for t in range(RO):
-        s0, s1 = t % 2, (t + 1) % 2
-        piece = {
-            "close": close, "cut": cut, "digits": lambda k: digits((s1, s0)[k]), "low": low,
-            "lists": lists, "offsets": offsets,
-            "rep": lambda k: repeat((s0, s1)[k], k == 0),
-            "stack": lambda k: stack((s0, s1)[k], k == 0),
-            "stv": lambda k: stacked("v", (s0, s1)[k], k == 0), "sta": lambda k: stacked("a", (s0, s1)[k], k == 0),
-            "winv": lambda k: window("v", (s0, s1)[k // 2], k < 2, k % 2),
-            "wina": lambda k: window("a", (s0, s1)[k // 2], k < 2, k % 2),
-            "mask": mask, "num": lambda c: numbers(c, t), "bsum": number_sums, "list": cand_list,
-            "xy": cand_digits, "difv": lambda i: differences("v", i), "difa": lambda i: differences("a", i),
-            "check": check, "presub": before_subtract, "now": numbers_now,
-            "cv": lambda: first_candidate("v"), "ca": lambda: first_candidate("a"),
-            "open": lambda i: open_sum("pe%d" % i, 2 * t + 1 + i),
-            "max": lambda i: slot_max(*[(T.ka, "ka"), (T.kb, "kb")][i]),
-            "notmax": add_not_max, "adddig": add_digits, "skip": add_skips, "sum": round_sums,
-            "fa": scalar_features, "sub": subtract, "aa": scalar_abs, "fv": round_features, "av": round_abs,
-            "step": lambda i: step(T.kb, "kb", T.ka, "ka", "pe0"),
-            "zt": start_lists, "ob": lambda: cp(T.ob[:], T.pb0[:, 128:256], ["pb0:z"], ["ob"]),
-            "own": own_features, "iopen": start_open, "if": start_features, "ia": start_abs,
-            "ka": lambda: cp(T.ka[:], T.pe1[:, 0:4, :], ["pe1:"], ["ka"])}
-        order = [n for n in (FIRST if t == 0 else LATER).split() if t < RO - 1 or n[:-1] not in ("low", "digits")]
-        last = {}
-        for name in order:
-            if name[:-1] in ("notmax", "adddig", "skip", "sum"):
-                k = int(name[-1])
-                last[{"sum": CH[k][0] // V, "skip": min(k // 2, 1)}.get(name[:-1], k)] = name
-        for name in order:
-            if name in last.values():
-                piece[name[:-1]](int(name[-1]), True)
-            elif name[-1].isdigit():
-                piece[name[:-1]](int(name[-1]))
-            else:
-                piece[name]()
-
-    ts(T.di[:], T.ka[:, HI0:HI1 + 1, :], 12, ALU.logical_shift_right, ["ka"], ["di"])
-    ts(T.pb1[:, 128:256], T.dgi[:, HI0:HI1 + 1, :], 128.0, ALU.mult, ["dgi0", "dgi1"], ["pb1:n"])
-    cp(T.da[:], T.di[:], ["di"], ["da"])
-    for s in range(2):
-        tt(T.un[:, 64 * s:64 * s + 64], T.pb1[:, 128 + 64 * s:192 + 64 * s], T.dgi[:, BLK[s][1], :], ALU.add,
-           ["pb1:n", "dgi%d" % s], ["un%d" % s])
-    writer["un"] = writer["un1"]
+    order = [(n.lstrip("+"), t + n.count("+")) for t in range(RO)
+             for n in (FIRST, LATER, EVEN or LATER, LAST)[t].split()]
+    last, seen = set(), {}
+    for k, (n, _) in enumerate(order):
+        name = n.rstrip("0123456789x")
+        if name in ("below", "adddig", "dadd", "skip", "sum", "isum", "again"):
+            i = int(n[-1]) if name != "again" else 1
+            seen[{"skip": min(i // 2, 1), "sum": CH[i][0] // V, "isum": 1}.get(name, i)] = k
+        if n in ("step0", "top1") and 0 in seen:
+            last.add(seen.pop(0))
+        if name in ("close", "closeall", "ka") and 1 in seen:
+            last.add(seen.pop(1))
+    for k, (n, t) in enumerate(order):
+        name = n.rstrip("0123456789x")
+        x = [c if c == "x" else int(c) for c in n[len(name):]]
+        stop = k in last
+        s = (x[0] + t) % 2 if x and x[0] != "x" else None
+        CUR[0] = (t, k, n)
+        {"const": lambda: constants("v", *x), "consta": lambda: constants("a", *x), "entry": lambda: entry(*x), "first": lambda: first_digits(*x),
+         "firstlow": lambda: first_low(*x),
+         "close": lambda: close(s), "cut": lambda: cut(s), "digits": lambda: digits(s), "low": lambda: low(*x),
+         "lists": lambda: lists(x) if x else lists(), "offsets": lambda: offsets(x[0], x[0] + 1) if x else offsets(),
+         "rep": lambda: repeat(s, *x),
+         "winv": lambda: window("v", s, *x), "wina": lambda: window("a", s, *x),
+         "mask": lambda: mask("a", *x), "maskv": lambda: mask("v", *x), "num": lambda: numbers(*x, t),
+         "bsum": lambda: number_sums(*x), "list": lambda: cand_list(*x), "xy": lambda: cand_digits(*x),
+         "difv": lambda: joined("v", *x), "difa": lambda: joined("a", *x), "check": lambda: check(*x),
+         "nowv": lambda: numbers_now("v"), "nowa": lambda: numbers_now("a"),
+         "cv": lambda: copy("v", T.ref[:, 0, :], T[XY[0]][:, 2, :], [XY[0] + ":xy"], ["c0"]),
+         "ca": lambda: copy("a", T.ref[:, 0, :], T[XY[0]][:, 2, :], [XY[0] + ":xy"], ["c0"]),
+         "open": lambda: open_keys(*x, 2 * t + 1 + x[0], (0,)), "adddig": lambda: add_digits(*x, stop),
+         "pair": lambda: pair_check(*x), "digitsall": all_digits,
+         "closeall": lambda: tt(T.ka[:], T.kb[:], T.pe1[:, 0:4, :], ALU.min, ["kb", "pe1:"], KA),
+         "cutall": lambda: ts(T.dgi[:], T.ka[:], 127, ALU.bitwise_and, KA, ["dgi0", "dgi1"]),
+         "lowall": lambda: cp(T.ol[:], T.dgi[:, LO, :], ["dgi0", "dgi1"], ["low0", "low1"]),
+         "dsum": lambda: digit_sum(*x), "dcv": lambda: digit_copy("v", *x), "dca": lambda: digit_copy("a", *x),
+         "dadd": lambda: digit_add(*x, stop), "skip": lambda: add_skips(*x, stop), "top": lambda: top(*x),
+         "below": lambda: below(*x, [(0,), (1, 2)][x[0]], "pen%d" % x[0], stop),
+         "again": lambda: below(1, (0,), "pen0", stop),
+         "step": lambda: tt(T.kb[:], T.ka[:], T.pe0[:, 0:4, :], ALU.min, KA + ["pe0:"], ["kb"]),
+         "fv": lambda: features(*CH[x[0]], T.oc, "oc%d" % (CH[x[0]][0] // 512), T.dif, "r"),
+         "av": lambda: absolute(*CH[x[0]], T.dif, T.ab, "r"),
+         "fa": lambda: scalar_features(*x), "presub": lambda: before_subtract(*x), "sub": lambda: subtract(*x),
+         "aa": lambda: scalar_abs(*x),
+         "sum": lambda: sums("pe%d" % (CH[x[0]][0] // V), slice(0, 4), *CH[x[0]], T.ab, "r", stop),
+         "zt": start_lists, "ob": lambda: cp(T.ob[:], T.pb0[:, 2:4, :], ["pb0:z"], ["ob"]),
+         "own": lambda: own_features(*x), "iopen": start_open,
+         "if": lambda: features(*START[x[0]], T.ob, "ob", T.dif0, "i"),
+         "ia": lambda: absolute(*START[x[0]], T.dif0, T.ab0, "i"), "ir": lambda: positive(*START[x[0]], T.dif0, T.ab0, "i"),
+         "isum": lambda: sums("pe1", SLOT[START[x[0]][0] // V], *START[x[0]], T.ab0, "i", stop),
+         "ka": lambda: cp(T.ka[:], T.pe1[:, 0:4, :], ["pe1:"], KA),
+         "out": lambda: RESULT[x[0]]()}[name]()
 
     dma("s", T.od[:, 0:64, :], T.un[:], "o1", ["un"], ["od1"])
     dma("a", T.od[:, 64:128, :], T.da[:], "o2", ["da"], ["od2"])
-    dma("s", T.ob2[r, 0:64, :], T.un[mine, :], "o3", ["un"], ["ol1own"])
-    dma("a", T.ob2[r, 64:128, :], T.da[mine, :], "o4", ["da"], ["ol2own"])
+    home = slice(16 * place(r), 16 * place(r) + 16)
+    dma("s", T.ob2[r, 0:64, :], T.un[home, :], "o3", ["un"], ["ol1own"])
+    dma("a", T.ob2[r, 64:128, :], T.da[home, :], "o4", ["da"], ["ol2own"])
     need("g", ["od1", "od2"], [])
     g.remote_dma_fused([RemoteDMATransfer(dst_ids=[dst(s)], dma_engine_mask=bits(eng[2 * k:2 * k + 2]),
-                                          remote_sem=S.oarr, src=T.od[s], dst=T.ob2[r])
+                                          remote_sem=S.oarr, src=T.od[place(s)], dst=T.ob2[r])
                         for k, s in enumerate(others)], local_sem=S.osent)
     writer["ol"] = [("oarr", 2 * (N - 1))]
     dma("s", T.ynb[:], T.ob2[:, 0:64, :], "y1", ["ol", "ol1own"], ["y1"])

from concourse.bass import DstId, RemoteDMATransfer
from concourse.mybir import AluOpType as ALU, ActivationFunctionType as ACT

N = 8
V = 1024
RO = 4
BIG = float(1 << 24)
DS = 4096.0
HALF = 2048
WB = ["w0", "pe2", "w2", "w3"]
BANKS = WB + ["pb0", "pb1", "pe0", "pe1"]
HI0, HI1, LO0, LO1 = range(4)
BLK = [(HI0, LO0), (HI1, LO1)]
PART = [slice(0, 32), slice(32, 64)]
ROWS = [slice(0, 64), slice(64, 128)]
SLOT = [slice(0, 4, 2), slice(1, 4, 2)]
HI, LO = slice(0, 2), slice(2, 4)
GATE = 1
SHARED = 8
MERGE = False
CH = [(0, 512), (512, 1024), (1024, 1536), (1536, 1792), (1792, 2048)]
OWN = [(0, 256), (256, 512), (512, V)]
START = OWN + [(V, 1536), (1536, 2 * V)]
XY, SUB = WB[:2], [WB[2], WB[3], WB[2]]

TAIL = " +close0 +close1 +cut0 +cut1 +low0 +digits0 +low1 +digits1"
FIRST = """const0 const1 const2 const3 const5 const6 const7 const4 entry first0 firstlow first1 lists rep00 rep01 mask0 offsets
    mask1 winv00 mask2 winv01 rep10 rep11 num1 wina10 num0 iopen wina11 bsum1 mask3 bsum0 num2 xy0 list0x zt difv0 num3 own1
    nowa own0 open0 own2 ob check0 fa1 adddig0 if1 bsum3 bsum2 list1x xy1 presub0 ia1 isum1 presub1 if2 if3 if0 if4 skip0 fa0
    ia2 isum2 check1 ia3 isum3 sub0 ia0 isum0 sub1 fv2 ia4 isum4 ca ka difa1 fv4 top0 aa0 check2 skip1 fv3 open1 adddig1 aa1
    sum0 below0 again av2 sum1 skip2 check3 top1 step0 check4 av4 skip3 sum2 skip4 av3 sum4 below1 sum3""" + TAIL
HEAD = """top0 mask1 mask0 rep00 rep01 winv00 wina01 lists mask2 offsets rep10 rep11 winv10 open1 num0 open0 below0
    again num1 presub0 bsum0 list00 wina11 presub1 num2 mask3 bsum1 list01 xy0 bsum2 fa0 sub0 difa0 num3 xy1 nowv list10 fa1 aa0
    check1 sub1 fv2 bsum3 adddig0 skip1 difa1 adddig1 aa1 check0 sum0 skip0 list11 cv fv4 sum1 check3 skip3 check4 fv3 av2
    skip4 sum2 check2 av4 skip2 top1 sum4 av3 below1 step0 sum3"""
LATER = HEAD + TAIL
LAST = HEAD + " +close0 +close1 out0 +cut0 +cut1 out1 out2 out3"
FIRST = "const0 const2 const8 const6 const5 const1 const3 const7 const4 entry0 entry1 first1 firstlow0 firstlow1 first0 rep10 mask1 winv10 lists offsets rep00 rep01 wina00 winv01 num1 mask0 num0 rep11 wina11 bsum0 zt mask2 num2 mask3 own0 xy0 ob num3 bsum1 list0x bsum2 own1 bsum3 own2 if1 iopen if0 if2 presub0 xy1 open0 if3 ir2 nowa ia1 fa0 difa0 adddig0 sub0 if4 isum2 fa1 ia3 ia0 presub1 sub1 isum3 isum0 check0 check1 list1x ir4 skip1 fv2 isum4 isum1 ka difa1 check4 check3 skip0 aa0 sum0 ca open1 adddig1 top0 fv3 below0 aa1 sum1 skip3 skip4 fv4 av2 again av3 sum2 sum3 check2 skip2 top1 below1 step0 av4 sum4 +close1 +close0 +cut1 +cut0 +low0 +digits0 +digits1 +low1"
LAST = "open1 top0 rep00 mask0 winv00 mask1 rep01 wina01 rep10 winv10 lists again rep11 wina11 offsets num0 num1 open0 below0 mask2 presub0 bsum0 mask3 list00 bsum1 num2 list01 xy0 presub1 bsum2 fa0 sub0 difa0 num3 list10 xy1 fa1 sub1 check1 nowv fv2 bsum3 aa0 list11 adddig0 difa1 check0 adddig1 sum0 skip1 cv aa1 av2 fv4 sum1 av4 skip0 check3 skip3 check4 skip4 sum2 fv3 av3 check2 skip2 top1 sum4 step0 below1 sum3 +close1 +close0 +cut1 +cut0 out0 out1 out2 out3"
FIRST = "consta8 const6 const2 const3 entry0 consta7 entry1 consta0 firstlow0 first1 rep10 first0 rep00 const4 consta5 firstlow1 consta1 lists winv10 mask1 offsets wina00 rep01 winv01 num1 mask0 num0 rep11 wina11 iopen xy0 zt mask2 num2 nowa ob bsum1 mask3 num3 own0 if0 open0 bsum0 list0x difa0 check0 adddig0 own1 if3 skip0 own2 fa1 presub1 bsum3 if2 fa0 if1 bsum2 presub0 if4 ia3 list1x xy1 ia0 sub1 isum0 ir2 check1 ir4 ia1 sub0 isum1 isum3 isum2 isum4 fv2 skip1 aa1 sum1 ka fv3 aa0 sum0 difa1 check4 open1 top0 ca adddig1 skip4 check3 below0 again fv4 check2 skip3 av2 sum2 av3 sum3 top1 skip2 below1 step0 av4 sum4 +close1 +close0 +cut1 +cut0 +low0 +digits0 +low1 +digits1"
LATER = "open0 mask0 open1 rep01 wina01 rep00 mask1 top0 winv00 lists offsets rep10 winv10 rep11 presub0 num0 bsum0 mask2 below0 num1 list00 wina11 presub1 bsum1 mask3 xy0 num2 again bsum2 fa0 sub0 difa0 list01 fa1 num3 list10 xy1 nowv fv2 bsum3 list11 aa0 check1 sub1 aa1 adddig0 cv skip1 difv1 sum0 check0 adddig1 sum1 av2 fv4 av4 check2 check3 skip2 check4 skip0 skip3 fv3 sum2 skip4 top1 av3 sum4 below1 step0 sum3 +close0 +close1 +cut0 +low0 +cut1 +digits0 +low1 +digits1"
EVEN = "mask1 top0 rep00 lists0 rep01 winv00 rep10 mask0 lists1 wina01 open0 winv10 rep11 offsets0 presub0 offsets1 num0 num1 wina11 presub1 bsum0 list00 mask2 num2 open1 again mask3 fa0 bsum1 list01 xy0 num3 below0 bsum2 sub0 list10 difa0 adddig0 nowv xy1 fv2 fa1 sub1 bsum3 aa0 sum0 check0 skip0 difa1 cv adddig1 check1 list11 fv4 skip1 check3 check4 aa1 sum1 skip3 skip4 fv3 av2 check2 top1 sum2 av4 skip2 sum4 av3 step0 below1 sum3 +close1 +close0 +cut1 +cut0 +low0 +digits0 +digits1 +low1"
LAST = "rep01 rep00 lists top0 winv00 rep10 mask0 rep11 offsets open1 again winv10 wina01 num0 presub0 mask1 open0 wina11 below0 bsum0 num1 list00 xy0 bsum1 presub1 mask2 num2 bsum2 difv0 adddig0 list01 mask3 num3 fa0 fa1 nowv list10 sub0 aa0 check0 xy1 fv2 sub1 bsum3 list11 skip0 check1 sum0 difa1 cv fv3 aa1 check4 check3 skip1 av2 check2 fv4 adddig1 sum1 skip4 av3 skip3 sum2 skip2 av4 top1 step0 sum3 below1 sum4 +close0 +close1 +cut0 +cut1 out0 out1 out2 out3"
TRACE, CUR = [], [None]

SCRATCH = {}
for _names, _where, _shape, _dt in [
        ("xs own", "sbuf", [128, V], "bfloat16"),
        ("xr xw", "sbuf", [128, N * V], "bfloat16"),
        ("nbd nbl", "dram", [N, 128, 16], "int32"),
        ("od ob2", "dram", [N, 128, 32], "float32"),
        ("pidx", "sbuf", [128, 8], "int32"),
        ("pbit", "sbuf", [128, 16], "int32"),
        ("pf pc", "sbuf", [128, 16], "float32"),
        ("un da", "sbuf", [128, 2, 64], "float32"),
        ("lx ly", "sbuf", [128, 144], "bfloat16"),
        ("j192", "sbuf", [128, 192], "bfloat16"),
        ("down up", "sbuf", [128, 128], "bfloat16"),
        ("sel", "sbuf", [128, 32], "bfloat16"),
        ("owi", "sbuf", [128, 64], "int32"),
        ("zoi", "sbuf", [128, 16], "float32"),
        ("j16 j8 per one neg big nbig ones wx wy wz dlow dhigh swx swy", "sbuf", [128, 128], "bfloat16"),
        ("pen", "sbuf", [128, 3, 64], "bfloat16"),
        ("rep xy zt", "sbuf", [128, 256], "bfloat16"),
        ("rw", "sbuf", [128, N * 128], "bfloat16"),
        ("fold", "sbuf", [128, 4, 192], "bfloat16"),
        ("selw", "sbuf", [128, 8], "bfloat16"),
        ("sel4 seld selr", "sbuf", [128, 4, 8], "bfloat16"),
        ("k0", "sbuf", [128, (2 * RO + 1) * 4, 64], "bfloat16"),
        ("ref", "sbuf", [128, 4, 64], "float32"),
        ("eq", "sbuf", [128, 5, 64], "bfloat16"),
        ("ow", "sbuf", [128, 64], "uint16"),
        ("zo", "sbuf", [128, 16], "uint16"),
        ("oc ob", "sbuf", [128, 128], "uint16"),
        ("of ol", "sbuf", [128, 2, 64], "uint16"),
        ("ui di", "sbuf", [128, 2, 64], "int32"),
        ("ka kb dgi dgs", "sbuf", [128, 4, 64], "int32"),
        ("dg dd", "sbuf", [128, 4, 64], "bfloat16"),
        ("win msk g1 dif ab dif0 ab0", "sbuf", [128, 2048], "bfloat16"),
        (" ".join(BANKS), "psum", [128, 8, 64], "float32")]:
    for _n in _names.split():
        SCRATCH[_n] = (_where, _shape, _dt)

SEMAPHORES = ["cv", "ca", "cp", "cg", "xld", "go", "nbs", "nbo", "nbarr", "nbsent", "nbld", "xarr", "xsent",
              "o1", "o2", "o3", "o4", "oarr", "osent", "y1", "y2"]


def bits(engines):
    m = 0
    for e in engines:
        m |= 1 << e
    return m


def place(rank):
    return N // 2 * (rank % 2) + rank // 2


def x_calls(T, topo, r):
    me = T.cores[r]
    others = [(r + k) % N for k in range(1, N)]
    far = [s for s in others if topo.die(T.cores[s]) != topo.die(me)]
    near = [s for s in others if topo.die(T.cores[s]) == topo.die(me)]
    calls = []
    while far or near:
        pair = ([far.pop(0)] if far else []) + ([near.pop(0)] if near else [])
        calls.append([(s, topo.engines(me, T.cores[s])[k::len(pair)]) for k, s in enumerate(pair)])
    return sorted(calls, key=len)


def rank_program(g, core, T, topo):
    r = T.rank_of(core)
    if r is None:
        return
    S = T.sem
    queue = {"v": g.vector, "a": g.scalar, "p": g.tensor, "g": g, "s": g.sync}
    own_sem = {"v": "cv", "a": "ca", "p": "cp", "g": "cg"}
    count = {"v": 0, "a": 0, "p": 0, "g": 0}
    waited = {e: {} for e in queue}
    writer = {}
    readers = {}
    bank = {b: {} for b in BANKS}

    def wait(e, tok):
        if waited[e].get(tok[0], 0) < tok[1]:
            queue[e].wait_ge(S[tok[0]], tok[1])
            waited[e][tok[0]] = tok[1]

    def need(e, R, W):
        toks = {}

        def add(t):
            toks[t[0]] = max(toks.get(t[0], 0), t[1])
        for k in R:
            for t in writer.get(k, []):
                if e != "p" or t[0] != "cp":
                    add(t)
        for k in W:
            for t in writer.get(k, []) + readers.get(k, []):
                if t[0] != own_sem.get(e):
                    add(t)
        for k in list(R) + list(W):
            for e2, t in bank.get(k.split(":")[0], {}).items():
                if e2 != e:
                    add(t)
        for s, n in toks.items():
            wait(e, (s, n))

    def note(e, tok, R, W):
        for k in R:
            readers.setdefault(k, []).append(tok)
        for k in W:
            writer[k] = [tok]
            readers[k] = []
        for k in list(R) + list(W):
            b = k.split(":")[0]
            if b in bank:
                bank[b][e] = tok

    def op(e, call, R, W):
        TRACE.append((CUR[0], R, W))
        need(e, R, W)
        count[e] += 1
        call().then_inc(S[own_sem[e]], 1)
        note(e, (own_sem[e], count[e]), R, W)

    def dma(e, out, in_, sem, R, W):
        need(e, R, W)
        queue[e].dma_start(out, in_).then_inc(S[sem], 16)
        note(e, (sem, 16), R, W)

    v, a, p = g.vector, g.scalar, g.tensor

    def tt(out, in0, in1, o, R, W):
        op("v", lambda: v.tensor_tensor(out, in0, in1, o), R, W)

    def ts(out, in0, s1, o0, R, W, s2=None, o1=None):
        if o1 is None:
            op("v", lambda: v.tensor_scalar(out, in0, s1, None, o0), R, W)
        else:
            op("v", lambda: v.tensor_scalar(out, in0, s1, s2, o0, o1), R, W)

    def cp(out, in_, R, W):
        op("v", lambda: v.tensor_copy(out, in_), R, W)

    def fill(out, c, W):
        op("v", lambda: v.memset(out, c), [], W)

    def act(out, in_, f, R, W):
        op("a", lambda: a.activation(out, in_, f), R, W)

    def copy(e, out, in_, R, W):
        if e == "v":
            cp(out, in_, R, W)
        else:
            act(out, in_, ACT.Copy, R, W)

    def mm(out, lhsT, rhs, R, W, start=True, stop=True):
        op("p", lambda: p.matmul(out, lhsT, rhs, start, stop), R, W)

    def group(out, terms, R, W):
        for k, (lhsT, rhs) in enumerate(terms):
            mm(out, lhsT, rhs, R, W, k == 0, k == len(terms) - 1)

    def dst(s):
        rid, pid, _ = topo.addr(T.cores[s])
        return DstId(rid=rid, pnc=pid)

    others = [(r + k) % N for k in range(1, N)]
    eng = topo.engines(core, T.cores[others[0]])
    mine = slice(16 * r, 16 * r + 16)

    dma("s", T.nbd[:], T.nb[:], "nbs", [], ["nbd"])
    dma("s", T.xs[:], T.x[:], "xld", [], ["xs"])
    dma("s", T.nbl[place(r)], T.nb[mine, :], "nbo", [], ["nblown"])

    def iota(out, pattern, base, cm, key, flt=True):
        if flt:
            op("g", lambda: g.iota(out, pattern, base, cm, allow_small_or_imprecise_dtypes=True), [], [key])
        else:
            op("g", lambda: g.iota(out, pattern, base, cm), [], [key])

    iota(T.pidx[:], [[0, 8]], 0, 1, "pidx", False)
    iota(T.j16[:], [[0, 8], [1, 16]], 0, 0, "j16")
    iota(T.j192[:], [[1, 192]], 0, 0, "j192")
    iota(T.j8[:], [[0, 16], [1, 8]], 0, 0, "j8")
    FIELD = dict(p=(0, 127), p31=(0, 31), high=(3, 1), upper=(6, 1), grp=(4, 7), pno8=(0, 119), p7=(0, 7), p120=(0, 120),
                 p6=(0, 6), p1=(0, 1), p48=(0, 48), p63=(0, 63), p56=(0, 56), p112=(0, 112))
    col = {name: T.pf[:, k:k + 1] for k, name in enumerate(FIELD)}
    for k, (sh, m) in enumerate(FIELD.values()):
        ts(T.pbit[:, k:k + 1], T.pidx[:, 0:1], sh, ALU.logical_shift_right, ["pidx"], ["pbit"], m, ALU.bitwise_and)
    cp(T.pf[:, 0:len(FIELD)], T.pbit[:, 0:len(FIELD)], ["pbit"], list(FIELD))
    for k, (name, scale, src, bias) in enumerate([
            ("dq", 8.0, "upper", "p7"), ("wlow", -127.0, "high", 128.0), ("wjoin", 127.0, "upper", -128.0),
            ("lower", -1.0, "upper", 1.0), ("za", 128.0, "p6", "p1"), ("zb", 64.0, "high", "grp"),
            ("self0", 127.0, "p48", "p63"),
            ("rwat", 2.0, "p56", "dq"), ("low", -1.0, "high", 1.0), ("whigh", 127.0, "high", 1.0),
            ("aty", -8.0, "high", "p112"), ("z", 2.0, "zb", "za"), ("self", float(V), "upper", "self0")]):
        col[name] = T.pc[:, k:k + 1]
        op("a", lambda: a.activation(col[name], col[src], ACT.Identity, bias=col.get(bias, bias), scale=scale),
           [src, str(bias)], [name])

    def shifted(name, out, src, key, shift, at):
        ts(out, src, float(shift), ALU.add, [key, at], [name], col[at], ALU.is_equal)

    def scaled(name, out, src, key, w, bias=0.0):
        if by[0] == "v":
            ts(out, src, col.get(w, w), ALU.mult, [key, str(w), str(bias)], [name], col.get(bias, bias), ALU.add)
        else:
            op("a", lambda: a.activation(out, src, ACT.Identity, bias=col.get(bias, bias), scale=col.get(w, w)),
               [key, str(w), str(bias)], [name])

    by = ["v"]

    def constants(e, k):
        by[0] = e
        CONST[k]()

    for k in range(2):
        shifted("rep%d" % k, T.rep[:, 128 * k:128 * k + 128], T.j16[:], "j16", 16 * k, "p31")
    shifted("one", T.one[:], T.j192[:, 0:128], "j192", 0, "p")
    shifted("down", T.down[:], T.j192[:, 0:128], "j192", 0, "pno8")
    shifted("up", T.up[:], T.j192[:, 0:128], "j192", -8, "pno8")
    shifted("fold", T.fold[:, 3, :], T.j192[:], "j192", -64, "p63")
    shifted("lx", T.lx[:], T.j192[:, 0:144], "j192", -7, "p120")
    shifted("sel", T.sel[:], T.j8[:, 0:32], "j8", 0, "grp")
    shifted("per", T.per[:], T.j8[:], "j8", 0, "p7")

    def late(*rows):
        for name, src, w in rows:
            if src == "fold":
                scaled(name, T.fold[:, int(name[-1]), :], T.fold[:, 3, :], src, w)
            else:
                scaled(name, T[name][:], T[src][:, 0:8] if name == "selw" else T[src][:], src, w)

    def fixed_lists():
        ts(T.zo[:], T.zoi[:], col["z"], ALU.add, ["zoi", "z"], ["zo"])
        cp(T.ow[:], T.owi[:], ["owi"], ["ow"])

    def fills():
        scaled("ref", T.ref[:, 1, :], T.j192[:, 0:64], "j192", 16.0, "self")
        scaled("ones", T.ones[:], T.one[:], "one", 0.0, 1.0)

    CONST = [lambda: late(("fold0", "fold", "wjoin")), lambda: late(("fold1", "fold", "lower"), ("fold2", "fold", "upper")),
             lambda: late(("selw", "sel", "wlow"), ("wx", "down", "wlow"), ("wz", "up", "wlow"), ("wy", "up", "whigh")),
             lambda: late(("sel4", "sel", DS), ("seld", "sel", -DS), ("selr", "sel", 2 * DS)), fixed_lists, fills,
             lambda: late(("neg", "one", -1.0), ("big", "one", BIG), ("nbig", "one", -BIG)),
             lambda: late(("dlow", "down", "low"), ("swx", "down", "high"), ("swy", "up", "low"), ("dhigh", "up", "high")),
             lambda: shifted("ly", T.ly[:], T.j192[:, 0:144], "j192", -15, "aty")]

    need("g", ["nbd"], [])
    g.remote_dma_fused([RemoteDMATransfer(dst_ids=[dst(s)], dma_engine_mask=bits(eng[2 * k:2 * k + 1]),
                                          remote_sem=S.nbarr, src=T.nbd[s], dst=T.nbl[place(r)])
                        for k, s in enumerate(others)], local_sem=S.nbsent)
    writer["nbl"] = [("nbarr", N - 1)]
    dma("s", T.ui[:], T.nbl[:], "nbld", ["nbl", "nblown"], ["ui"])
    g.sync.sem_inc(S.go, 1)

    xcalls = x_calls(T, topo, r)
    sent = 0

    def spread(k, s):
        to = T.xw if s == r else T.xr
        b0, b1 = WB[2 * (k % 2)], WB[2 * (k % 2) + 1]
        rows = slice(32 * (s // 2), 32 * (s // 2) + 32)
        lhs = T.rep[rows, 128 * (s % 2):128 * (s % 2) + 128]
        mm(T[b0][:], lhs, T.xs[rows, 0:512], ["rep%d" % (s % 2), "xs"], [b0 + ":"])
        mm(T[b1][:], lhs, T.xs[rows, 512:V], ["rep%d" % (s % 2), "xs"], [b1 + ":"])
        copy("v" if k < SHARED else "a", to[:, V * s:V * s + 512], T[b0][:], [b0 + ":"], ["xr%da" % s])
        act(to[:, V * s + 512:V * s + V], T[b1][:], ACT.Copy, [b1 + ":"], ["xr%db" % s])
        shifted("rw%d" % k, T.rw[:, 128 * k:128 * k + 128], T.j16[:], "j16", 16 * k, "rwat")

    for k, s in enumerate([s for call in xcalls for s, _ in call] + [r]):
        spread(k, s)
    for k, call in enumerate(xcalls):
        if k == GATE:
            iota(T.owi[:], [[128, 8], [V, 2], [2 * V, 4]], 0, 1, "owi", False)
            iota(T.zoi[:], [[1024, 2], [16, 8]], 0, 0, "zoi")
            wait("g", ("go", 1))
        need("g", [k % s for s, _ in call for k in ("xr%da", "xr%db")], [])
        if len(call) == 1:
            s, e = call[0]
            rid, pid, _ = topo.addr(T.cores[s])
            g.remote_dma(T.xw[:, V * r:V * r + V], T.xr[:, V * s:V * s + V], S.xarr, S.xsent, pid, rid, bits(e))
        else:
            g.remote_dma_fused([RemoteDMATransfer(dst_ids=[dst(s)], dma_engine_mask=bits(e), remote_sem=S.xarr,
                                                  src=T.xr[:, V * s:V * s + V], dst=T.xw[:, V * r:V * r + V])
                                for s, e in call], local_sem=S.xsent)
        sent += sum(len(e) for _, e in call)
    arrive = sum(len(e) for q in others for c in x_calls(T, topo, q) for s, e in c if s == r)
    writer["xw"] = [("xarr", arrive)] + writer["xr%da" % r] + writer["xr%db" % r]

    for f in range(2 * RO + 1):
        iota(T.k0[:, 4 * f:4 * f + 4, :], [[0, 2], [-HALF, 2], [0, 64]], HALF + 128 * f, 0, "k0%d" % f)

    KA, DG = ["ka0", "ka1"], ["dg0", "dg1"]

    def entry(s):
        for h in range(2):
            ts(T.dgs[ROWS[0], 2 * s + h, :], T.ui[ROWS[h], s, :], 7, ALU.logical_shift_right, ["ui"], [])
            ts(T.dgs[ROWS[1], 2 * s + h, :], T.ui[ROWS[h], s, :], 127, ALU.bitwise_and, ["ui"], ["dgs%d" % s])

    def first_digits(s):
        cp(T.dg[:, 2 * s:2 * s + 2, :], T.dgs[:, 2 * s:2 * s + 2, :], ["dgs%d" % s], ["dg%d" % s])

    def first_low(s):
        for h in range(2):
            cp(T.ol[ROWS[h], s, :], T.dgs[ROWS[1], 2 * s + h, :], ["dgs%d" % s], ["low%d" % s])

    def close(s):
        tt(T.ka[:, SLOT[s], :], T.kb[:, SLOT[s], :], T.pe1[:, SLOT[s], :], ALU.min, ["kb", "pe1:"], ["ka%d" % s])

    def cut(s):
        ts(T.dgi[:, SLOT[s], :], T.ka[:, SLOT[s], :], 127, ALU.bitwise_and, ["ka%d" % s], ["dgi%d" % s])

    def digits(s):
        for d in range(2):
            for h in range(2):
                cp(T.dg[ROWS[d], 2 * s + h, :], T.dgi[ROWS[h], BLK[s][d], :], ["dgi%d" % s], ["dg%d" % s])

    def all_digits():
        for d, kind in enumerate((HI, LO)):
            for h in range(2):
                cp(T.dg[ROWS[d], h:4:2, :], T.dgi[ROWS[h], kind, :], ["dgi0", "dgi1"], DG)

    def low(s):
        cp(T.ol[:, s, :], T.dgi[:, BLK[s][1], :], ["dgi%d" % s], ["low%d" % s])

    def unstack(out, w, s, W, whole=True):
        for h in range(2):
            mm(out, T.fold[:, w, 64 - 64 * h:192 - 64 * h], T.dg[:, 2 * s + h, :], ["dg%d" % s, "fold%d" % w], W,
               whole and h == 0, whole and h == 1)

    NOW = ["pb1:n0", "pb1:n1"]

    def lists(ss=(0, 1)):
        for s in ss:
            unstack(T.pb1[:, 2 + s, :], 0, s, [NOW[s]])

    def offsets(lo=0, hi=2):
        ts(T.of[:, lo:hi, :], T.pb1[:, 2 + lo:2 + hi, :], -0.125, ALU.mult, NOW[lo:hi], ["of0", "of1"][lo:hi], -0.4375, ALU.add)

    def numbers_now(e):
        if e == "a":
            op("a", lambda: a.activation(T.ref[:, 2:4, :], T.pb1[:, 2:4, :], ACT.Copy, scale=-1.0), NOW, ["now"])
        else:
            ts(T.ref[:, 2:4, :], T.pb1[:, 2:4, :], -1.0, ALU.mult, NOW, ["now"])

    def repeat(s, j, h):
        b = WB[2 * j + h]
        for u in range(4 * h, 4 * h + 4):
            mm(T[b][:, 2 * (u & 2):2 * (u & 2) + 4, u % 2:64:2], T.rw[:, 128 * u:128 * u + 128], T.dg[:, 2 * s:2 * s + 2, :],
               ["dg%d" % s, "rw%d" % u], [b + ":", b + ":xy", b + ":d"])

    def window(e, s, j, h):
        c = V * s + 512 * h
        copy(e, T.win[:, c:c + 512], T[WB[2 * j + h]][:], [WB[2 * j + h] + ":"], ["win%d%d" % (s, h)])

    def mask(e, c):
        copy(e, T.msk[:, 512 * c:512 * c + 512], T.per[:].indirect(T.ol[:, c // 2, PART[c % 2]]),
             ["per", "low%d" % (c // 2)], ["msk%d" % c])

    def numbers(c, t):
        s = (c // 2 + t) % 2
        tt(T.g1[:, 512 * c:512 * c + 512], T.win[:, V * s:V * s + V].indirect(T.of[:, c // 2, PART[c % 2]]),
           T.msk[:, 512 * c:512 * c + 512], ALU.mult, ["win%d0" % s, "win%d1" % s, "of%d" % (c // 2), "msk%d" % c], ["g1%d" % c])

    def number_sums(c):
        b = "pb%d" % (c // 2)
        for y in range(4 * c, 4 * c + 4):
            mm(T[b][:, 0, 8 * (y % 8):8 * (y % 8) + 8], T.g1[:, 128 * y:128 * y + 128], T.selw[:],
               ["g1%d" % c, "selw"], ["%s:c%d" % (b, c % 2)])

    def cand_list(i, h):
        hs = (0, 1) if h == "x" else (h,)
        lo, hi = 32 * hs[0], 32 * hs[-1] + 32
        cp(T.oc[:, 64 * i + lo:64 * i + hi], T["pb%d" % i][:, 0, lo:hi], ["pb%d:c%d" % (i, x) for x in hs],
           ["oc%d" % (2 * i + x) for x in hs])

    def cand_digits(i):
        for h, (m, key) in enumerate([(T.lx, "lx"), (T.ly, "ly")]):
            group(T[XY[i]][:, h, :], [(m[:, 7 - q:135 - q], T.g1[:, V * i + 8 * h + q:V * i + V:16]) for q in range(8)],
                  [key, "g1%d" % (2 * i), "g1%d" % (2 * i + 1)], [XY[i] + ":", XY[i] + ":xy"])

    def X(i):
        return T.xy[:, 128 * i:128 * i + 64]

    def Y(i):
        return T.xy[:, 128 * i + 64:128 * i + 128]

    def joined(e, i):
        copy(e, T.xy[:, 128 * i:128 * i + 128], T[XY[i]][:, 0:2, :], [XY[i] + ":xy"], ["xy%d" % i])
        for blk in (2, 3, 6)[:2 + i if MERGE else 1]:
            group(T[XY[i]][:, blk, :], [(T.wx[:], X(i)), (T.wy[:], Y(i))], ["xy%d" % i, "wx", "wy"], [XY[i] + ":xy"])

    def pair_check(i):
        tt(T.eq[:, 3 * i:3 * i + 2, :], T[XY[i]][:, 2:4, :], T.ref[:, 1:4:2 - i, :][:, 0:2, :] if False else
           (T.ref[:, 1:4:2, :] if i == 0 else T.ref[:, 1:3, :]), ALU.is_equal, [XY[i] + ":xy", "now", "ref"],
           ["eq%d" % k for k in ((0, 1), (3, 4))[i]])

    def check(k):
        i = min(k // 2, 1)
        tt(T.eq[:, k, :], T[XY[i]][:, 2, :], T.ref[:, (3, 1, 0, 1, 2)[k], :], ALU.is_equal,
           [XY[i] + ":xy", ("now", "ref", "c0", "ref", "now")[k]], ["eq%d" % k])

    def add(i, terms, R, stop):
        for k, (blk, lhsT, rhs) in enumerate(terms):
            mm(T["pe%d" % i][:, blk, :], lhsT, rhs, R, ["pe%d:" % i], False, stop and k == len(terms) - 1)

    def open_keys(i, f, under):
        mm(T["pe%d" % i][:, 0:4, :], T.one[:], T.k0[:, 4 * f:4 * f + 4, :], ["one", "k0%d" % f], ["pe%d:" % i], True, False)
        add(i, [(SLOT[s], T.nbig[:], T.ones[:]) for s in under], ["nbig", "ones"], False)

    def add_digits(i, stop):
        pick = [(T.dlow, T.dhigh), (T.swx, T.swy)]
        add(i, [(blk, pick[blk // 2][y][:], (X, Y)[y](i)) for blk in range(4) for y in range(2)],
            ["xy%d" % i, "dlow", "dhigh", "swx", "swy"], stop)

    def digit_sum(i):
        ks = [(0, 1), (2, 3, 4)][i]
        for d, (wx, wy) in enumerate([(T.dlow, T.dhigh), (T.swx, T.swy)]):
            group(T[XY[i]][:, 4 + d, :], [(wx[:], X(i)), (wy[:], Y(i))] + [(T.big[:], T.eq[:, k, :]) for k in ks],
                  ["xy%d" % i, "dlow", "dhigh", "swx", "swy", "big"] + ["eq%d" % k for k in ks], [XY[i] + ":d"])

    def digit_copy(e, i):
        copy(e, T.dd[:, 2 * i:2 * i + 2, :], T[XY[i]][:, 4:6, :], [XY[i] + ":d"], ["dd%d" % i])

    def digit_add(i, stop):
        add(i, [(SLOT[s], T.one[:], T.dd[:, 2 * i:2 * i + 2, :]) for s in range(2)], ["one", "dd%d" % i], stop)

    def add_skips(k, stop):
        add(min(k // 2, 1), [(blk, T.big[:], T.eq[:, k, :]) for blk in range(4)], ["big", "eq%d" % k], stop)

    def top(i):
        if i == 0:
            tt(T.pen[:, 0, :], T.ka[:, HI1, :], T.ka[:, HI0, :], ALU.is_gt, KA, ["pen0"])
        else:
            tt(T.pen[:, 1:3, :], T.ka[:, HI1:LO0 + 1, :], T.pe0[:, HI, :], ALU.is_gt, KA + ["pe0:"], ["pen1"])

    def below(i, pens, key, stop):
        add(i, [(blk, (T.big, T.nbig)[(blk + k // 2) % 2][:], T.pen[:, k, :]) for k in pens for blk in range(4)],
            ["big", "nbig", key], stop)

    def own_keys(lo, hi):
        return ["own%d" % x for x, y in OWN if x < hi and lo < y]

    def features(lo, hi, off, okey, dif, tag):
        o = lo % V
        tt(dif[:, lo:hi], T.xw[:].indirect(off[:, lo // 16:hi // 16]), T.own[:, o:o + hi - lo], ALU.subtract,
           ["xw", okey] + own_keys(o, o + hi - lo), ["dif%s%d" % (tag, lo)])

    def absolute(lo, hi, dif, ab, tag):
        act(ab[:, lo:hi], dif[:, lo:hi], ACT.Abs, ["dif%s%d" % (tag, lo)], ["ab%s%d" % (tag, lo)])

    relu = {}

    def positive(lo, hi, dif, ab, tag):
        ts(ab[:, lo:hi], dif[:, lo:hi], 0.0, ALU.max, ["dif%s%d" % (tag, lo)], ["ab%s%d" % (tag, lo)])
        relu[tag, lo] = dif

    def sums(b, blks, lo, hi, ab, tag, stop):
        n = len(range(4)[blks])
        dif = relu.pop((tag, lo), None)
        terms = [(ab, T.sel4)] if dif is None else [(ab, T.selr), (dif, T.seld)]
        for y in range(lo // 128, hi // 128):
            for k, (data, sel) in enumerate(terms):
                mm(T[b][:, blks, 8 * (y % 8):8 * (y % 8) + 8], data[:, 128 * y:128 * y + 128], sel[:, 0:n, :],
                   ["ab%s%d" % (tag, lo), "sel4", "selr", "seld"] + ["dif%s%d" % (tag, lo)] * k, [b + ":"], False,
                   stop and y == hi // 128 - 1 and k == len(terms) - 1)

    def sub_bank(k):
        return T[SUB[k]][:, 0:(CH[k][1] - CH[k][0]) // 64, :]

    def scalar_features(k):
        lo, hi = CH[k]
        act(T.dif[:, lo:hi], T.xw[:].indirect(T.oc[:, lo // 16:hi // 16]), ACT.Copy, ["xw", "oc%d" % (lo // 512)],
            ["difr%d" % lo])

    def before_subtract(k):
        lo, hi = CH[k]
        o = lo % V
        mm(sub_bank(k), T.neg[:], T.own[:, o:o + hi - lo], ["neg"] + own_keys(o, o + hi - lo), [SUB[k] + ":"], True, False)

    def subtract(k):
        lo, hi = CH[k]
        mm(sub_bank(k), T.one[:], T.dif[:, lo:hi], ["one", "difr%d" % lo], [SUB[k] + ":"], False, True)

    def scalar_abs(k):
        lo, hi = CH[k]
        act(T.ab[:, lo:hi], sub_bank(k), ACT.Abs, [SUB[k] + ":"], ["abr%d" % lo])

    def start_lists():
        cp(T.zt[:], T.win[:].indirect(T.zo[:]), ["win00", "win01", "win10", "win11", "zo"], ["zt"])
        group(T.pb0[:, 2:4, :], [(T.wx[:], T.zt[:, 0:256:2]), (T.wz[:], T.zt[:, 1:256:2])], ["zt", "wx", "wz"], ["pb0:z"])

    def own_features(k):
        lo, hi = OWN[k]
        act(T.own[:, lo:hi], T.xw[:].indirect(T.ow[:, lo // 16:hi // 16]), ACT.Copy, ["xw", "ow"], ["own%d" % lo])

    def start_open():
        open_keys(1, 0, (0, 1))
        for blk in range(4):
            unstack(T.pe1[:, blk, :], 1 + blk // 2, blk % 2, ["pe1:"], False)

    RESULT = [lambda: ts(T.di[:], T.ka[:, HI, :], 12, ALU.logical_shift_right, KA, ["di"], 4095, ALU.bitwise_and),
              lambda: ts(T.pb1[:, 2:4, :], T.dgi[:, HI, :], 128.0, ALU.mult, ["dgi0", "dgi1"], NOW),
              lambda: cp(T.da[:], T.di[:], ["di"], ["da"]),
              lambda: tt(T.un[:], T.pb1[:, 2:4, :], T.dgi[:, LO, :], ALU.add, NOW + ["dgi0", "dgi1"], ["un"])]

    order = [(n.lstrip("+"), t + n.count("+")) for t in range(RO)
             for n in (FIRST, LATER, EVEN or LATER, LAST)[t].split()]
    last, seen = set(), {}
    for k, (n, _) in enumerate(order):
        name = n.rstrip("0123456789x")
        if name in ("below", "adddig", "dadd", "skip", "sum", "isum", "again"):
            i = int(n[-1]) if name != "again" else 1
            seen[{"skip": min(i // 2, 1), "sum": CH[i][0] // V, "isum": 1}.get(name, i)] = k
        if n in ("step0", "top1") and 0 in seen:
            last.add(seen.pop(0))
        if name in ("close", "closeall", "ka") and 1 in seen:
            last.add(seen.pop(1))
    for k, (n, t) in enumerate(order):
        name = n.rstrip("0123456789x")
        x = [c if c == "x" else int(c) for c in n[len(name):]]
        stop = k in last
        s = (x[0] + t) % 2 if x and x[0] != "x" else None
        CUR[0] = (t, k, n)
        {"const": lambda: constants("v", *x), "consta": lambda: constants("a", *x), "entry": lambda: entry(*x), "first": lambda: first_digits(*x),
         "firstlow": lambda: first_low(*x),
         "close": lambda: close(s), "cut": lambda: cut(s), "digits": lambda: digits(s), "low": lambda: low(*x),
         "lists": lambda: lists(x) if x else lists(), "offsets": lambda: offsets(x[0], x[0] + 1) if x else offsets(),
         "rep": lambda: repeat(s, *x),
         "winv": lambda: window("v", s, *x), "wina": lambda: window("a", s, *x),
         "mask": lambda: mask("a", *x), "maskv": lambda: mask("v", *x), "num": lambda: numbers(*x, t),
         "bsum": lambda: number_sums(*x), "list": lambda: cand_list(*x), "xy": lambda: cand_digits(*x),
         "difv": lambda: joined("v", *x), "difa": lambda: joined("a", *x), "check": lambda: check(*x),
         "nowv": lambda: numbers_now("v"), "nowa": lambda: numbers_now("a"),
         "cv": lambda: copy("v", T.ref[:, 0, :], T[XY[0]][:, 2, :], [XY[0] + ":xy"], ["c0"]),
         "ca": lambda: copy("a", T.ref[:, 0, :], T[XY[0]][:, 2, :], [XY[0] + ":xy"], ["c0"]),
         "open": lambda: open_keys(*x, 2 * t + 1 + x[0], (0,)), "adddig": lambda: add_digits(*x, stop),
         "pair": lambda: pair_check(*x), "digitsall": all_digits,
         "closeall": lambda: tt(T.ka[:], T.kb[:], T.pe1[:, 0:4, :], ALU.min, ["kb", "pe1:"], KA),
         "cutall": lambda: ts(T.dgi[:], T.ka[:], 127, ALU.bitwise_and, KA, ["dgi0", "dgi1"]),
         "lowall": lambda: cp(T.ol[:], T.dgi[:, LO, :], ["dgi0", "dgi1"], ["low0", "low1"]),
         "dsum": lambda: digit_sum(*x), "dcv": lambda: digit_copy("v", *x), "dca": lambda: digit_copy("a", *x),
         "dadd": lambda: digit_add(*x, stop), "skip": lambda: add_skips(*x, stop), "top": lambda: top(*x),
         "below": lambda: below(*x, [(0,), (1, 2)][x[0]], "pen%d" % x[0], stop),
         "again": lambda: below(1, (0,), "pen0", stop),
         "step": lambda: tt(T.kb[:], T.ka[:], T.pe0[:, 0:4, :], ALU.min, KA + ["pe0:"], ["kb"]),
         "fv": lambda: features(*CH[x[0]], T.oc, "oc%d" % (CH[x[0]][0] // 512), T.dif, "r"),
         "av": lambda: absolute(*CH[x[0]], T.dif, T.ab, "r"),
         "fa": lambda: scalar_features(*x), "presub": lambda: before_subtract(*x), "sub": lambda: subtract(*x),
         "aa": lambda: scalar_abs(*x),
         "sum": lambda: sums("pe%d" % (CH[x[0]][0] // V), slice(0, 4), *CH[x[0]], T.ab, "r", stop),
         "zt": start_lists, "ob": lambda: cp(T.ob[:], T.pb0[:, 2:4, :], ["pb0:z"], ["ob"]),
         "own": lambda: own_features(*x), "iopen": start_open,
         "if": lambda: features(*START[x[0]], T.ob, "ob", T.dif0, "i"),
         "ia": lambda: absolute(*START[x[0]], T.dif0, T.ab0, "i"), "ir": lambda: positive(*START[x[0]], T.dif0, T.ab0, "i"),
         "isum": lambda: sums("pe1", SLOT[START[x[0]][0] // V], *START[x[0]], T.ab0, "i", stop),
         "ka": lambda: cp(T.ka[:], T.pe1[:, 0:4, :], ["pe1:"], KA),
         "out": lambda: RESULT[x[0]]()}[name]()

    dma("s", T.od[:, 0:64, :], T.un[:], "o1", ["un"], ["od1"])
    dma("a", T.od[:, 64:128, :], T.da[:], "o2", ["da"], ["od2"])
    home = slice(16 * place(r), 16 * place(r) + 16)
    dma("s", T.ob2[r, 0:64, :], T.un[home, :], "o3", ["un"], ["ol1own"])
    dma("a", T.ob2[r, 64:128, :], T.da[home, :], "o4", ["da"], ["ol2own"])
    need("g", ["od1", "od2"], [])
    g.remote_dma_fused([RemoteDMATransfer(dst_ids=[dst(s)], dma_engine_mask=bits(eng[2 * k:2 * k + 2]),
                                          remote_sem=S.oarr, src=T.od[place(s)], dst=T.ob2[r])
                        for k, s in enumerate(others)], local_sem=S.osent)
    writer["ol"] = [("oarr", 2 * (N - 1))]
    dma("s", T.ynb[:], T.ob2[:, 0:64, :], "y1", ["ol", "ol1own"], ["y1"])
    dma("a", T.yd[:], T.ob2[:, 64:128, :], "y2", ["ol", "ol2own"], ["y2"])
    for tok in [("nbsent", N - 1), ("xsent", sent), ("osent", 2 * (N - 1)), ("cv", count["v"]),
                ("ca", count["a"]), ("cp", count["p"]), ("cg", count["g"]), ("y1", 16), ("y2", 16)]:
        wait("g", tok)
